import numpy as np, ml_dtypes
CORES = [5,29,101,125,133,157,229,253]
N = 8
import mx_ref
BF = ml_dtypes.bfloat16
def gcols(t, e):
    v = np.concatenate([t.reshape(8, 16, -1, 4), np.zeros((8, 16, 1, 4), BF)], axis=2)
    return np.ascontiguousarray(np.stack([v[g][:, e[g]] for g in range(8)])).reshape(128, -1)
def tile(rs):
    return np.stack(rs, axis=2).reshape(128, -1).astype(BF)
def cut(t, i, w=512):
    return t[:, w * i:w * i + w]
def pick(q, e):
    c = np.concatenate([q[0].reshape(128, -1, 4), np.zeros((128, 1, 4), np.uint8)], axis=1); s = np.concatenate([q[1], np.ones((16, 1), np.uint8)], axis=1)
    return (np.ascontiguousarray(c[:, e].reshape(128, -1)), np.ascontiguousarray(s[:, e]))
def join(*qs):
    return (np.concatenate([q[0] for q in qs], axis=1), np.concatenate([q[1] for q in qs], axis=1))
def put(q, e, v):
    c, s = q[0].reshape(128, -1, 4).copy(), q[1].copy(); c[:, e] = v[0].reshape(128, -1, 4); s[:, e] = v[1]
    return (c.reshape(128, -1), s)
def pk(c, s):
    return (np.ascontiguousarray(c), mx_ref.live(s))
def emit(q):
    return q[0], q[1]
def packed(v, rng):
    q = [mx_ref.quantize(np.ascontiguousarray(v[r])) for r in range(N)]
    return np.stack([a for a, b in q]), np.stack([mx_ref.plane(b, rng) for a, b in q])
def values_of_codes():
    e, c = np.zeros((128, 128, 4), np.float32), np.zeros((128, 2, 4), np.uint8)
    e[np.arange(128), np.arange(128), 0] = 1
    c[:127, :, 0] = np.arange(256).reshape(2, 128).T[:127]
    return mx_ref.matmul(mx_ref.quantize(e.reshape(128, 512).astype(BF)), (c.reshape(128, 8), np.full((16, 2), 127, np.uint8))).T.reshape(-1).astype(np.float64)
CODE_VALUE, SCALE_VALUE = values_of_codes(), 2.0 ** (np.arange(256) - 127.0)
def decode(q):
    return (CODE_VALUE[q[0]].reshape(16, 8, -1, 4) * SCALE_VALUE[q[1]][:, None, :, None] + 0.0).reshape(128, -1).astype(np.float32)
def f(rng, *shape):
    return mx_ref.flush((rng.standard_normal(shape, dtype=np.float32) * np.exp2(rng.integers(-2, 3, shape[:-1] + (1,)))).astype(BF))
def wide(rng, *shape, cols=0):
    v = rng.standard_normal(shape, dtype=np.float32) * np.exp2(rng.integers(-12, 13, shape)).astype(np.float32)
    if cols: v *= np.repeat(np.exp2(rng.integers(-cols, cols + 1, shape[:-2] + (1, shape[-1] // 4))) * (rng.random(shape[:-2] + (1, shape[-1] // 4)) > 0.0625), 4, axis=-1).astype(np.float32)
    return mx_ref.flush(v.astype(BF))
S, C, L, Q1, Q2, R = 256, 192, 32, 14, 52, 3
def numbers_of(rng):
    return {"x": np.array(f(rng, N, 128, 4 * C)), "u": np.array(f(rng, N, 128, 512)), "v": np.array(f(rng, N, 128, 512))}
def weights(rng, w):
    c, p = packed(w, rng)
    return {"wc": c, "ws": p}
def shift(rng, mix=False):
    w = np.zeros((128, 4, 128, 4), np.float32)
    i = np.arange(128)
    first = i[i % 16 < 8]
    i = i[(i % 16 >= 8) & (i % 16 < 14)]
    for b in range(4):
        w[i, b, i, b] = -64
        w[i + 2, b, i, b] = 64
        if mix: w[(first + 16) % 128, b, first, b] = 64
    return weights(rng, np.stack([w.reshape(128, 2048).astype(BF)] * N))
def planned(rng, a, step, k, mix=False):
    d = numbers_of(rng)
    x = d["x"].astype(np.float32).reshape(N, 8, 16, C, 4)
    g = ((a[..., None] >> np.arange(8)) & 1) * 2.0 ** np.arange(8) * step
    x[:, :, 8:] = g.reshape(4, N, 8, C, 2, 4).transpose(1, 2, 0, 4, 3, 5).reshape(N, 8, 8, C, 4)
    u = d["u"].reshape(N, 128, 128, 4)
    u[:, :, ::16] = 0
    for h in range(0, 128, 16): u[:, h + 8:h + 10, h] = k.astype(np.float32).astype(BF)[:, None, None]
    return {"x": d["x"], "u": u.reshape(N, 128, 512), "v": d["v"], **shift(rng, mix)}, x
def with_x(d, x):
    d["x"] = x.astype(np.float32).reshape(N, 128, 4 * C).astype(BF)
    return d
def setup_inputs(rng):
    return {**numbers_of(rng), **weights(rng, f(rng, N, 128, 2048))}
def setup_inputs_ties(rng):
    o = rng.permutation(N)
    a = rng.integers(0, 3, (4, N, 8, C))
    a[:, o[0]] = 1
    d, x = planned(rng, a, 1.0, np.ones(N))
    x[o[1]] = 0
    s = rng.integers(0, 6, (4, 8, C))
    x[o[2], :, 8:] = 0
    for i in range(4):
        x[o[2], :, 8 + 2 * i, :, 0] = (8 + s[i]) * 2.0 ** -33
        x[o[2], :, 9 + 2 * i, :, 0] = (9 + s[i]) * 2.0 ** -33
    u = d["u"].reshape(N, 128, 128, 4)
    for h in range(0, 128, 16):
        u[o[2], h + 8, h] = BF(9 * 2.0 ** -33)
        u[o[2], h + 9, h] = BF(-2.0 ** -30)
    d["u"] = u.reshape(N, 128, 512)
    return with_x(d, x)
def setup_inputs_near(rng):
    k = (np.arange(N) + rng.integers(N)) % N < N // 2
    k = np.where(k, 2.0 ** -30, 1.0)
    d, x = planned(rng, rng.integers(0, 256, (4, N, 8, C)), 2.0 ** -23, k)
    x[:, :, :8] = (0.25 + 0.75 * rng.random((N, 8, 8, C, 4))) * rng.choice([-1.0, 1.0], (N, 8, 8, C, 4))
    x[:, :, 0] = 0
    x[:, :, 0, :, 0] = (rng.permutation(8) % 2 * 2.0 - 1.0)[None, :, None]
    x[k < 1] *= np.float32(2.0 ** -7)
    u = d["u"].reshape(N, 128, 128, 4)
    for h in range(0, 128, 16): u[:, h, h, 0] = k.astype(np.float32).astype(BF)
    d["u"] = u.reshape(N, 128, 512)
    return with_x(d, x)
def setup_inputs_huge(rng):
    d = numbers_of(rng)
    x = 2.0 ** 30 * (0.6 + 0.4 * rng.random((N, 128, C, 4)))
    c = np.stack([rng.permutation(C) % 2 * 2.0 - 1.0 for r in range(N)])
    c[rng.permutation(N) < N // 2] = 1
    x *= c[:, None, :, None]
    u = d["u"].reshape(N, 128, 128, 4)
    s = np.stack([rng.permutation(8) % 2 * 2.0 - 1.0 for r in range(N)])
    u[:, :, ::16] = (2.0 ** 30 * (1 - 0.25 * rng.random((N, 128, 8, 4))) * s[:, None, :, None]).astype(np.float32).astype(BF)
    w = np.zeros((128, 4, 128, 4), np.float32)
    i = np.arange(128)
    for b in range(4): w[i, b, i, b] = 2.0 ** -10
    return with_x({"x": d["x"], "u": u.reshape(N, 128, 512), "v": d["v"], **weights(rng, np.stack([w.reshape(128, 2048).astype(BF)] * N))}, x)
def entering(m, h, rng):
    n = S // 16
    w = np.zeros(n, int)
    rest = L
    if m < 2:
        o = rng.permutation(n // 4)
        w[4 * o[0]:4 * o[0] + 4] = Q1 - h
        rest -= 4 * (Q1 - h)
        for i in o[1:]:
            c = min(rest, Q2 - 4 * h + int(m == 1 and i == o[1]))
            w[4 * i + rng.integers(4)] = c
            rest -= c
    elif m == 2:
        a = int(rng.integers(n))
        w[a] = Q1 + 1 - h
        rest -= Q1 + 1 - h
        for i in rng.permutation(n):
            if i // 4 != a // 4:
                w[i] = min(rest, Q1 - h)
                rest -= w[i]
    elif m == 3: w[rng.integers(n)] = L
    else: w = np.bincount(rng.integers(0, n, L), minlength=n)
    return w
def setup_inputs_crowd(rng):
    n = S // 16
    leaf = np.arange(C) * S // C // 16
    a = rng.integers(0, 256, (4, N, 8, C))
    a[3] = rng.integers(100, 104, (N, 8, C))
    stay = np.ones((N, 8, C), bool)
    m = np.stack([rng.permutation(8) for r in range(N)])
    gone = [[[0], [0, 1], [int(rng.integers(1, n - 2)), n - 1]][i % 3] for i in rng.permutation(N)]
    for r in range(N):
        for g in range(8):
            a[0, r, g] = rng.permutation(C)
            k = np.full(n, L // n)
            if m[r, g] == 6:
                other = np.setdiff1d(np.arange(n), gone[r])
                k[gone[r]] = C // n
                k[rng.permutation(other)] = (L - len(gone[r]) * (C // n) + np.arange(len(other))) // len(other)
            for i in range(n):
                e = rng.permutation(np.flatnonzero(leaf == i))
                if i == 0: e = np.concatenate([[0], e[e > 0]])
                stay[r, g, e[:k[i]]] = False
    for r in range(N):
        for g in range(8):
            if m[r, g] == 4: e = np.zeros(L, int)
            elif m[r, g] == 5: e = np.full(L, C - 1)
            else:
                if m[r, g] == 6:
                    room = Q1 - np.bincount(leaf[stay[r, g]], minlength=n)
                    room[gone[r]] = 0
                    first = np.zeros(6, int)
                    if gone[r][0] > 0:
                        c = gone[r][0] - 1
                        room[[c, n - 2]] -= 2
                        i = int(np.flatnonzero(stay[r, g] & (leaf == c))[-1])
                        first = np.array([i, i, C - 1, C - 1])
                    w = np.bincount(rng.permutation(np.repeat(np.arange(n), room))[:L - len(first)], minlength=n)
                else:
                    w = entering(m[r, g], C // n - L // n, rng)
                    first = np.zeros(L - int(np.sum(w)), int)
                e = np.concatenate([first] + [rng.choice(np.flatnonzero(stay[r, g] & (leaf == i)), w[i]) for i in np.flatnonzero(w)])
            s = (r - 1) % N
            b = rng.integers(C, 256, C)
            b[~stay[s, g][a[0, s, g]]] = rng.permutation(e)
            a[1, s, g] = b
    d, x = planned(rng, a, 1.0, np.ones(N), True)
    return with_x(d, x)
def setup_inputs_spread(rng):
    d = setup_inputs(rng)
    d["x"] = wide(rng, N, 128, 4 * C, cols=6)
    return d
def check_inputs(d):
    b = []
    for k in ("x", "u", "v"):
        a = np.abs(d[k].astype(np.float32))
        if not (np.isfinite(a).all() and ((a == 0) | (a >= 2.0 ** -30) & (a <= 2.0 ** 30)).all()): b.append("a value of " + k)
    for r in range(N):
        if ((d["wc"][r] & 127) == 127).any(): b.append("a code of wc that is no number")
        with np.errstate(over="ignore"): a = np.abs(decode(pk(d["wc"][r], d["ws"][r])))
        if not ((a == 0) | (a >= 2.0 ** -30) & (a <= 2.0 ** 30)).all(): b.append("a value of W (wc, ws)")
    return b
def respread(h, key, new):
    n = np.searchsorted(key[h], new, side="right")
    leaf = np.where(n > 0, h[np.maximum(n - 1, 0)], 0) // 16
    k = np.concatenate([key[h], new])
    i = np.argsort(k, kind="stable")
    src = np.concatenate([h, S + np.arange(L)])[i]
    at = src.copy()
    lf = np.concatenate([h // 16, leaf])[i]
    count = np.bincount(lf, minlength=S // 16)
    size = np.where(count <= Q1, 16, np.where(np.repeat(np.sum(count.reshape(-1, 4), axis=1), 4) <= Q2, 64, S))
    size[np.bincount(leaf, minlength=S // 16) == 0] = 0
    for w in (16, 64, S):
        for s in range(0, S, w):
            if (size[s // 16:(s + w) // 16] == w).any():
                e = np.flatnonzero(lf * 16 // w == s // w)
                at[e] = s + np.arange(len(e)) * w // len(e)
    to, kept = np.full(S, -1), np.zeros(S, np.float32)
    to[at] = src
    kept[at] = k[i]
    return to, kept
def reference(x, u, v, wc, ws):
    qu = [mx_ref.quantize(u[r]) for r in range(N)]
    lay = [pk(wc[r], ws[r]) for r in range(N)]
    start = np.arange(C) * S // C
    now, key, held = [], [], []
    for r in range(N):
        p = mx_ref.matmul(qu[r], mx_ref.quantize(x[r]))[::16] + np.float32(0.0)
        o = np.argsort(p, axis=1, kind="stable")
        e, k = np.full((8, S), -1), np.zeros((8, S), np.float32)
        e[:, start] = o
        k[:, start] = np.take_along_axis(p, o, axis=1)
        now.append(gcols(x[r], e))
        key.append(k)
        held.append(e >= 0)
    y, ol = np.zeros((N, 128, S), np.float32), np.zeros((N, 8, S), np.float32)
    oc, osc = np.zeros((N, 128, 4 * S), np.uint8), np.zeros((N, 16, S), np.uint8)
    for t in range(R):
        made, new, border = [], [], []
        for r in range(N):
            q = mx_ref.quantize(now[r])
            made.append(tile([mx_ref.matmul(pick(lay[r], np.arange(128 * b, 128 * b + 128)), q) * np.float32(0.015625) + now[r][:, b::4].astype(np.float32) for b in range(4)]))
            p = mx_ref.matmul(qu[r], mx_ref.quantize(made[r]))[::16] + np.float32(0.0)
            o = np.argsort(np.where(held[r], p, np.float32(np.inf)), axis=1, kind="stable")[:, :L]
            new.append(np.take_along_axis(p, o, axis=1))
            np.put_along_axis(held[r], o, False, axis=1)
            border.append(mx_ref.quantize(gcols(made[r], o)))
        came = decode(join(*border)).astype(BF)
        for r in range(N):
            e = (r - 1) % N
            to, k = np.full((8, S), -1), np.zeros((8, S), np.float32)
            for g in range(8): to[g], k[g] = respread(np.flatnonzero(held[r][g]), key[r][g], new[e][g])
            now[r] = gcols(np.concatenate([made[r], cut(came, e, 4 * L)], axis=1), to)
            key[r], held[r], ol[r] = k, to >= 0, to
    for r in range(N):
        q = mx_ref.quantize(now[r])
        y[r] = mx_ref.matmul(mx_ref.quantize(v[r]), q)
        oc[r], osc[r] = emit(q)
    return {"y": y, "ol": ol, "oc": oc, "osc": osc}

@@ -1,0 +1,518 @@
+from concourse.bass import DstId, RemoteDMATransfer
+from concourse.mybir import dt, AluOpType, AxisListType, ActivationFunctionType
+
+ALU, AF, AX = AluOpType, ActivationFunctionType, AxisListType
+S_, C_, L_, R_ = 256, 192, 32, 3
+K_ = C_ - L_
+NV = 7
+NS = 12 - NV
+PW = 208
+BNS, B16, B64, B256, IO1, IO2, TOP = 0, 16, 64, 264, 280, 480, 680
+CX, U8, BF, F32, I32, U16 = "float8_e4m3fn_x4", "uint8", "bfloat16", "float32", "int32", "uint16"
+
+
+def _sb(n, d):
+    return ("sbuf", [128, n], d)
+
+
+SCRATCH = {
+    "xt": _sb(768, BF), "ut": _sb(512, BF), "vt": _sb(512, BF), "et": _sb(2048, BF),
+    "qu": _sb(128, CX), "su": _sb(128, U8), "qur": _sb(128, CX), "sur": _sb(128, U8),
+    "qv": _sb(128, CX), "sv": _sb(128, U8), "qw": _sb(512, CX), "sw": _sb(512, U8), "qe": _sb(512, CX), "se": _sb(512, U8),
+    "qf": _sb(256, CX), "sf": _sb(256, U8), "qt": _sb(256, CX), "st": _sb(256, U8),
+    "ft": _sb(1024, BF), "f64": _sb(1024, BF), "tt": _sb(1024, BF), "t64": _sb(1024, BF), "tc": _sb(4 * PW, BF), "bt": _sb(512, BF),
+    "pi": _sb(8, I32), "ic": _sb(8, F32), "iu": _sb(24, I32), "offu": _sb(8, U16), "bco": _sb(12, U16), "coff": _sb(4, U16),
+    "ioj": _sb(256, BF), "iob": _sb(256, BF), "iof": _sb(64, F32), "ones": _sb(512, BF),
+    "dm": _sb(256, BF), "rm": _sb(256, BF), "gt": _sb(192, BF), "wt": _sb(256, BF), "bm": _sb(192, BF), "mk": _sb(64, BF),
+    "eqt": _sb(208, BF), "eqs": _sb(192, BF), "stt": _sb(192, BF), "yc": _sb(16, F32), "kc": _sb(16, F32), "idr": _sb(32, BF), "zr": _sb(32, BF),
+    "gx": _sb(144, F32), "mm": _sb(16, F32), "cw": _sb(16, F32), "aoff": _sb(2, U16), "tab": _sb(688, F32),
+    "dc": _sb(16, F32), "cr": _sb(8, F32), "yy": _sb(384, F32), "yi": _sb(384, I32), "y2": _sb(384, F32), "cols": _sb(32, F32),
+    "psb": _sb(256, F32), "pc": _sb(192, F32), "msk": _sb(192, F32), "sc": _sb(192, F32), "eq": _sb(192, BF), "cor": _sb(192, BF),
+    "cmp": _sb(192 * NV, BF), "cs": _sb(192 * NV, BF), "sg": _sb(PW * NS, BF), "gl": _sb(32, F32),
+    "rk": _sb(16, F32), "roff": _sb(12, U16), "k0": _sb(192, F32),
+    "sr": _sb(PW, BF), "pre": _sb(192, BF), "hh": _sb(64, F32), "doff": _sb(12, U16),
+    "pr": _sb(256, BF), "pls": _sb(K_ * L_ + 16, BF), "m1": _sb(256, BF), "m2": _sb(256, BF), "pl": _sb(12, U16), "poff": _sb(12, U16),
+    "kw": _sb(PW, F32), "kp": _sb(256, F32), "sig": _sb(16, F32), "jk": _sb(512, BF), "tbs": _sb(4 * 176, BF),
+    "ck": _sb(320, BF), "cn": _sb(320, BF), "noff": _sb(2, U16), "qo": _sb(2, U16), "aa": _sb(192, BF), "tb": _sb(PW, BF),
+    "ju": _sb(128, F32), "yd": _sb(8, F32), "thr": _sb(8, F32), "rs": _sb(8, F32), "sm": _sb(64, F32),
+    "voff": _sb(2, U16), "xo": _sb(2, U16), "gq": _sb(32, F32), "qq": _sb(16, F32), "qoff": _sb(16, U16), "to": _sb(16, U16),
+    "uq": _sb(16, U16), "ax": _sb(64, F32), "ay": _sb(64, F32), "olw": _sb(PW, F32), "olr": _sb(256, F32), "ys": _sb(256, F32),
+    "p0": ("psum", [128, 512], F32), "p1": ("psum", [128, 512], F32), "p2": ("psum", [128, 512], F32), "p3": ("psum", [128, 512], F32),
+    "pp": ("psum", [128, 512], F32), "py": ("psum", [128, 512], F32),
+}
+for _t in range(R_):
+    SCRATCH["ko%d" % _t] = _sb(8, F32)
+    SCRATCH["ka%d" % _t] = _sb(8, F32)
+    SCRATCH["qb%d" % _t] = _sb(160, CX)
+    SCRATCH["sb%d" % _t] = _sb(256, U8)
+SEMAPHORES = ["cV", "cS", "cP", "cG", "sent"] + ["d%d" % _t for _t in range(14)] + ["aK%d" % _t for _t in range(R_)] + ["aB%d" % _t for _t in range(R_)]
+
+
+def _bits(es):
+    return sum(1 << e for e in es)
+
+
+def _relays(src, dst, topo):
+    c = [k for k in topo.cores_of(src) if k != src and topo.may_write(k, dst)]
+    c.sort(key=lambda k: topo.die(k) != topo.die(src))
+    return c[0], c[1], c[2]
+
+
+def _send(g, T, topo, src, dst, out, in_, sem):
+    rid, pid = topo.addr(dst, src)
+    es = topo.engines(src, dst)
+    g.remote_dma(out, in_, T.sem[sem], T.sem.sent, pid, rid, _bits(es))
+    return len(es)
+
+
+def _send_b(g, T, topo, src, dst, dst2, codes, scales, t):
+    es = [e for e in topo.engines(src, dst) if e in topo.engines(src, dst2)]
+    h = len(es) // 2
+    d, d2 = [[DstId(rid=a[0], pnc=a[1])] for a in (topo.addr(dst, src), topo.addr(dst2, src))]
+    g.remote_dma_fused([
+        RemoteDMATransfer(dst_ids=d, dma_engine_mask=_bits(es[:h]), remote_sem=T.sem["aB%d" % t], src=codes, dst=T["qb%d" % t][:, 0:32].bitcast(dt.uint8)),
+        RemoteDMATransfer(dst_ids=d2, dma_engine_mask=_bits(es[h:]), remote_sem=T.sem["aB%d" % t], src=scales, dst=T["sb%d" % t][:, 0:128]),
+    ], local_sem=T.sem.sent)
+    return 2 * h
+
+
+def rank_program(g, core, T, topo):
+    cores = list(T.cores)
+    n = len(cores)
+    rank = T.rank_of(core)
+    if rank is None:
+        for r in range(n):
+            src, dst = cores[r], cores[(r + 1) % n]
+            rk, rb, rs = _relays(src, dst, topo)
+            sent = 0
+            for t in range(R_):
+                if core == rk:
+                    g.wait_ge(T.sem["aK%d" % t], len(topo.engines(src, core)))
+                    sent += _send(g, T, topo, core, dst, T["ka%d" % t][:, 0:2], T["ka%d" % t][:, 0:2], "aK%d" % t)
+                if core in (rb, rs):
+                    ap = T["qb%d" % t][:, 0:32].bitcast(dt.uint8) if core == rb else T["sb%d" % t][:, 96:128]
+                    g.wait_ge(T.sem["aB%d" % t], len(topo.engines(src, core)) // 2)
+                    sent += _send(g, T, topo, core, dst, ap, ap, "aB%d" % t)
+            if sent:
+                g.wait_ge(T.sem.sent, sent)
+        return
+    relay_k, relay_b, relay_s = _relays(core, cores[(rank + 1) % n], topo)
+    from_k, from_b, from_s = _relays(cores[(rank - 1) % n], core, topo)
+
+    Q = {"V": g.vector, "S": g.scalar, "P": g.tensor, "G": g, "Y": g.sync}
+    cnt = {"cV": 0, "cS": 0, "cP": 0, "cG": 0, "sent": 0}
+    clock = {q: {} for q in Q}
+    snap, wrote, read = {}, {}, {}
+    ndma = [0]
+
+    def order(q, rd, wr):
+        ev = {}
+        for k in rd + wr:
+            if k in wrote:
+                ev[wrote[k]] = 1
+        for k in wr:
+            for e in read.get(k, []):
+                ev[e] = 1
+        ev = [e for e in ev if clock[q].get(e[0], 0) < e[1]]
+        for e in ev:
+            if any(o != e and snap[o].get(e[0], 0) >= e[1] for o in ev):
+                continue
+            Q[q].wait_ge(T.sem[e[0]], e[1])
+            for s, v in snap[e].items():
+                clock[q][s] = max(clock[q].get(s, 0), v)
+
+    def done(q, e, rd, wr):
+        snap[e] = dict(clock[q])
+        snap[e][e[0]] = e[1]
+        for k in rd:
+            read.setdefault(k, []).append(e)
+        for k in wr:
+            wrote[k] = e
+            read[k] = []
+
+    def op(q, rd, wr, fn):
+        rd, wr = rd.split(), wr.split()
+        order(q, rd, wr)
+        s = "c" + q
+        cnt[s] += 1
+        fn().then_inc(T.sem[s], 1)
+        done(q, (s, cnt[s]), rd, wr)
+
+    def dma(q, rd, wr, out, in_):
+        rd, wr = rd.split(), wr.split()
+        order(q, rd, wr)
+        s = "d%d" % ndma[0]
+        ndma[0] += 1
+        cnt[s] = 16
+        Q[q].dma_start(out, in_).then_inc(T.sem[s], 16)
+        done(q, (s, 16), rd, wr)
+
+    def arrives(key, sem, val):
+        snap[(sem, val)] = {sem: val}
+        wrote[key] = (sem, val)
+
+    V, A = g.vector, g.scalar
+
+    def ts(rd, wr, out, in0, s1, o0, s2=None, o1=None):
+        if o1 is None:
+            op("V", rd, wr, lambda: V.tensor_scalar(out, in0, s1, None, o0))
+        else:
+            op("V", rd, wr, lambda: V.tensor_scalar(out, in0, s1, s2, o0, o1))
+
+    def tt(rd, wr, out, a, b, o):
+        op("V", rd, wr, lambda: V.tensor_tensor(out, a, b, o))
+
+    def cp(rd, wr, out, a):
+        op("V", rd, wr, lambda: V.tensor_copy(out, a))
+
+    def ms(wr, out, c):
+        op("V", "", wr, lambda: V.memset(out, c))
+
+    def scan(rd, wr, out, a, b, init, o0, o1):
+        op("V", rd, wr, lambda: V.tensor_tensor_scan(out, a, b, init, o0, o1))
+
+    def act(rd, wr, out, a, f, **kw):
+        op("S", rd, wr, lambda: A.activation(out, a, f, **kw))
+
+    def quant(rd, wr, q, s, a):
+        op("V", rd, wr, lambda: V.quantize_mx(q, s, a))
+
+    def mm(rd, wr, out, lq, ls, rq, rs):
+        op("P", rd, wr, lambda: g.tensor.matmul_mx(out, lq, ls, rq, rs, True, True))
+
+    def iota(wr, out, pat, base=0, cm=0, whole=False):
+        if whole:
+            op("G", "", wr, lambda: g.iota(out, pat, base, cm))
+        else:
+            op("G", "", wr, lambda: g.iota(out, pat, base, cm, allow_small_or_imprecise_dtypes=True))
+
+    def fill(wr, out, w, c):
+        iota(wr, out, [[0, w]], c)
+
+    def col(k):
+        return T.cols[:, k:k + 1]
+
+    PS = [T.p0, T.p1, T.p2, T.p3]
+    I_ = T.ic[:, 0:1]
+
+    dma("Y", "", "ut", T.ut[:], T.u[:])
+    dma("S", "", "xt", T.xt[:], T.x[:])
+    dma("Y", "", "qw", T.qw[:].bitcast(dt.uint8), T.wc[:])
+    dma("Y", "", "sw", T.sw[:], T.ws[:])
+    dma("Y", "", "vt", T.vt[:], T.v[:])
+
+    iota("pi", T.pi[:, 0:1], [[0, 1]], 0, 1, True)
+    iota("iu", T.iu[:, 0:8], [[16, 8]], 0, 0, True)
+    iota("iof", T.iof[:], [[1, 64]])
+    iota("ioj", T.ioj[:], [[0, 16], [1, 16]])
+    iota("cr", T.cr[:], [[16, 4], [1, 2]])
+    iota("iu2", T.iu[:, 8:20], [[16, 12]], 15, 0, True)
+    iota("kc", T.kc[:], [[16, 16]], 448)
+    fill("yca", T.yc[:, 0:NV], NV, -1)
+    iota("ycb", T.yc[:, NV:12], [[16, NS]], 16 * NV + 15)
+    iota("iob", T.iob[:], [[1, 256]])
+    for b in range(4):
+        fill("tcz%d" % b, T.tc[:, PW * b + C_:PW * b + PW], 16, 0)
+    fill("tb1", T.tb[:, C_:PW], 16, C_)
+    fill("kwz", T.kw[:, C_:PW], 16, 0)
+    fill("srz", T.sr[:, C_:PW], 16, 0)
+    fill("eqt0", T.eqt[:, 0:16], 16, 0)
+    fill("eqt1", T.eqt[:, 32:208], 176, 0)
+    fill("eqs", T.eqs[:, 32:192], 160, 0)
+    fill("stt0", T.stt[:, 0:L_], L_, 0)
+    fill("stt1", T.stt[:, L_:C_], K_, 1)
+    fill("col20", col(20), 1, 16 + IO1 + B16)
+    fill("col21", col(21), 1, 16 + IO1)
+    fill("col23", col(23), 1, 16 + IO2)
+    iota("cw", T.cw[:], [[1, 4], [0, 4]])
+    iota("gx", T.gx[:], [[1, 144]], -B16)
+    fill("gx", T.gx[:, B16 + 15:B16 + 64], 49, 100)
+    iota("gx", T.gx[:, B16 + 64:B16 + 79], [[1, 15]])
+    fill("gx", T.gx[:, B16 + 79:144], 49, 300)
+    iota("thr", T.thr[:, 0:4], [[50, 4]], -51)
+    iota("thr", T.thr[:, 3:7], [[100, 4]], -151)
+    fill("thr", T.thr[:, 3:4], 1, 149)
+    fill("thr", T.thr[:, 4:5], 1, -1)
+    fill("rs", T.rs[:], 8, 1)
+    fill("rs", T.rs[:, 4:5], 1, 0)
+    fill("yd6", T.yd[:, 6:7], 1, 32 * TOP)
+    iota("idr", T.idr[:], [[1, 32]], K_)
+    fill("zr", T.zr[:], 32, 0)
+    iota("olw1", T.olw[:, K_:C_], [[1, 32]], S_)
+    fill("olw2", T.olw[:, C_:PW], 16, -1)
+    fill("tabj", T.tab[:, 32:64], 32, 0)
+    fill("tabk", T.tab[:, 224:B256], 40, 0)
+    iota("tabi", T.tab[:, IO1:TOP], [[0, 2], [1, 200]])
+    fill("tabt", T.tab[:, TOP:688], 8, 0)
+    fill("aa", T.aa[:], 192, 1)
+
+    ms("rm", T.rm[:], 1.0)
+    ms("ones", T.ones[:], 1.0)
+    ms("rm", T.rm[:, 0::16], 0.0)
+    ts("pi", "pj0", T.pi[:, 4:5], T.pi[:, 0:1], 15, ALU.bitwise_and)
+    ts("pi", "pj1", T.pi[:, 5:6], T.pi[:, 0:1], 2, ALU.arith_shift_right, 3, ALU.bitwise_and)
+    ts("pi", "pj2", T.pi[:, 6:7], T.pi[:, 0:1], 3, ALU.bitwise_and)
+    ts("pi", "pj3", T.pi[:, 7:8], T.pi[:, 0:1], 4, ALU.arith_shift_right, 1, ALU.bitwise_and)
+    cp("iu", "offu", T.offu[:], T.iu[:, 0:8])
+    cp("pj0 pj1 pj2 pj3", "ic", T.ic[:, 0:4], T.pi[:, 4:8])
+    for b in range(4):
+        op("G", "ones", "et%d" % b, lambda: g.affine_select(T.et[:, 512 * b:512 * b + 512], T.ones[:], [[-1, 512]], ALU.is_equal, 0.0, b, 4))
+    ms("btz", T.bt[:, 0:384], 0.0)
+    ms("col16", T.cols[:, 16:20:2], 0.5)
+    ts("ioj ic", "dm", T.dm[:], T.ioj[:], I_, ALU.is_equal)
+    ts("cr ic", "dc64", T.dc[:, 0:8], T.cr[:], I_, ALU.add, 1.0 / 64, ALU.mult)
+    ts("cr ic", "dc16", T.dc[:, 8:10], T.cr[:, 0:2], I_, ALU.add, 1.0 / 16, ALU.mult)
+    ts("ioj ic", "gt", T.gt[:], T.ioj[:, 0:192], I_, ALU.is_gt)
+    ts("ioj ic", "bm", T.bm[:], T.ioj[:, 0:192], I_, ALU.is_le, 512.0, ALU.mult)
+    cp("iu2", "bco", T.bco[:], T.iu[:, 8:20])
+    ts("kc ic", "kc", T.kc[:], T.kc[:], I_, ALU.add)
+
+    HALF = 0.4921875
+    act("ic", "dca", T.dc[:, 10:11], I_, AF.Identity, scale=0.75, bias=HALF)
+    act("ic", "dcb", T.dc[:, 11:12], I_, AF.Identity, scale=0.75, bias=HALF + 0.75)
+    for h in range(2):
+        act("iof dca dcb", "yyc%d" % h, T.yy[:, 192 * h + 176:192 * h + 192], T.iof[:, 0:16], AF.Identity, scale=12.0, bias=T.dc[:, 10 + h:11 + h])
+    for h in range(2):
+        act("iof dc16", "yya%d" % h, T.yy[:, 192 * h:192 * h + 16], T.iof[:, 0:16], AF.Identity, scale=T.dc[:, 8 + h:9 + h], bias=HALF)
+        for lp in range(4):
+            a = 192 * h + 16 + 40 * lp
+            act("iof dc64", "yyb%d%d" % (h, lp), T.yy[:, a:a + 40], T.iof[:, 14:54], AF.Identity, scale=T.dc[:, 2 * lp + h:2 * lp + h + 1], bias=HALF)
+
+    def table(lo, hi, rd, parts):
+        for h in range(2):
+            cp(rd, "yi%d%d" % (h, lo), T.yi[:, 192 * h + lo:192 * h + hi], T.yy[:, 192 * h + lo:192 * h + hi])
+        ts("yi0%d" % lo, "y20%d" % lo, T.y2[:, lo:hi], T.yi[:, lo:hi], 257.0, ALU.mult, 256.0, ALU.add)
+        ts("yi1%d" % lo, "y21%d" % lo, T.y2[:, 192 + lo:192 + hi], T.yi[:, 192 + lo:192 + hi], 256.0, ALU.mult)
+        for key, at, a, b in parts:
+            tt("y20%d y21%d" % (lo, lo), key, T.tab[:, at:at + b - a], T.y2[:, a:b], T.y2[:, 192 + a:192 + b], ALU.subtract)
+
+    table(176, 192, "yyc0 yyc1", [("tab256", B256, 176, 192)])
+    quant("ut", "qu", T.qu[:], T.su[:], T.ut[:])
+    cp("tab256", "qq", T.qq[:], T.tab[:, B256:B256 + 16])
+    cp("qu offu", "qur", T.qur[:].bitcast(dt.uint32), T.qu[:].bitcast(dt.uint32).indirect(T.offu[:]))
+    cp("qu offu", "sur", T.sur[:], T.su[:].indirect(T.offu[:]))
+    quant("xt", "qt", T.qt[:, 0:C_], T.st[:, 0:C_], T.xt[:])
+    mm("qur sur qt", "pp", T.pp[:, 0:C_], T.qur[:], T.sur[:], T.qt[:, 0:C_], T.st[:, 0:C_])
+
+    for k, c, s, b in [(0, 0, 1.0, 0.0), (1, 0, 1.0, -1.0), (2, 1, 4.0, 3.0), (3, 1, 4.0, -1.0), (4, 0, 16.0, 15.0),
+                       (5, 2, 32.0 * 40, 32.0 * (B64 - 14 + 52)), (8, 0, 1.0, 16.0), (22, 2, 40.0, 16.0 + IO2 + B64 - 14)]:
+        act("ic", "col%d" % k, col(k), T.ic[:, c:c + 1], AF.Identity, scale=s, bias=b)
+    act("ic", "yd0", T.yd[:, 0:1], I_, AF.Identity, scale=32.0, bias=32.0 * BNS)
+    act("ic", "yd3", T.yd[:, 3:4], I_, AF.Identity, scale=32.0, bias=32.0 * B256)
+    ts("dm", "wu", T.hh[:, 48:64], T.dm[:, 0:16], -257.0, ALU.mult, 1.0, ALU.add)
+    cp("dm", "eqt", T.eqt[:, 16:32], T.dm[:, 0:16])
+    cp("dm", "eqa", T.eqs[:, 0:16], T.dm[:, 0:16])
+    ts("dm", "eqb", T.eqs[:, 16:32], T.dm[:, 0:16], -1.0, ALU.mult)
+    tt("wu gt", "wt", T.wt[:, 0:16], T.hh[:, 48:64], T.gt[:, 0:16], ALU.subtract)
+
+    def constants_2():
+        for f in range(4):
+            ts("iof col%d" % f, "mk%d" % f, T.mk[:, 16 * f:16 * f + 16], T.iof[:, 0:16], col(f), ALU.is_equal)
+        ts("ones col4", "coff", T.coff[:], T.ones[:, 0:4], col(4), ALU.mult)
+        ts("ic", "col17", T.cols[:, 17:20:2], T.ic[:, 0:2], 1.0, ALU.min, -0.5, ALU.add)
+
+    def constants_3():
+        ts("cw ic", "cw", T.cw[:], T.cw[:], T.ic[:, 1:2], ALU.is_equal, 100.0, ALU.mult)
+        ts("dm", "mm", T.mm[:], T.dm[:, 0:16], 20.0, ALU.mult, -120.0, ALU.add)
+        ts("ic", "col9", col(9), T.ic[:, 3:4], 16.0, ALU.mult, I_, ALU.add)
+        tt("mm cw", "mm", T.mm[:], T.mm[:], T.cw[:], ALU.add)
+        ts("iof col9", "aoff", T.aoff[:], T.iof[:, 0:64:32], col(9), ALU.add)
+        table(0, 176, "yya0 yya1 " + " ".join("yyb%d%d" % (h, lp) for h in range(2) for lp in range(4)),
+              [("tab16", B16, 0, 16), ("tab64", B64, 16, 176)])
+        quant("et0 et1 et2 et3", "qe", T.qe[:], T.se[:], T.et[:])
+
+    def ranks(row, rkey):
+        scan("rm mskb", "scb", T.sc[:, 96:192], T.rm[:, 0:96], T.msk[:, 96:192], 0.0, ALU.mult, ALU.add)
+        scan("rm msk", "sc", T.sc[:, 0:96], T.rm[:, 0:96], T.msk[:, 0:96], 0.0, ALU.mult, ALU.add)
+
+        def s(c):
+            return T.sc[:, 16 * c + 15:16 * c + 16]
+
+        def compare(c):
+            e = 16 * c + 16
+            ts(rkey + " sc scb", "cma%d" % c, T.cmp[:, 192 * c:192 * c + e], row[:, 0:e], s(c), ALU.is_le)
+            ts(rkey + " sc scb", "cmb%d" % c, T.cmp[:, 192 * c + e:192 * c + 192], row[:, e:192], s(c), ALU.is_lt)
+        for k in range(NS):
+            act(rkey + " scb", "sga%d sgb%d" % (k, k), T.sg[:, PW * k:PW * k + 192], row[:, 0:192], AF.Sign, scale=-1.0, bias=s(NV + k))
+        tt(rkey + " sc scb bco", "eq", T.eq[:], T.sc[:].indirect(T.bco[:]), row[:, 0:192], ALU.is_equal)
+        compare(0)
+        scan("eq gt", "cor", T.cor[:], T.eq[:], T.gt[:], 0.0, ALU.add, ALU.mult)
+        compare(1)
+        tt("cor ycb", "sgy", T.sg[:, 192::PW], T.yc[:, NV:12], T.cor[:, 16 * NV + 15::16], ALU.subtract)
+        tt("cor yca", "yv", T.gl[:, 16:16 + NV], T.yc[:, 0:NV], T.cor[:, 15:16 * NV:16], ALU.subtract)
+        for c in range(2, NV):
+            compare(c)
+        for k in range(NS):
+            e = PW * k + 16 * (NV + k) + 16
+            act("sga%d" % k, "sga%d gf%d" % (k, k), T.sg[:, PW * k:e], T.sg[:, PW * k:e], AF.Relu, scale=-1.0, accum_out=T.gl[:, k:k + 1])
+        for k in range(NS):
+            e = PW * k + 16 * (NV + k) + 16
+            act("sgb%d sgy" % k, "sgb%d lb%d" % (k, k), T.sg[:, e:PW * k + 193], T.sg[:, e:PW * k + 193], AF.Relu, accum_out=T.gl[:, 8 + k:9 + k])
+        for c in range(NV):
+            scan("ones yv cma%d cmb%d" % (c, c), "cs%d" % c, T.cs[:, 192 * c:192 * c + 192], T.ones[:, 0:192], T.cmp[:, 192 * c:192 * c + 192],
+                 T.gl[:, 16 + c:17 + c], ALU.mult, ALU.add)
+        cp(" ".join("cs%d" % c for c in range(NV)), "rka", T.rk[:, 0:NV], T.cs[:, 191::192])
+        tt(" ".join("gf%d lb%d" % (k, k) for k in range(NS)), "rkb", T.rk[:, NV:12], T.gl[:, 8:8 + NS], T.gl[:, 0:NS], ALU.subtract)
+        cp("rka rkb", "roff", T.roff[:], T.rk[:, 0:12])
+
+    def rising(rd, a, w):
+        scan(rd + " bm", "m2", T.m2[:, 0:w], T.bm[:, 0:w], a, 0.0, ALU.add, ALU.min)
+        return T.m2[:, 15:w:16]
+
+    def new_state(more):
+        ts("qq", "qoff", T.qoff[:], T.qq[:], float(C_), ALU.min)
+        if more:
+            tt("kc qq", "hh0", T.hh[:, 0:16], T.kc[:], T.qq[:], ALU.subtract)
+        tt("tb tb1 qoff dm", "m1", T.m1[:], T.tb[:].indirect(T.qoff[:]), T.dm[:], ALU.mult)
+        if more:
+            tt("hh0 qq", "hh1", T.hh[:, 16:32], T.hh[:, 0:16], T.qq[:], ALU.min)
+        scan("m1 rm", "m2", T.m2[:], T.rm[:], T.m1[:], 0.0, ALU.mult, ALU.add)
+        if more:
+            cp("hh1", "uq", T.uq[:], T.hh[:, 16:32])
+        cp("m2", "to", T.to[:], T.m2[:, 15::16])
+        for b in range(4):
+            rd = "to tcz%d tcs%d tca%d" % (b, b, b)
+            w = T.tc[:, PW * b:PW * b + PW].indirect(T.to[:])
+            if b < 2:
+                cp(rd, "ft%d" % b, T.ft[:, b::4], w)
+            else:
+                act(rd, "ft%d" % b, T.ft[:, b::4], w, AF.Copy)
+        quant("ft0 ft1 ft2 ft3", "qf", T.qf[:], T.sf[:], T.ft[:])
+
+    tt("dm", "msk mskb pp", T.msk[:], T.pp[:, 0:C_], T.dm[:, 0:C_], ALU.mult)
+    act("", "kws kwa pp", T.kw[:, 0:C_], T.pp[:, 0:C_], AF.Copy)
+    ranks(T.kw, "kws kwa")
+    cp("roff iob", "tb", T.tb[:, 0:C_].indirect(T.roff[:]), T.iob[:, 0:C_])
+    for b in range(4):
+        act("xt", "tcs%d tca%d" % (b, b), T.tc[:, PW * b:PW * b + C_], T.xt[:, b::4], AF.Copy)
+    for k in range(4):
+        act("wt", "wt", T.wt[:, 16 << k:32 << k], T.wt[:, 0:16 << k], AF.Copy)
+    new_state(True)
+
+    for t in range(R_):
+        ko, ka, qb, sb = T["ko%d" % t], T["ka%d" % t], T["qb%d" % t], T["sb%d" % t]
+        for b in range(4):
+            mm("qw sw qf", "p%d" % b, PS[b][:, 0:S_], T.qw[:, 128 * b:128 * b + 128], T.sw[:, 128 * b:128 * b + 128], T.qf[:], T.sf[:])
+            act("ft%d" % b, "f6%d" % b, T.f64[:, 256 * b:256 * b + 256], T.ft[:, b::4], AF.Copy, scale=64.0)
+        cp("uq iob", "pr", T.pr[:].indirect(T.uq[:, 0:8]), T.iob[:, 0:128])
+        for b in range(4):
+            pl64 = T.t64[:, 256 * b:256 * b + 256]
+            tt("f6%d" % b, "t6%d p%d" % (b, b), pl64, PS[b][:, 0:S_], T.f64[:, 256 * b:256 * b + 256], ALU.add)
+            if b < 2:
+                act("t6%d" % b, "tt%d" % b, T.tt[:, b::4], pl64, AF.Copy, scale=1.0 / 64)
+        for b in range(2, 4):
+            ts("t6%d" % b, "tt%d" % b, T.tt[:, b::4], T.t64[:, 256 * b:256 * b + 256], 1.0 / 64, ALU.mult)
+        quant("tt0 tt1 tt2 tt3", "qt", T.qt[:], T.st[:], T.tt[:])
+        mm("qur sur qt", "pp", T.pp[:, 0:S_], T.qur[:], T.sur[:], T.qt[:], T.st[:])
+        act("kws kwa kwz to", "kp", T.kp[:], T.kw[:].indirect(T.to[:]), AF.Copy)
+        act("", "psb pp", T.psb[:], T.pp[:, 0:S_], AF.Copy)
+        cp("uq iob", "pr", T.pr[:].indirect(T.uq[:, 8:16]), T.iob[:, 128:256])
+        cp("m2", "poff", T.poff[:], rising("pr", T.pr[:, 0:C_], C_))
+        tt("psb poff dm", "mskb", T.msk[:, 96:192], T.psb[:].indirect(T.poff[:, 6:12]), T.dm[:, 0:96], ALU.mult)
+        tt("psb poff dm", "msk", T.msk[:, 0:96], T.psb[:].indirect(T.poff[:, 0:6]), T.dm[:, 0:96], ALU.mult)
+        act("psb poff", "pc", T.pc[:], T.psb[:].indirect(T.poff[:]), AF.Copy)
+        ranks(T.pc, "pc")
+        act("stt0 stt1 roff", "sr", T.sr[:, 0:C_], T.stt[:].indirect(T.roff[:]), AF.Copy)
+        tt("eqt eqt0 eqt1 roff pc", "k0", T.k0[:], T.eqt[:, 16:208].indirect(T.roff[:]), T.pc[:], ALU.mult)
+        tt("eqt roff pc", "msk mskb", T.msk[:], T.eqt[:, 0:192].indirect(T.roff[:]), T.pc[:], ALU.mult)
+        act("k0", "k0 koa", T.k0[:], T.k0[:], AF.Identity, accum_out=ko[:, 0:1])
+        op("V", "msk mskb", "kob", lambda: V.tensor_reduce(ko[:, 1:2], T.msk[:], AX.X, ALU.add))
+        order("G", ["koa", "kob"], [])
+        cnt["sent"] += _send(g, T, topo, core, relay_k, ka[:, 0:2], ko[:, 0:2], "aK%d" % t)
+        arrives("ka", "aK%d" % t, len(topo.engines(from_k, core)))
+        arrives("qba", "aB%d" % t, len(topo.engines(from_b, core)) + len(topo.engines(from_s, core)))
+
+        tt("eqs eqa eqb roff pr", "eq", T.eq[:], T.eqs[:].indirect(T.roff[:]), T.pr[:, 0:C_], ALU.mult)
+        act("rka rkb", "hh1", T.hh[:, 16:28], T.rk[:, 0:12], AF.Identity, scale=-float(K_), bias=float(K_ * L_))
+        act("sr srz qoff", "sp", T.jk[:, 0:256], T.sr[:].indirect(T.qoff[:]), AF.Copy)
+        for c in range(2):
+            act("eq", "cma%d cmb%d gll%d" % (c, c, c), T.cmp[:, 192 * c:192 * c + 192], T.eq[:], AF.Relu, scale=1.0 - 2 * c, accum_out=T.gl[:, 5 + c:6 + c])
+        scan("sr ones", "pre", T.pre[:], T.ones[:, 0:C_], T.sr[:, 0:C_], -1.0, ALU.mult, ALU.add)
+        if t == 0:
+            constants_2()
+        d = rising("pre", T.pre[:], C_)
+        scan("sp ones", "px", T.jk[:, 256:512], T.ones[:, 0:256], T.jk[:, 0:256], 0.0, ALU.mult, ALU.add)
+        tt("m2 hh1", "hh0", T.hh[:, 0:12], d, T.hh[:, 16:28], ALU.max)
+        tt("px coff mk0 mk1 mk2 mk3", "cor", T.cor[:, 0:64], T.jk[:, 256:512].indirect(T.coff[:]), T.mk[:], ALU.mult)
+        cp("gll0 gll1", "plb", T.pl[:, 10:12], T.gl[:, 5:7])
+        for b in range(4):
+            act("plb t6%d" % b, "bt%d" % b, T.bt[:, 384 + b::4], T.t64[:, 256 * b:256 * b + 256].indirect(T.pl[:, 10:12]), AF.Copy, scale=1.0 / 64)
+        scan("cor rm", "cum", T.cor[:, 64:128], T.rm[:, 0:64], T.cor[:, 0:64], 0.0, ALU.mult, ALU.add)
+        cp("hh0", "doff", T.doff[:], T.hh[:, 0:12])
+        tt("cum cor col16 col17", "lim", T.sig[:, 0:4], T.cor[:, 79:128:16], T.cols[:, 16:20], ALU.add)
+        tt("cum cor col20 col21 col22 col23", "bia", T.sig[:, 8:12], T.cor[:, 79:128:16], T.cols[:, 20:24], ALU.add)
+        tt("cum cor thr", "thr1", T.thr[:, 1:2], T.cor[:, 79:80], T.cor[:, 95:96], ALU.subtract)
+        quant("btz bt0 bt1 bt2 bt3", "qbo", qb[:, 32:160], sb[:, 128:256], T.bt[:])
+        order("G", ["qbo"], [])
+        cnt["sent"] += _send_b(g, T, topo, core, relay_b, relay_s, qb[:, 128:160].bitcast(dt.uint8), sb[:, 128:256], t)
+        if t:
+            fill("aa", T.aa[:], 192, 1)
+        cp("doff pr", "pls", T.pls[:].indirect(T.doff[:]), T.pr[:, 0:C_])
+        for f in range(4):
+            act("iob lim", "tbs%d" % f, T.tbs[:, 176 * f:176 * f + 176], T.iob[:, 0:176], AF.Sign, scale=-1.0, bias=T.sig[:, f:f + 1])
+        cp("m2", "pl", T.pl[:, 0:10], rising("pls", T.pls[:, 0:K_], K_))
+        act("kp pl", "kws", T.kw[:, 0:K_], T.kp[:].indirect(T.pl[:, 0:10]), AF.Copy)
+        tt("sr srz qoff wt", "m1", T.m1[:], T.sr[:].indirect(T.qoff[:]), T.wt[:], ALU.mult)
+        scan("m1 rm", "m2", T.m2[:], T.rm[:], T.m1[:], 0.0, ALU.mult, ALU.add)
+        ts("m2", "tabn", T.tab[:, BNS:BNS + 16], T.m2[:, 15::16], 256.0, ALU.add)
+        if t == 0:
+            constants_3()
+        if t == R_ - 1:
+            quant("vt", "qv", T.qv[:], T.sv[:], T.vt[:])
+
+        def stayers(b):
+            act("pl t6%d" % b, "tcs%d" % b, T.tc[:, PW * b:PW * b + K_], T.t64[:, 256 * b:256 * b + 256].indirect(T.pl[:, 0:10]), AF.Copy, scale=1.0 / 64)
+        stayers(0)
+
+        for c in range(2):
+            ts("kws ka", "ck%d" % c, T.ck[:, 160 * c:160 * c + 160], T.kw[:, 0:K_], ka[:, c:c + 1], ALU.is_le)
+        for c in range(2):
+            scan("ones ck%d" % c, "cn%d" % c, T.cn[:, 160 * c:160 * c + 160], T.ones[:, 0:K_], T.ck[:, 160 * c:160 * c + 160], 0.0, ALU.mult, ALU.add)
+        ts("cn0 ic", "qoa", T.qo[:, 0:1], T.cn[:, 159:160], I_, ALU.add)
+        cp("cn0 cn1", "noff", T.noff[:], T.cn[:, 159::160])
+        for f, key, o in [(2, "hi1", T.sig[:, 5:6]), (3, "yd5", T.yd[:, 5:6]), (0, "hi0", T.sig[:, 4:5]), (1, "yd4", T.yd[:, 4:5])]:
+            act("noff tbs0 tbs1 tbs2 tbs3 bia", "ju%d %s" % (f, key), T.ju[:, 32 * f:32 * f + 32], T.tbs[:, 176 * f:176 * f + 176].indirect(T.noff[:]),
+                AF.Identity, scale=16.0, bias=T.sig[:, 8 + f:9 + f], accum_out=o)
+        if t < R_ - 1:
+            for c in range(2):
+                act("ones ka", "ax%d" % c, T.ax[:, 32 * c:32 * c + 32], T.ones[:, 0:32], AF.Copy, scale=ka[:, c:c + 1])
+        for b in range(1, 4):
+            stayers(b)
+        if t == R_ - 1:
+            act("pls", "olw0", T.olw[:, 0:K_], T.pls[:, 0:K_], AF.Copy)
+        for b in range(4):
+            mm("qe qba qbo", "p%d" % b, PS[b][:, 0:128], T.qe[:, 128 * b:128 * b + 128], T.se[:, 128 * b:128 * b + 128], qb[:, 0:128], sb[:, 96:224])
+        for b in range(4):
+            act("", "tca%d p%d" % (b, b), T.tc[:, PW * b + K_:PW * b + C_], PS[b][:, 0:32], AF.Copy)
+        ts("cn1 col8", "qob", T.qo[:, 1:2], T.cn[:, 319:320], col(8), ALU.add)
+        cp("qoa qob zr", "aa", T.aa[:].indirect(T.qo[:]), T.zr[:])
+        scan("aa ones", "tb", T.tb[:, 0:C_], T.ones[:, 0:C_], T.aa[:], -1.0, ALU.mult, ALU.add)
+        tt("hi0 hi1 yd4 yd5", "yd1", T.yd[:, 1:3], T.sig[:, 4:6], T.yd[:, 4:6], ALU.subtract)
+        ts("yd1 col5", "sm0", T.sm[:, 0:1], T.yd[:, 2:3], col(5), ALU.is_gt, 32.0 * 64, ALU.mult)
+        ts("yd1 sm0", "voff", T.voff[:, 0:1], T.yd[:, 1:2], T.sm[:, 0:1], ALU.add, 1.0 / 32, ALU.mult)
+        cp("qoa qob idr", "tb", T.tb[:, 0:C_].indirect(T.qo[:]), T.idr[:])
+        tt("gx voff mm", "sm1", T.sm[:, 16:32], T.gx[:].indirect(T.voff[:, 0:1]), T.mm[:], ALU.add)
+        op("V", "sm1", "sm2", lambda: V.tensor_reduce(T.sm[:, 1:2], T.sm[:, 16:32], AX.X, ALU.max))
+        if t < R_ - 1:
+            op("V", "ax0 ax1", "ay", lambda: V.transpose(T.ay[:], T.ax[:]))
+        ts("sm2 thr thr1", "sm3", T.sm[:, 32:39], T.thr[:, 0:7], T.sm[:, 1:2], ALU.is_lt)
+        tt("sm3 yd0 yd1 yd3 yd4 yd5 yd6", "sm4", T.sm[:, 40:47], T.sm[:, 32:39], T.yd[:, 0:7], ALU.mult)
+        scan("sm4 rs", "sm5", T.sm[:, 48:55], T.rs[:, 0:7], T.sm[:, 40:47], 0.0, ALU.mult, ALU.max)
+        ts("sm5", "xo", T.xo[:], T.sm[:, 51:55:3], 1.0 / 32, ALU.mult)
+        cp("xo tabj tabk tabi tabt tabn tab16 tab64 tab256", "gq", T.gq[:], T.tab[:].indirect(T.xo[:]))
+        tt("gq", "qq", T.qq[:], T.gq[:, 0:16], T.gq[:, 16:32], ALU.add)
+        if t < R_ - 1:
+            act("ay aoff", "kwa", T.kw[:, K_:C_], T.ay[:].indirect(T.aoff[:]), AF.Copy)
+        new_state(t < R_ - 1)
+
+    mm("qv qf", "py", T.py[:, 0:S_], T.qv[:], T.sv[:], T.qf[:], T.sf[:])
+    act("olw0 olw1 olw2 to", "olr", T.olr[:], T.olw[:].indirect(T.to[:]), AF.Copy)
+    dma("Y", "qf", "", T.oc[:], T.qf[:].bitcast(dt.uint8))
+    act("", "ys py", T.ys[:], T.py[:, 0:S_], AF.Copy)
+    dma("S", "ys", "", T.y[:], T.ys[:])
+    for k in range(4):
+        dma("Y", "qf", "", T.osc[4 * k:4 * k + 4, :], T.sf[32 * k:32 * k + 4, :])
+    dma("S", "olr", "", T.ol[:], T.olr[0:128:16, :])
+    for s, v in cnt.items():
+        if v:
+            g.wait_ge(T.sem[s], v)

@@ -3,11 +3,17 @@ from concourse.mybir import dt, AluOpType, AxisListType, ActivationFunctionType
 
 ALU, AF, AX = AluOpType, ActivationFunctionType, AxisListType
 S_, C_, L_, R_ = 256, 192, 32, 3
+Q1, Q2 = 14, 52
 K_ = C_ - L_
 NV = 7
 NS = 12 - NV
+CW = C_ + 1
 PW = 208
-BNS, B16, B64, B256, IO1, IO2, TOP = 0, 16, 64, 264, 280, 480, 680
+GAP = 512
+B64, IO, TABW = 16, 224, 424
+ZS = L_ + 6
+ZW = 2 * ZS - 1
+KW = K_ + 2
 CX, U8, BF, F32, I32, U16 = "float8_e4m3fn_x4", "uint8", "bfloat16", "float32", "int32", "uint16"
 
 
@@ -16,30 +22,29 @@ def _sb(n, d):
 
 
 SCRATCH = {
-    "xt": _sb(768, BF), "ut": _sb(512, BF), "vt": _sb(512, BF), "et": _sb(2048, BF),
+    "xt": _sb(768, BF), "ut": _sb(512, BF), "vt": _sb(512, BF), "et": _sb(528, BF),
     "qu": _sb(128, CX), "su": _sb(128, U8), "qur": _sb(128, CX), "sur": _sb(128, U8),
     "qv": _sb(128, CX), "sv": _sb(128, U8), "qw": _sb(512, CX), "sw": _sb(512, U8), "qe": _sb(512, CX), "se": _sb(512, U8),
     "qf": _sb(256, CX), "sf": _sb(256, U8), "qt": _sb(256, CX), "st": _sb(256, U8),
     "ft": _sb(1024, BF), "f64": _sb(1024, BF), "tt": _sb(1024, BF), "t64": _sb(1024, BF), "tc": _sb(4 * PW, BF), "bt": _sb(512, BF),
-    "pi": _sb(8, I32), "ic": _sb(8, F32), "iu": _sb(24, I32), "offu": _sb(8, U16), "bco": _sb(12, U16), "coff": _sb(4, U16),
-    "ioj": _sb(256, BF), "iob": _sb(256, BF), "iof": _sb(64, F32), "ones": _sb(512, BF),
-    "dm": _sb(256, BF), "rm": _sb(256, BF), "gt": _sb(192, BF), "wt": _sb(256, BF), "bm": _sb(192, BF), "mk": _sb(64, BF),
-    "eqt": _sb(208, BF), "eqs": _sb(192, BF), "stt": _sb(192, BF), "yc": _sb(16, F32), "kc": _sb(16, F32), "idr": _sb(32, BF), "zr": _sb(32, BF),
-    "gx": _sb(144, F32), "mm": _sb(16, F32), "cw": _sb(16, F32), "aoff": _sb(2, U16), "tab": _sb(688, F32),
-    "dc": _sb(16, F32), "cr": _sb(8, F32), "yy": _sb(384, F32), "yi": _sb(384, I32), "y2": _sb(384, F32), "cols": _sb(32, F32),
+    "pi": _sb(8, I32), "ic": _sb(4, F32), "iu": _sb(24, I32), "cu": _sb(24, U16), "aoff": _sb(2, U16),
+    "ioj": _sb(256, BF), "iob": _sb(256, BF), "iof": _sb(64, F32), "cr": _sb(8, F32), "dc": _sb(16, F32),
+    "dm": _sb(256, BF), "rm": _sb(256, BF), "gt": _sb(192, BF), "bm": _sb(192, BF), "wt": _sb(256, BF), "rs": _sb(4 * CW, BF), "rk2": _sb(2 * KW, BF),
+    "eqt": _sb(208, BF), "eqs": _sb(192, BF), "nst": _sb(192, BF), "yc": _sb(12, F32), "kc": _sb(16, F32), "idr": _sb(32, BF), "zr": _sb(32, BF),
+    "lv": _sb(112, BF), "mw": _sb(16, F32), "tab": _sb(TABW, F32), "yy": _sb(384, F32), "yr": _sb(384, F32), "xs": _sb(8, F32),
+    "zi": _sb(ZW, F32), "zm": _sb(ZW, F32), "zz": _sb(ZW, F32), "zo": _sb(ZW, F32),
     "psb": _sb(256, F32), "pc": _sb(192, F32), "msk": _sb(192, F32), "sc": _sb(192, F32), "eq": _sb(192, BF), "cor": _sb(192, BF),
-    "cmp": _sb(192 * NV, BF), "cs": _sb(192 * NV, BF), "sg": _sb(PW * NS, BF), "gl": _sb(32, F32),
-    "rk": _sb(16, F32), "roff": _sb(12, U16), "k0": _sb(192, F32),
-    "sr": _sb(PW, BF), "pre": _sb(192, BF), "hh": _sb(64, F32), "doff": _sb(12, U16),
-    "pr": _sb(256, BF), "pls": _sb(K_ * L_ + 16, BF), "m1": _sb(256, BF), "m2": _sb(256, BF), "pl": _sb(12, U16), "poff": _sb(12, U16),
-    "kw": _sb(PW, F32), "kp": _sb(256, F32), "sig": _sb(16, F32), "jk": _sb(512, BF), "tbs": _sb(4 * 176, BF),
-    "ck": _sb(320, BF), "cn": _sb(320, BF), "noff": _sb(2, U16), "qo": _sb(2, U16), "aa": _sb(192, BF), "tb": _sb(PW, BF),
-    "ju": _sb(128, F32), "yd": _sb(8, F32), "thr": _sb(8, F32), "rs": _sb(8, F32), "sm": _sb(64, F32),
-    "voff": _sb(2, U16), "xo": _sb(2, U16), "gq": _sb(32, F32), "qq": _sb(16, F32), "qoff": _sb(16, U16), "to": _sb(16, U16),
+    "cmp": _sb(CW * 12, BF), "cs": _sb(CW * NV, BF), "gl": _sb(24, F32), "roff": _sb(12, U16), "k0": _sb(192, F32), "k1": _sb(192, F32),
+    "nsr": _sb(PW, BF), "pre": _sb(192, BF), "hh": _sb(32, F32), "doff": _sb(12, U16), "jk": _sb(4 * 192, BF),
+    "pr": _sb(C_ + S_, BF), "pls": _sb((K_ + 16) * L_ + 16, BF), "m1": _sb(256, BF), "m2": _sb(256, BF), "m3": _sb(256, BF), "m4": _sb(256, BF),
+    "m5": _sb(192, BF), "pl": _sb(12, U16), "poff": _sb(12, U16),
+    "kw": _sb(PW, F32), "kp": _sb(256, F32), "ck": _sb(2 * KW, BF), "cn": _sb(2 * KW, BF), "noff": _sb(2, U16), "qo": _sb(2, U16),
+    "aa": _sb(192, BF), "tb": _sb(PW, BF), "ju": _sb(64, BF), "sm": _sb(32, F32), "tn": _sb(16, F32),
+    "xo": _sb(4, U16), "vo": _sb(4, U16), "gq": _sb(64, F32), "cand": _sb(96, F32), "qoff": _sb(16, U16), "to": _sb(16, U16),
     "uq": _sb(16, U16), "ax": _sb(64, F32), "ay": _sb(64, F32), "olw": _sb(PW, F32), "olr": _sb(256, F32), "ys": _sb(256, F32),
-    "p0": ("psum", [128, 512], F32), "p1": ("psum", [128, 512], F32), "p2": ("psum", [128, 512], F32), "p3": ("psum", [128, 512], F32),
-    "pp": ("psum", [128, 512], F32), "py": ("psum", [128, 512], F32),
 }
+for _t in ["p0", "p1", "p2", "p3", "pp", "pq"]:
+    SCRATCH[_t] = ("psum", [128, 512], F32)
 for _t in range(R_):
     SCRATCH["ko%d" % _t] = _sb(8, F32)
     SCRATCH["ka%d" % _t] = _sb(8, F32)
@@ -76,443 +81,456 @@ def _send_b(g, T, topo, src, dst, dst2, codes, scales, t):
     return 2 * h
 
 
+def _hand_on(g, core, T, topo):
+    cores = list(T.cores)
+    for r in range(len(cores)):
+        src, dst = cores[r], cores[(r + 1) % len(cores)]
+        rk, rb, rs = _relays(src, dst, topo)
+        sent = 0
+        for t in range(R_):
+            if core == rk:
+                g.wait_ge(T.sem["aK%d" % t], len(topo.engines(src, core)))
+                sent += _send(g, T, topo, core, dst, T["ka%d" % t][:, 0:2], T["ka%d" % t][:, 0:2], "aK%d" % t)
+            if core in (rb, rs):
+                ap = T["qb%d" % t][:, 0:32].bitcast(dt.uint8) if core == rb else T["sb%d" % t][:, 96:128]
+                g.wait_ge(T.sem["aB%d" % t], len(topo.engines(src, core)) // 2)
+                sent += _send(g, T, topo, core, dst, ap, ap, "aB%d" % t)
+        if sent:
+            g.wait_ge(T.sem.sent, sent)
+
+
 def rank_program(g, core, T, topo):
     cores = list(T.cores)
     n = len(cores)
     rank = T.rank_of(core)
     if rank is None:
-        for r in range(n):
-            src, dst = cores[r], cores[(r + 1) % n]
-            rk, rb, rs = _relays(src, dst, topo)
-            sent = 0
-            for t in range(R_):
-                if core == rk:
-                    g.wait_ge(T.sem["aK%d" % t], len(topo.engines(src, core)))
-                    sent += _send(g, T, topo, core, dst, T["ka%d" % t][:, 0:2], T["ka%d" % t][:, 0:2], "aK%d" % t)
-                if core in (rb, rs):
-                    ap = T["qb%d" % t][:, 0:32].bitcast(dt.uint8) if core == rb else T["sb%d" % t][:, 96:128]
-                    g.wait_ge(T.sem["aB%d" % t], len(topo.engines(src, core)) // 2)
-                    sent += _send(g, T, topo, core, dst, ap, ap, "aB%d" % t)
-            if sent:
-                g.wait_ge(T.sem.sent, sent)
-        return
+        return _hand_on(g, core, T, topo)
     relay_k, relay_b, relay_s = _relays(core, cores[(rank + 1) % n], topo)
     from_k, from_b, from_s = _relays(cores[(rank - 1) % n], core, topo)
+
+    def v(name, a=0, b=None, s=1, by=None, cast=None):
+        b = SCRATCH[name][1][1] if b is None else b
+        ap = T[name][:, a:b:s]
+        if cast is not None:
+            ap = ap.bitcast(cast)
+        use = [(name, _bits(range(a, b, s)))]
+        if by is not None:
+            ap, use = ap.indirect(by[0]), use + by[1]
+        return ap, use
+
+    def col(name, k):
+        return v(name, k, k + 1)
 
     Q = {"V": g.vector, "S": g.scalar, "P": g.tensor, "G": g, "Y": g.sync}
     cnt = {"cV": 0, "cS": 0, "cP": 0, "cG": 0, "sent": 0}
     clock = {q: {} for q in Q}
-    snap, wrote, read = {}, {}, {}
+    snap, seen = {}, {}
     ndma = [0]
 
-    def order(q, rd, wr):
-        ev = {}
-        for k in rd + wr:
-            if k in wrote:
-                ev[wrote[k]] = 1
-        for k in wr:
-            for e in read.get(k, []):
-                ev[e] = 1
-        ev = [e for e in ev if clock[q].get(e[0], 0) < e[1]]
-        for e in ev:
-            if any(o != e and snap[o].get(e[0], 0) >= e[1] for o in ev):
-                continue
-            Q[q].wait_ge(T.sem[e[0]], e[1])
-            for s, v in snap[e].items():
-                clock[q][s] = max(clock[q].get(s, 0), v)
+    def touches(rd, wr):
+        out = []
+        for views, w in ((rd, False), (wr, True)):
+            for x in views:
+                if isinstance(x, tuple):
+                    for k, (name, bits) in enumerate(x[1]):
+                        out.append((name, 1, w or "bank") if SCRATCH[name][0] == "psum" else (name, bits, w and k == 0))
+        return out
 
-    def done(q, e, rd, wr):
+    def order(q, use):
+        ev = {}
+        for name, bits, w in use:
+            for e, b2, w2 in seen.get(name, []):
+                if bits & b2 and (w or w2) and clock[q].get(e[0], 0) < e[1] and not (w == w2 == "bank" and e[0] == "c" + q):
+                    ev[e] = 1
+        for e in ev:
+            if not any(o != e and snap[o].get(e[0], 0) >= e[1] for o in ev):
+                Q[q].wait_ge(T.sem[e[0]], e[1])
+                for s, k in snap[e].items():
+                    clock[q][s] = max(clock[q].get(s, 0), k)
+
+    def done(q, e, use):
         snap[e] = dict(clock[q])
         snap[e][e[0]] = e[1]
-        for k in rd:
-            read.setdefault(k, []).append(e)
-        for k in wr:
-            wrote[k] = e
-            read[k] = []
+        for name, bits, w in use:
+            if w is True:
+                seen[name] = [o for o in seen.get(name, []) if o[1] & ~bits]
+        for name, bits, w in use:
+            seen.setdefault(name, []).append((e, bits, w))
 
     def op(q, rd, wr, fn):
-        rd, wr = rd.split(), wr.split()
-        order(q, rd, wr)
+        use = touches(rd, wr)
+        order(q, use)
         s = "c" + q
         cnt[s] += 1
         fn().then_inc(T.sem[s], 1)
-        done(q, (s, cnt[s]), rd, wr)
+        done(q, (s, cnt[s]), use)
 
     def dma(q, rd, wr, out, in_):
-        rd, wr = rd.split(), wr.split()
-        order(q, rd, wr)
+        use = touches(rd, wr)
+        order(q, use)
         s = "d%d" % ndma[0]
         ndma[0] += 1
         cnt[s] = 16
         Q[q].dma_start(out, in_).then_inc(T.sem[s], 16)
-        done(q, (s, 16), rd, wr)
+        done(q, (s, 16), use)
 
-    def arrives(key, sem, val):
+    def arrives(views, sem, val):
         snap[(sem, val)] = {sem: val}
-        wrote[key] = (sem, val)
+        for name, bits, w in touches([], views):
+            seen.setdefault(name, []).append(((sem, val), bits, True))
 
     V, A = g.vector, g.scalar
 
-    def ts(rd, wr, out, in0, s1, o0, s2=None, o1=None):
+    def x(a):
+        return a[0] if isinstance(a, tuple) else a
+
+    def ts(out, a, s1, o0, s2=None, o1=None):
         if o1 is None:
-            op("V", rd, wr, lambda: V.tensor_scalar(out, in0, s1, None, o0))
+            op("V", [a, s1], [out], lambda: V.tensor_scalar(out[0], a[0], x(s1), None, o0))
         else:
-            op("V", rd, wr, lambda: V.tensor_scalar(out, in0, s1, s2, o0, o1))
+            op("V", [a, s1, s2], [out], lambda: V.tensor_scalar(out[0], a[0], x(s1), x(s2), o0, o1))
 
-    def tt(rd, wr, out, a, b, o):
-        op("V", rd, wr, lambda: V.tensor_tensor(out, a, b, o))
+    def tt(out, a, b, o):
+        op("V", [a, b], [out], lambda: V.tensor_tensor(out[0], a[0], b[0], o))
 
-    def cp(rd, wr, out, a):
-        op("V", rd, wr, lambda: V.tensor_copy(out, a))
+    def cp(out, a):
+        op("V", [a], [out], lambda: V.tensor_copy(out[0], a[0]))
 
-    def ms(wr, out, c):
-        op("V", "", wr, lambda: V.memset(out, c))
+    def ms(out, c):
+        op("V", [], [out], lambda: V.memset(out[0], c))
 
-    def scan(rd, wr, out, a, b, init, o0, o1):
-        op("V", rd, wr, lambda: V.tensor_tensor_scan(out, a, b, init, o0, o1))
+    def scan(out, a, b, init, o0, o1):
+        op("V", [a, b, init], [out], lambda: V.tensor_tensor_scan(out[0], a[0], b[0], x(init), o0, o1))
 
-    def act(rd, wr, out, a, f, **kw):
-        op("S", rd, wr, lambda: A.activation(out, a, f, **kw))
+    def reduce(out, a, o):
+        op("V", [a], [out], lambda: V.tensor_reduce(out[0], a[0], AX.X, o))
 
-    def quant(rd, wr, q, s, a):
-        op("V", rd, wr, lambda: V.quantize_mx(q, s, a))
+    def act(out, a, f=AF.Copy, scale=None, bias=None, acc=None):
+        kw = {k: x(p) for k, p in (("scale", scale), ("bias", bias), ("accum_out", acc)) if p is not None}
+        op("S", [a, scale, bias], [out, acc], lambda: A.activation(out[0], a[0], f, **kw))
 
-    def mm(rd, wr, out, lq, ls, rq, rs):
-        op("P", rd, wr, lambda: g.tensor.matmul_mx(out, lq, ls, rq, rs, True, True))
+    def quant(q, s, a):
+        op("V", [a], [q, s], lambda: V.quantize_mx(q[0], s[0], a[0]))
 
-    def iota(wr, out, pat, base=0, cm=0, whole=False):
-        if whole:
-            op("G", "", wr, lambda: g.iota(out, pat, base, cm))
+    def mm(bank, w, lq, ls, rq, rs):
+        op("P", [lq, ls, rq, rs], [v(bank)], lambda: g.tensor.matmul_mx(v(bank, 0, w)[0], lq[0], ls[0], rq[0], rs[0], True, True))
+
+    def iota(out, pat, base=0, cm=0):
+        if SCRATCH[out[1][0][0]][2] == I32:
+            op("G", [], [out], lambda: g.iota(out[0], pat, base, cm))
         else:
-            op("G", "", wr, lambda: g.iota(out, pat, base, cm, allow_small_or_imprecise_dtypes=True))
+            op("G", [], [out], lambda: g.iota(out[0], pat, base, cm, allow_small_or_imprecise_dtypes=True))
 
-    def fill(wr, out, w, c):
-        iota(wr, out, [[0, w]], c)
+    def fill(out, c):
+        iota(out, [[0, bin(out[1][0][1]).count("1")]], c)
 
-    def col(k):
-        return T.cols[:, k:k + 1]
+    def plane(name, b, w, stride=S_, at=0, by=None):
+        return v(name, stride * b + at, stride * b + at + w, by=by)
 
-    PS = [T.p0, T.p1, T.p2, T.p3]
-    I_ = T.ic[:, 0:1]
+    I_, I12, I3, I16 = [col("ic", k) for k in range(4)]
+    ones = v("rs", 1, CW)
+    offu, bco, axo = v("cu", 0, 8), v("cu", 8, 20), v("cu", 20, 24)
 
-    dma("Y", "", "ut", T.ut[:], T.u[:])
-    dma("S", "", "xt", T.xt[:], T.x[:])
-    dma("Y", "", "qw", T.qw[:].bitcast(dt.uint8), T.wc[:])
-    dma("Y", "", "sw", T.sw[:], T.ws[:])
-    dma("Y", "", "vt", T.vt[:], T.v[:])
+    dma("Y", [], [v("ut")], T.ut[:], T.u[:])
+    dma("S", [], [v("xt")], T.xt[:], T.x[:])
+    dma("Y", [], [v("qw")], T.qw[:].bitcast(dt.uint8), T.wc[:])
+    dma("Y", [], [v("sw")], T.sw[:], T.ws[:])
+    dma("Y", [], [v("vt")], T.vt[:], T.v[:])
 
-    iota("pi", T.pi[:, 0:1], [[0, 1]], 0, 1, True)
-    iota("iu", T.iu[:, 0:8], [[16, 8]], 0, 0, True)
-    iota("iof", T.iof[:], [[1, 64]])
-    iota("ioj", T.ioj[:], [[0, 16], [1, 16]])
-    iota("cr", T.cr[:], [[16, 4], [1, 2]])
-    iota("iu2", T.iu[:, 8:20], [[16, 12]], 15, 0, True)
-    iota("kc", T.kc[:], [[16, 16]], 448)
-    fill("yca", T.yc[:, 0:NV], NV, -1)
-    iota("ycb", T.yc[:, NV:12], [[16, NS]], 16 * NV + 15)
-    iota("iob", T.iob[:], [[1, 256]])
-    for b in range(4):
-        fill("tcz%d" % b, T.tc[:, PW * b + C_:PW * b + PW], 16, 0)
-    fill("tb1", T.tb[:, C_:PW], 16, C_)
-    fill("kwz", T.kw[:, C_:PW], 16, 0)
-    fill("srz", T.sr[:, C_:PW], 16, 0)
-    fill("eqt0", T.eqt[:, 0:16], 16, 0)
-    fill("eqt1", T.eqt[:, 32:208], 176, 0)
-    fill("eqs", T.eqs[:, 32:192], 160, 0)
-    fill("stt0", T.stt[:, 0:L_], L_, 0)
-    fill("stt1", T.stt[:, L_:C_], K_, 1)
-    fill("col20", col(20), 1, 16 + IO1 + B16)
-    fill("col21", col(21), 1, 16 + IO1)
-    fill("col23", col(23), 1, 16 + IO2)
-    iota("cw", T.cw[:], [[1, 4], [0, 4]])
-    iota("gx", T.gx[:], [[1, 144]], -B16)
-    fill("gx", T.gx[:, B16 + 15:B16 + 64], 49, 100)
-    iota("gx", T.gx[:, B16 + 64:B16 + 79], [[1, 15]])
-    fill("gx", T.gx[:, B16 + 79:144], 49, 300)
-    iota("thr", T.thr[:, 0:4], [[50, 4]], -51)
-    iota("thr", T.thr[:, 3:7], [[100, 4]], -151)
-    fill("thr", T.thr[:, 3:4], 1, 149)
-    fill("thr", T.thr[:, 4:5], 1, -1)
-    fill("rs", T.rs[:], 8, 1)
-    fill("rs", T.rs[:, 4:5], 1, 0)
-    fill("yd6", T.yd[:, 6:7], 1, 32 * TOP)
-    iota("idr", T.idr[:], [[1, 32]], K_)
-    fill("zr", T.zr[:], 32, 0)
-    iota("olw1", T.olw[:, K_:C_], [[1, 32]], S_)
-    fill("olw2", T.olw[:, C_:PW], 16, -1)
-    fill("tabj", T.tab[:, 32:64], 32, 0)
-    fill("tabk", T.tab[:, 224:B256], 40, 0)
-    iota("tabi", T.tab[:, IO1:TOP], [[0, 2], [1, 200]])
-    fill("tabt", T.tab[:, TOP:688], 8, 0)
-    fill("aa", T.aa[:], 192, 1)
+    iota(col("pi", 0), [[0, 1]], 0, 1)
+    iota(v("iu", 0, 8), [[16, 8]])
+    iota(v("iof"), [[1, 64]])
+    iota(v("cr"), [[16, 4], [1, 2]])
+    iota(v("ioj"), [[0, 16], [1, 16]])
+    iota(v("iu", 8, 20), [[16, 12]], 15)
+    iota(v("iu", 20, 24), [[1, 2], [0, 2]])
+    fill(v("yc", 0, NV), -1)
+    iota(v("yc", NV), [[16, NS]], 16 * NV + 15)
+    ms(v("et"), 1.0)
+    op("G", [v("et")], [v("et")], lambda: g.affine_select(T.et[:], T.et[:], [[-1, 528]], ALU.is_equal, 0.0, 3, 4))
+    iota(v("iob"), [[1, 256]])
+    iota(v("mw"), [[4, 4], [0, 4]])
+    iota(v("kc"), [[16, 16]], C_)
+    for view, c in [(v("eqt", 0, 16), 0), (v("eqt", 32), 0), (v("eqs", 32), 0), (v("nst", 0, L_), 1), (v("nst", L_), 0), (col("nsr", C_), 1),
+                    (v("pls", 0, 16), 0), (v("bt", 0, 384), 0), (v("rk2"), 1), (v("rk2", 0, 2 * KW, KW), 0), (v("ck", 0, 2 * KW, KW), 15),
+                    (v("zi"), 2), (v("zi", 0, ZW, ZS), 0), (v("zi", 2, ZW, ZS), 1), (v("zi", 3, ZW, ZS), -4), (v("zi", 4, ZW, ZS), 1),
+                    (col("zi", ZS - 1), 2 * GAP), (v("zz", 2, ZW, ZS), C_ // 2 + IO), (col("zz", ZS - 2), K_ // 2 + IO),
+                    (v("aa"), 1), (v("zr"), 0), (col("tb", C_), C_), (v("lv", 0, 2), -100), (v("lv", 2, Q2 + 3), 0), (v("lv", Q2 + 3), 48),
+                    (v("tab", 176, IO), 0), (v("cand", 64, 80), 0), (v("tc", C_, 4 * PW, PW), 0), (col("kw", C_), 0), (col("olw", C_), -1)]:
+        fill(view, c)
+    iota(v("idr"), [[1, 32]], K_)
+    iota(v("tab", IO), [[1, TABW - IO]])
+    iota(v("olw", K_, C_), [[1, 32]], S_)
 
-    ms("rm", T.rm[:], 1.0)
-    ms("ones", T.ones[:], 1.0)
-    ms("rm", T.rm[:, 0::16], 0.0)
-    ts("pi", "pj0", T.pi[:, 4:5], T.pi[:, 0:1], 15, ALU.bitwise_and)
-    ts("pi", "pj1", T.pi[:, 5:6], T.pi[:, 0:1], 2, ALU.arith_shift_right, 3, ALU.bitwise_and)
-    ts("pi", "pj2", T.pi[:, 6:7], T.pi[:, 0:1], 3, ALU.bitwise_and)
-    ts("pi", "pj3", T.pi[:, 7:8], T.pi[:, 0:1], 4, ALU.arith_shift_right, 1, ALU.bitwise_and)
-    cp("iu", "offu", T.offu[:], T.iu[:, 0:8])
-    cp("pj0 pj1 pj2 pj3", "ic", T.ic[:, 0:4], T.pi[:, 4:8])
-    for b in range(4):
-        op("G", "ones", "et%d" % b, lambda: g.affine_select(T.et[:, 512 * b:512 * b + 512], T.ones[:], [[-1, 512]], ALU.is_equal, 0.0, b, 4))
-    ms("btz", T.bt[:, 0:384], 0.0)
-    ms("col16", T.cols[:, 16:20:2], 0.5)
-    ts("ioj ic", "dm", T.dm[:], T.ioj[:], I_, ALU.is_equal)
-    ts("cr ic", "dc64", T.dc[:, 0:8], T.cr[:], I_, ALU.add, 1.0 / 64, ALU.mult)
-    ts("cr ic", "dc16", T.dc[:, 8:10], T.cr[:, 0:2], I_, ALU.add, 1.0 / 16, ALU.mult)
-    ts("ioj ic", "gt", T.gt[:], T.ioj[:, 0:192], I_, ALU.is_gt)
-    ts("ioj ic", "bm", T.bm[:], T.ioj[:, 0:192], I_, ALU.is_le, 512.0, ALU.mult)
-    cp("iu2", "bco", T.bco[:], T.iu[:, 8:20])
-    ts("kc ic", "kc", T.kc[:], T.kc[:], I_, ALU.add)
+    ms(v("rs"), 1.0)
+    for k, m in enumerate((15, 12, 3, 16)):
+        ts(col("pi", 4 + k), col("pi", 0), m, ALU.bitwise_and)
+    ms(v("rs", 0, 4 * CW, CW), 0.0)
+    cp(v("ic"), v("pi", 4, 8))
+    cp(offu, v("iu", 0, 8))
+    ts(v("dc", 0, 8), v("cr"), I_, ALU.add, 1.0 / 64, ALU.mult)
+    ts(v("dc", 8, 10), v("cr", 0, 2), I_, ALU.add, 1.0 / 16, ALU.mult)
+    ts(v("dm"), v("ioj"), I_, ALU.is_equal)
+    ts(v("rm"), v("ioj"), 1.0, ALU.min)
+    ts(v("gt"), v("ioj", 0, C_), I_, ALU.is_gt)
+    ts(v("bm"), v("ioj", 0, C_), I_, ALU.is_le, 512.0, ALU.mult)
+    cp(v("cu", 8, 24), v("iu", 8, 24))
+    ts(v("m3", 0, 16), v("ioj", 0, 16), I_, ALU.is_lt)
+    ts(v("m3", 16, 32), v("dm", 0, 16), float(GAP), ALU.mult)
+    cp(v("eqt", 16, 32), v("dm", 0, 16))
+    cp(v("eqs", 0, 16), v("dm", 0, 16))
+    tt(v("wt", 0, 16), v("m3", 16, 32), v("m3", 0, 16), ALU.subtract)
+    ts(v("eqs", 16, 32), v("dm", 0, 16), -1.0, ALU.mult)
+    quant(v("qu"), v("su"), v("ut"))
+    quant(v("qt", 0, C_), v("st", 0, C_), v("xt"))
+    cp(v("qur", cast=dt.uint32), v("qu", cast=dt.uint32, by=offu))
 
-    HALF = 0.4921875
-    act("ic", "dca", T.dc[:, 10:11], I_, AF.Identity, scale=0.75, bias=HALF)
-    act("ic", "dcb", T.dc[:, 11:12], I_, AF.Identity, scale=0.75, bias=HALF + 0.75)
+    HALF, BIG = 0.4921875, 12582912.0
     for h in range(2):
-        act("iof dca dcb", "yyc%d" % h, T.yy[:, 192 * h + 176:192 * h + 192], T.iof[:, 0:16], AF.Identity, scale=12.0, bias=T.dc[:, 10 + h:11 + h])
+        act(col("dc", 10 + h), I_, AF.Identity, 0.75, HALF + 0.75 * h)
     for h in range(2):
-        act("iof dc16", "yya%d" % h, T.yy[:, 192 * h:192 * h + 16], T.iof[:, 0:16], AF.Identity, scale=T.dc[:, 8 + h:9 + h], bias=HALF)
+        act(v("yy", 192 * h, 192 * h + 16), v("iof", 0, 16), AF.Identity, col("dc", 8 + h), HALF)
         for lp in range(4):
             a = 192 * h + 16 + 40 * lp
-            act("iof dc64", "yyb%d%d" % (h, lp), T.yy[:, a:a + 40], T.iof[:, 14:54], AF.Identity, scale=T.dc[:, 2 * lp + h:2 * lp + h + 1], bias=HALF)
+            act(v("yy", a, a + 40), v("iof", Q1, Q1 + 40), AF.Identity, col("dc", 2 * lp + h), HALF)
+        act(v("yy", 192 * h + 176, 192 * h + 192), v("iof", 0, 16), AF.Identity, 12.0, col("dc", 10 + h))
+    act(v("sur"), v("su", by=offu))
+    for bank in ("pp", "pq"):
+        mm(bank, C_, v("qur"), v("sur"), v("qt", 0, C_), v("st", 0, C_))
+    act(v("yr"), v("yy"), AF.Identity, 1.0, BIG)
 
-    def table(lo, hi, rd, parts):
-        for h in range(2):
-            cp(rd, "yi%d%d" % (h, lo), T.yi[:, 192 * h + lo:192 * h + hi], T.yy[:, 192 * h + lo:192 * h + hi])
-        ts("yi0%d" % lo, "y20%d" % lo, T.y2[:, lo:hi], T.yi[:, lo:hi], 257.0, ALU.mult, 256.0, ALU.add)
-        ts("yi1%d" % lo, "y21%d" % lo, T.y2[:, 192 + lo:192 + hi], T.yi[:, 192 + lo:192 + hi], 256.0, ALU.mult)
-        for key, at, a, b in parts:
-            tt("y20%d y21%d" % (lo, lo), key, T.tab[:, at:at + b - a], T.y2[:, a:b], T.y2[:, 192 + a:192 + b], ALU.subtract)
+    def constants_s():
+        for k in range(4):
+            act(v("wt", 16 << k, 32 << k), v("wt", 0, 16 << k))
+        for k, c, b in ((0, I_, 0), (1, I_, 16), (2, I12, 0), (3, I12, 64)):
+            act(col("xs", k), c, AF.Identity, 16.0, b - 0.5)
+        act(col("xs", 4), I3, AF.Identity, 40.0)
+        act(col("zz", ZW - 1), I3, AF.Identity, 40.0, float(K_ // 2 + IO + B64 - Q1))
 
-    table(176, 192, "yyc0 yyc1", [("tab256", B256, 176, 192)])
-    quant("ut", "qu", T.qu[:], T.su[:], T.ut[:])
-    cp("tab256", "qq", T.qq[:], T.tab[:, B256:B256 + 16])
-    cp("qu offu", "qur", T.qur[:].bitcast(dt.uint32), T.qu[:].bitcast(dt.uint32).indirect(T.offu[:]))
-    cp("qu offu", "sur", T.sur[:], T.su[:].indirect(T.offu[:]))
-    quant("xt", "qt", T.qt[:, 0:C_], T.st[:, 0:C_], T.xt[:])
-    mm("qur sur qt", "pp", T.pp[:, 0:C_], T.qur[:], T.sur[:], T.qt[:, 0:C_], T.st[:, 0:C_])
-
-    for k, c, s, b in [(0, 0, 1.0, 0.0), (1, 0, 1.0, -1.0), (2, 1, 4.0, 3.0), (3, 1, 4.0, -1.0), (4, 0, 16.0, 15.0),
-                       (5, 2, 32.0 * 40, 32.0 * (B64 - 14 + 52)), (8, 0, 1.0, 16.0), (22, 2, 40.0, 16.0 + IO2 + B64 - 14)]:
-        act("ic", "col%d" % k, col(k), T.ic[:, c:c + 1], AF.Identity, scale=s, bias=b)
-    act("ic", "yd0", T.yd[:, 0:1], I_, AF.Identity, scale=32.0, bias=32.0 * BNS)
-    act("ic", "yd3", T.yd[:, 3:4], I_, AF.Identity, scale=32.0, bias=32.0 * B256)
-    ts("dm", "wu", T.hh[:, 48:64], T.dm[:, 0:16], -257.0, ALU.mult, 1.0, ALU.add)
-    cp("dm", "eqt", T.eqt[:, 16:32], T.dm[:, 0:16])
-    cp("dm", "eqa", T.eqs[:, 0:16], T.dm[:, 0:16])
-    ts("dm", "eqb", T.eqs[:, 16:32], T.dm[:, 0:16], -1.0, ALU.mult)
-    tt("wu gt", "wt", T.wt[:, 0:16], T.hh[:, 48:64], T.gt[:, 0:16], ALU.subtract)
+    def constants_1():
+        ts(v("yy", 0, 192), v("yr", 0, 192), BIG, ALU.subtract, GAP + 1.0, ALU.mult)
+        ts(v("yy", 192, 384), v("yr", 192, 384), BIG + 1, ALU.subtract, float(GAP), ALU.mult)
 
     def constants_2():
-        for f in range(4):
-            ts("iof col%d" % f, "mk%d" % f, T.mk[:, 16 * f:16 * f + 16], T.iof[:, 0:16], col(f), ALU.is_equal)
-        ts("ones col4", "coff", T.coff[:], T.ones[:, 0:4], col(4), ALU.mult)
-        ts("ic", "col17", T.cols[:, 17:20:2], T.ic[:, 0:2], 1.0, ALU.min, -0.5, ALU.add)
+        tt(v("tab", 0, 176), v("yy", 0, 176), v("yy", 192, 368), ALU.subtract)
+        tt(v("cand", 48, 64), v("yy", 176, 192), v("yy", 368, 384), ALU.subtract)
 
     def constants_3():
-        ts("cw ic", "cw", T.cw[:], T.cw[:], T.ic[:, 1:2], ALU.is_equal, 100.0, ALU.mult)
-        ts("dm", "mm", T.mm[:], T.dm[:, 0:16], 20.0, ALU.mult, -120.0, ALU.add)
-        ts("ic", "col9", col(9), T.ic[:, 3:4], 16.0, ALU.mult, I_, ALU.add)
-        tt("mm cw", "mm", T.mm[:], T.mm[:], T.cw[:], ALU.add)
-        ts("iof col9", "aoff", T.aoff[:], T.iof[:, 0:64:32], col(9), ALU.add)
-        table(0, 176, "yya0 yya1 " + " ".join("yyb%d%d" % (h, lp) for h in range(2) for lp in range(4)),
-              [("tab16", B16, 0, 16), ("tab64", B64, 16, 176)])
-        quant("et0 et1 et2 et3", "qe", T.qe[:], T.se[:], T.et[:])
+        ts(v("qoff"), v("cand", 48, 64), float(C_), ALU.min)
+        cp(v("cand", 80, 96), v("cand", 48, 64))
 
-    def ranks(row, rkey):
-        scan("rm mskb", "scb", T.sc[:, 96:192], T.rm[:, 0:96], T.msk[:, 96:192], 0.0, ALU.mult, ALU.add)
-        scan("rm msk", "sc", T.sc[:, 0:96], T.rm[:, 0:96], T.msk[:, 0:96], 0.0, ALU.mult, ALU.add)
+    def constants_4():
+        ts(v("ck", KW - 1, 2 * KW, KW), v("iof", 0, 32, 16), I_, ALU.add, -15.0, ALU.add)
+        ts(v("zm"), v("zi"), 0.5, ALU.mult)
+        ts(v("mw"), v("mw"), I12, ALU.is_equal, 32.0, ALU.mult)
+        ts(v("aoff"), v("iof", 0, 64, 32), I_, ALU.add, I16, ALU.add)
+        ts(v("kc"), v("kc"), I_, ALU.add)
+        for b in range(4):
+            quant(v("qe", 128 * b, 128 * b + 128), v("se", 128 * b, 128 * b + 128), v("et", 3 - b, 515 - b))
+
+    def ranks(row):
+        for a in (96, 0):
+            scan(v("sc", a, a + 96), v("rm", 0, 96), v("msk", a, a + 96), 0.0, ALU.mult, ALU.add)
 
         def s(c):
-            return T.sc[:, 16 * c + 15:16 * c + 16]
+            return col("sc", 16 * c + 15)
+
+        def part(c, a, b):
+            return v("cmp", CW * c + a, CW * c + b)
 
         def compare(c):
             e = 16 * c + 16
-            ts(rkey + " sc scb", "cma%d" % c, T.cmp[:, 192 * c:192 * c + e], row[:, 0:e], s(c), ALU.is_le)
-            ts(rkey + " sc scb", "cmb%d" % c, T.cmp[:, 192 * c + e:192 * c + 192], row[:, e:192], s(c), ALU.is_lt)
-        for k in range(NS):
-            act(rkey + " scb", "sga%d sgb%d" % (k, k), T.sg[:, PW * k:PW * k + 192], row[:, 0:192], AF.Sign, scale=-1.0, bias=s(NV + k))
-        tt(rkey + " sc scb bco", "eq", T.eq[:], T.sc[:].indirect(T.bco[:]), row[:, 0:192], ALU.is_equal)
+            ts(part(c, 0, e), v(row, 0, e), s(c), ALU.is_le)
+            ts(part(c, e, C_), v(row, e, C_), s(c), ALU.is_lt)
+        for c in range(NV, 12):
+            act(part(c, 0, C_), v(row, 0, C_), AF.Sign, -1.0, s(c))
+        tt(v("eq"), v("sc", by=bco), v(row, 0, C_), ALU.is_equal)
         compare(0)
-        scan("eq gt", "cor", T.cor[:], T.eq[:], T.gt[:], 0.0, ALU.add, ALU.mult)
+        scan(v("cor"), v("eq"), v("gt"), 0.0, ALU.add, ALU.mult)
         compare(1)
-        tt("cor ycb", "sgy", T.sg[:, 192::PW], T.yc[:, NV:12], T.cor[:, 16 * NV + 15::16], ALU.subtract)
-        tt("cor yca", "yv", T.gl[:, 16:16 + NV], T.yc[:, 0:NV], T.cor[:, 15:16 * NV:16], ALU.subtract)
+        tt(v("cmp", C_, 12 * CW, CW), v("yc"), v("cor", 15, C_, 16), ALU.subtract)
         for c in range(2, NV):
             compare(c)
-        for k in range(NS):
-            e = PW * k + 16 * (NV + k) + 16
-            act("sga%d" % k, "sga%d gf%d" % (k, k), T.sg[:, PW * k:e], T.sg[:, PW * k:e], AF.Relu, scale=-1.0, accum_out=T.gl[:, k:k + 1])
-        for k in range(NS):
-            e = PW * k + 16 * (NV + k) + 16
-            act("sgb%d sgy" % k, "sgb%d lb%d" % (k, k), T.sg[:, e:PW * k + 193], T.sg[:, e:PW * k + 193], AF.Relu, accum_out=T.gl[:, 8 + k:9 + k])
-        for c in range(NV):
-            scan("ones yv cma%d cmb%d" % (c, c), "cs%d" % c, T.cs[:, 192 * c:192 * c + 192], T.ones[:, 0:192], T.cmp[:, 192 * c:192 * c + 192],
-                 T.gl[:, 16 + c:17 + c], ALU.mult, ALU.add)
-        cp(" ".join("cs%d" % c for c in range(NV)), "rka", T.rk[:, 0:NV], T.cs[:, 191::192])
-        tt(" ".join("gf%d lb%d" % (k, k) for k in range(NS)), "rkb", T.rk[:, NV:12], T.gl[:, 8:8 + NS], T.gl[:, 0:NS], ALU.subtract)
-        cp("rka rkb", "roff", T.roff[:], T.rk[:, 0:12])
+        for c in range(NV, 12):
+            act(part(c, 0, 16 * c + 16), part(c, 0, 16 * c + 16), AF.Relu, -1.0, acc=col("gl", c - NV))
+        for c in range(NV, 12):
+            act(part(c, 16 * c + 16, CW), part(c, 16 * c + 16, CW), AF.Relu, acc=col("gl", 8 + c - NV))
+        for a, b in ((0, 4), (4, NV)):
+            scan(v("cs", CW * a, CW * b), v("rs", 0, CW * (b - a)), v("cmp", CW * a, CW * b), 0.0, ALU.mult, ALU.add)
+        tt(v("gl", 16, 16 + NS), v("gl", 8, 8 + NS), v("gl", 0, NS), ALU.subtract)
+        cp(v("roff", 0, NV), v("cs", C_, CW * NV, CW))
+        cp(v("roff", NV), v("gl", 16, 16 + NS))
 
-    def rising(rd, a, w):
-        scan(rd + " bm", "m2", T.m2[:, 0:w], T.bm[:, 0:w], a, 0.0, ALU.add, ALU.min)
-        return T.m2[:, 15:w:16]
+    def rising(buf, a, w):
+        scan(v(buf, 0, w), v("bm", 0, w), a, 0.0, ALU.add, ALU.min)
+        return v(buf, 15, w, 16)
 
-    def new_state(more):
-        ts("qq", "qoff", T.qoff[:], T.qq[:], float(C_), ALU.min)
+    def new_state(w, more):
         if more:
-            tt("kc qq", "hh0", T.hh[:, 0:16], T.kc[:], T.qq[:], ALU.subtract)
-        tt("tb tb1 qoff dm", "m1", T.m1[:], T.tb[:].indirect(T.qoff[:]), T.dm[:], ALU.mult)
+            tt(v("hh", 0, 16), v("cand", by=col("vo", 2)), v("kc"), ALU.min)
+        scan(v("m2", 0, w), v("rm", 0, w), v("m1", 0, w), 0.0, ALU.mult, ALU.add)
         if more:
-            tt("hh0 qq", "hh1", T.hh[:, 16:32], T.hh[:, 0:16], T.qq[:], ALU.min)
-        scan("m1 rm", "m2", T.m2[:], T.rm[:], T.m1[:], 0.0, ALU.mult, ALU.add)
+            cp(v("uq"), v("hh", 0, 16))
+        cp(v("to", 0, w // 16), v("m2", 15, w, 16))
         if more:
-            cp("hh1", "uq", T.uq[:], T.hh[:, 16:32])
-        cp("m2", "to", T.to[:], T.m2[:, 15::16])
+            op("V", [v("ax")], [v("ay")], lambda: V.transpose(T.ay[:], T.ax[:]))
         for b in range(4):
-            rd = "to tcz%d tcs%d tca%d" % (b, b, b)
-            w = T.tc[:, PW * b:PW * b + PW].indirect(T.to[:])
-            if b < 2:
-                cp(rd, "ft%d" % b, T.ft[:, b::4], w)
-            else:
-                act(rd, "ft%d" % b, T.ft[:, b::4], w, AF.Copy)
-        quant("ft0 ft1 ft2 ft3", "qf", T.qf[:], T.sf[:], T.ft[:])
+            (cp if b < 2 else act)(v("ft", b, 4 * w, 4), plane("tc", b, min(w, C_ + 1), PW, by=v("to", 0, w // 16)))
+        if more:
+            cp(v("pr", by=v("uq", 0, 2)), v("iob", 0, 32))
+        quant(v("qf", 0, w), v("sf", 0, w), v("ft", 0, 4 * w))
 
-    tt("dm", "msk mskb pp", T.msk[:], T.pp[:, 0:C_], T.dm[:, 0:C_], ALU.mult)
-    act("", "kws kwa pp", T.kw[:, 0:C_], T.pp[:, 0:C_], AF.Copy)
-    ranks(T.kw, "kws kwa")
-    cp("roff iob", "tb", T.tb[:, 0:C_].indirect(T.roff[:]), T.iob[:, 0:C_])
+    def scores_from_psum():
+        for a in (96, 0):
+            tt(v("msk", a, a + 96), v("pp", a, a + 96), v("dm", 0, 96), ALU.mult)
+        act(v("pc"), v("pq", 0, C_))
+
+    scores_from_psum()
+    ranks("pc")
+    cp(v("tb", 0, C_, by=v("roff")), v("iob", 0, C_))
     for b in range(4):
-        act("xt", "tcs%d tca%d" % (b, b), T.tc[:, PW * b:PW * b + C_], T.xt[:, b::4], AF.Copy)
-    for k in range(4):
-        act("wt", "wt", T.wt[:, 16 << k:32 << k], T.wt[:, 0:16 << k], AF.Copy)
-    new_state(True)
+        act(plane("tc", b, C_, PW), v("xt", b, 768, 4))
+    tt(v("m1", 0, C_), v("tb", 0, C_), v("dm", 0, C_), ALU.mult)
+    constants_s()
+    new_state(C_, False)
 
     for t in range(R_):
-        ko, ka, qb, sb = T["ko%d" % t], T["ka%d" % t], T["qb%d" % t], T["sb%d" % t]
+        first, last = t == 0, t == R_ - 1
+        w = C_ if first else S_
+        ko, ka, qb, sb = ["%s%d" % (k, t) for k in ("ko", "ka", "qb", "sb")]
+        held = v("iob", 0, C_) if first else v("pr", 0, C_)
         for b in range(4):
-            mm("qw sw qf", "p%d" % b, PS[b][:, 0:S_], T.qw[:, 128 * b:128 * b + 128], T.sw[:, 128 * b:128 * b + 128], T.qf[:], T.sf[:])
-            act("ft%d" % b, "f6%d" % b, T.f64[:, 256 * b:256 * b + 256], T.ft[:, b::4], AF.Copy, scale=64.0)
-        cp("uq iob", "pr", T.pr[:].indirect(T.uq[:, 0:8]), T.iob[:, 0:128])
+            mm("p%d" % b, w, v("qw", 128 * b, 128 * b + 128), v("sw", 128 * b, 128 * b + 128), v("qf", 0, w), v("sf", 0, w))
+            act(plane("f64", b, w), v("ft", b, 4 * w, 4), scale=64.0)
+        if first:
+            constants_1()
+        else:
+            cp(v("pr", by=v("uq", 2, 10)), v("iob", 32, 160))
         for b in range(4):
-            pl64 = T.t64[:, 256 * b:256 * b + 256]
-            tt("f6%d" % b, "t6%d p%d" % (b, b), pl64, PS[b][:, 0:S_], T.f64[:, 256 * b:256 * b + 256], ALU.add)
+            tt(plane("t64", b, w), v("p%d" % b, 0, w), plane("f64", b, w), ALU.add)
             if b < 2:
-                act("t6%d" % b, "tt%d" % b, T.tt[:, b::4], pl64, AF.Copy, scale=1.0 / 64)
+                act(v("tt", b, 4 * w, 4), plane("t64", b, w), scale=1.0 / 64)
         for b in range(2, 4):
-            ts("t6%d" % b, "tt%d" % b, T.tt[:, b::4], T.t64[:, 256 * b:256 * b + 256], 1.0 / 64, ALU.mult)
-        quant("tt0 tt1 tt2 tt3", "qt", T.qt[:], T.st[:], T.tt[:])
-        mm("qur sur qt", "pp", T.pp[:, 0:S_], T.qur[:], T.sur[:], T.qt[:], T.st[:])
-        act("kws kwa kwz to", "kp", T.kp[:], T.kw[:].indirect(T.to[:]), AF.Copy)
-        act("", "psb pp", T.psb[:], T.pp[:, 0:S_], AF.Copy)
-        cp("uq iob", "pr", T.pr[:].indirect(T.uq[:, 8:16]), T.iob[:, 128:256])
-        cp("m2", "poff", T.poff[:], rising("pr", T.pr[:, 0:C_], C_))
-        tt("psb poff dm", "mskb", T.msk[:, 96:192], T.psb[:].indirect(T.poff[:, 6:12]), T.dm[:, 0:96], ALU.mult)
-        tt("psb poff dm", "msk", T.msk[:, 0:96], T.psb[:].indirect(T.poff[:, 0:6]), T.dm[:, 0:96], ALU.mult)
-        act("psb poff", "pc", T.pc[:], T.psb[:].indirect(T.poff[:]), AF.Copy)
-        ranks(T.pc, "pc")
-        act("stt0 stt1 roff", "sr", T.sr[:, 0:C_], T.stt[:].indirect(T.roff[:]), AF.Copy)
-        tt("eqt eqt0 eqt1 roff pc", "k0", T.k0[:], T.eqt[:, 16:208].indirect(T.roff[:]), T.pc[:], ALU.mult)
-        tt("eqt roff pc", "msk mskb", T.msk[:], T.eqt[:, 0:192].indirect(T.roff[:]), T.pc[:], ALU.mult)
-        act("k0", "k0 koa", T.k0[:], T.k0[:], AF.Identity, accum_out=ko[:, 0:1])
-        op("V", "msk mskb", "kob", lambda: V.tensor_reduce(ko[:, 1:2], T.msk[:], AX.X, ALU.add))
-        order("G", ["koa", "kob"], [])
-        cnt["sent"] += _send(g, T, topo, core, relay_k, ka[:, 0:2], ko[:, 0:2], "aK%d" % t)
-        arrives("ka", "aK%d" % t, len(topo.engines(from_k, core)))
-        arrives("qba", "aB%d" % t, len(topo.engines(from_b, core)) + len(topo.engines(from_s, core)))
-
-        tt("eqs eqa eqb roff pr", "eq", T.eq[:], T.eqs[:].indirect(T.roff[:]), T.pr[:, 0:C_], ALU.mult)
-        act("rka rkb", "hh1", T.hh[:, 16:28], T.rk[:, 0:12], AF.Identity, scale=-float(K_), bias=float(K_ * L_))
-        act("sr srz qoff", "sp", T.jk[:, 0:256], T.sr[:].indirect(T.qoff[:]), AF.Copy)
-        for c in range(2):
-            act("eq", "cma%d cmb%d gll%d" % (c, c, c), T.cmp[:, 192 * c:192 * c + 192], T.eq[:], AF.Relu, scale=1.0 - 2 * c, accum_out=T.gl[:, 5 + c:6 + c])
-        scan("sr ones", "pre", T.pre[:], T.ones[:, 0:C_], T.sr[:, 0:C_], -1.0, ALU.mult, ALU.add)
-        if t == 0:
+            ts(v("tt", b, 4 * w, 4), plane("t64", b, w), 1.0 / 64, ALU.mult)
+        quant(v("qt", 0, w), v("st", 0, w), v("tt", 0, 4 * w))
+        for bank in ("pp", "pq") if first else ("pp",):
+            mm(bank, w, v("qur"), v("sur"), v("qt", 0, w), v("st", 0, w))
+        if first:
+            act(v("kp", 0, C_), v("pc", by=v("to", 0, 12)))
             constants_2()
-        d = rising("pre", T.pre[:], C_)
-        scan("sp ones", "px", T.jk[:, 256:512], T.ones[:, 0:256], T.jk[:, 0:256], 0.0, ALU.mult, ALU.add)
-        tt("m2 hh1", "hh0", T.hh[:, 0:12], d, T.hh[:, 16:28], ALU.max)
-        tt("px coff mk0 mk1 mk2 mk3", "cor", T.cor[:, 0:64], T.jk[:, 256:512].indirect(T.coff[:]), T.mk[:], ALU.mult)
-        cp("gll0 gll1", "plb", T.pl[:, 10:12], T.gl[:, 5:7])
-        for b in range(4):
-            act("plb t6%d" % b, "bt%d" % b, T.bt[:, 384 + b::4], T.t64[:, 256 * b:256 * b + 256].indirect(T.pl[:, 10:12]), AF.Copy, scale=1.0 / 64)
-        scan("cor rm", "cum", T.cor[:, 64:128], T.rm[:, 0:64], T.cor[:, 0:64], 0.0, ALU.mult, ALU.add)
-        cp("hh0", "doff", T.doff[:], T.hh[:, 0:12])
-        tt("cum cor col16 col17", "lim", T.sig[:, 0:4], T.cor[:, 79:128:16], T.cols[:, 16:20], ALU.add)
-        tt("cum cor col20 col21 col22 col23", "bia", T.sig[:, 8:12], T.cor[:, 79:128:16], T.cols[:, 20:24], ALU.add)
-        tt("cum cor thr", "thr1", T.thr[:, 1:2], T.cor[:, 79:80], T.cor[:, 95:96], ALU.subtract)
-        quant("btz bt0 bt1 bt2 bt3", "qbo", qb[:, 32:160], sb[:, 128:256], T.bt[:])
-        order("G", ["qbo"], [])
-        cnt["sent"] += _send_b(g, T, topo, core, relay_b, relay_s, qb[:, 128:160].bitcast(dt.uint8), sb[:, 128:256], t)
-        if t:
-            fill("aa", T.aa[:], 192, 1)
-        cp("doff pr", "pls", T.pls[:].indirect(T.doff[:]), T.pr[:, 0:C_])
-        for f in range(4):
-            act("iob lim", "tbs%d" % f, T.tbs[:, 176 * f:176 * f + 176], T.iob[:, 0:176], AF.Sign, scale=-1.0, bias=T.sig[:, f:f + 1])
-        cp("m2", "pl", T.pl[:, 0:10], rising("pls", T.pls[:, 0:K_], K_))
-        act("kp pl", "kws", T.kw[:, 0:K_], T.kp[:].indirect(T.pl[:, 0:10]), AF.Copy)
-        tt("sr srz qoff wt", "m1", T.m1[:], T.sr[:].indirect(T.qoff[:]), T.wt[:], ALU.mult)
-        scan("m1 rm", "m2", T.m2[:], T.rm[:], T.m1[:], 0.0, ALU.mult, ALU.add)
-        ts("m2", "tabn", T.tab[:, BNS:BNS + 16], T.m2[:, 15::16], 256.0, ALU.add)
-        if t == 0:
+            scores_from_psum()
+        else:
+            act(v("kw", K_, C_), v("ay", by=v("aoff")))
+            act(v("kp"), v("kw", 0, C_ + 1, by=v("to")))
+            act(v("psb"), v("pp", 0, S_))
+            cp(v("pr", by=v("uq", 10, 16)), v("iob", 160, 256))
+            cp(v("poff"), rising("m5", held, C_))
+            for a in (6, 0):
+                tt(v("msk", 16 * a, 16 * a + 96), v("psb", by=v("poff", a, a + 6)), v("dm", 0, 96), ALU.mult)
+            act(v("pc"), v("psb", by=v("poff")))
+        ranks("pc")
+        act(v("nsr", 0, C_), v("nst", by=v("roff")))
+        tt(v("k0"), v("eqt", 16, 208, by=v("roff")), v("pc"), ALU.mult)
+        tt(v("k1"), v("eqt", 0, 192, by=v("roff")), v("pc"), ALU.mult)
+        act(v("k0"), v("k0"), AF.Identity, acc=col(ko, 0))
+        tt(v("eq"), v("eqs", by=v("roff")), held, ALU.mult)
+        act(v("k1"), v("k1"), AF.Identity, acc=col(ko, 1))
+        order("G", touches([v(ko, 0, 2)], []))
+        cnt["sent"] += _send(g, T, topo, core, relay_k, T[ka][:, 0:2], T[ko][:, 0:2], "aK%d" % t)
+        arrives([v(ka, 0, 2)], "aK%d" % t, len(topo.engines(from_k, core)))
+        arrives([v(qb, 0, 32), v(sb, 96, 128)], "aB%d" % t, len(topo.engines(from_b, core)) + len(topo.engines(from_s, core)))
+
+        scan(v("pre"), ones, v("nsr", 0, C_), 15.0, ALU.add, ALU.subtract)
+        ts(v("hh", 16, 28), v("roff"), -float(K_ + 16), ALU.mult, float((K_ + 16) * L_), ALU.add)
+        for c in range(2):
+            act(plane("jk", c, C_, C_), v("eq"), AF.Relu, 1.0 - 2 * c, acc=col("gl", 22 + c))
+        d = rising("m5", v("pre"), C_)
+        if first:
             constants_3()
-        if t == R_ - 1:
-            quant("vt", "qv", T.qv[:], T.sv[:], T.vt[:])
+        tt(v("hh", 0, 12), d, v("hh", 16, 28), ALU.max)
+        cp(v("pl", 10, 12), v("gl", 22, 24))
+        cp(v("doff"), v("hh", 0, 12))
+        for b in range(4):
+            act(v("bt", 384 + b, 512, 4), plane("t64", b, w, by=v("pl", 10, 12)), scale=1.0 / 64)
+        cp(v("pls", by=v("doff")), held)
+        quant(v(qb, 32, 160), v(sb, 128, 256), v("bt"))
+        order("G", touches([v(qb, 128, 160), v(sb, 128, 256)], []))
+        cnt["sent"] += _send_b(g, T, topo, core, relay_b, relay_s, T[qb][:, 128:160].bitcast(dt.uint8), T[sb][:, 128:256], t)
+        if t:
+            fill(v("aa"), 1)
+        stay = v("pls", 16, 16 + K_)
+        d = rising("m5", stay, K_)
+        tt(v("m3"), v("nsr", 0, C_ + 1, by=v("qoff")), v("wt"), ALU.mult)
+        cp(v("pl", 0, 10), d)
+        unit = S_ / w
+        at = (0, 3, ZS, ZS + 3)
+
+        def count(f):
+            act(plane("jk", f, K_, C_), stay, AF.Sign, -unit, col("xs", f), acc=col("zz", at[f]))
+        count(0)
+        count(1)
+        act(v("kw", 0, K_), v("kp", 0, w, by=v("pl", 0, 10)))
+        count(2)
+        count(3)
+        scan(v("m4"), v("rm"), v("m3"), 0.0, ALU.mult, ALU.add)
+        ts(col("sm", 0), col("zz", 3), col("zz", 0), ALU.subtract, 0.5, ALU.mult)
+        ts(v("tn"), v("m4", 15, S_, 16), I_, ALU.add)
+        ts(col("zz", ZS - 1), col("sm", 0), float(Q1), ALU.max, -float(GAP), ALU.mult)
+        if first:
+            constants_4()
+        if last:
+            quant(v("qv"), v("sv"), v("vt"))
 
         def stayers(b):
-            act("pl t6%d" % b, "tcs%d" % b, T.tc[:, PW * b:PW * b + K_], T.t64[:, 256 * b:256 * b + 256].indirect(T.pl[:, 0:10]), AF.Copy, scale=1.0 / 64)
+            act(plane("tc", b, K_, PW), plane("t64", b, w, by=v("pl", 0, 10)), scale=1.0 / 64)
         stayers(0)
 
         for c in range(2):
-            ts("kws ka", "ck%d" % c, T.ck[:, 160 * c:160 * c + 160], T.kw[:, 0:K_], ka[:, c:c + 1], ALU.is_le)
-        for c in range(2):
-            scan("ones ck%d" % c, "cn%d" % c, T.cn[:, 160 * c:160 * c + 160], T.ones[:, 0:K_], T.ck[:, 160 * c:160 * c + 160], 0.0, ALU.mult, ALU.add)
-        ts("cn0 ic", "qoa", T.qo[:, 0:1], T.cn[:, 159:160], I_, ALU.add)
-        cp("cn0 cn1", "noff", T.noff[:], T.cn[:, 159::160])
-        for f, key, o in [(2, "hi1", T.sig[:, 5:6]), (3, "yd5", T.yd[:, 5:6]), (0, "hi0", T.sig[:, 4:5]), (1, "yd4", T.yd[:, 4:5])]:
-            act("noff tbs0 tbs1 tbs2 tbs3 bia", "ju%d %s" % (f, key), T.ju[:, 32 * f:32 * f + 32], T.tbs[:, 176 * f:176 * f + 176].indirect(T.noff[:]),
-                AF.Identity, scale=16.0, bias=T.sig[:, 8 + f:9 + f], accum_out=o)
-        if t < R_ - 1:
-            for c in range(2):
-                act("ones ka", "ax%d" % c, T.ax[:, 32 * c:32 * c + 32], T.ones[:, 0:32], AF.Copy, scale=ka[:, c:c + 1])
-        for b in range(1, 4):
+            ts(v("ck", KW * c + 1, KW * c + 1 + K_), v("kw", 0, K_), col(ka, c), ALU.is_le)
+        scan(v("cn"), v("rk2"), v("ck"), 0.0, ALU.mult, ALU.add)
+        cp(v("noff"), v("cn", K_, 2 * KW, KW))
+        cp(v("qo"), v("cn", K_ + 1, 2 * KW, KW))
+        before = v("pls", 0, 16 + K_, by=v("noff"))
+        for f in (0, 2):
+            act(v("ju", 16 * f, 16 * f + 32), before, AF.Sign, -unit, col("xs", f), acc=col("zz", at[f] + 1))
+            ts(v("zz", at[f + 1] + 1, at[f + 1] + 1 + L_), before, unit, ALU.mult, col("xs", f + 1), ALU.is_lt)
+        stayers(1)
+        cp(v("aa", by=v("qo")), v("zr"))
+        scan(v("zo"), v("zm"), v("zz"), 0.0, ALU.mult, ALU.add)
+        scan(v("tb", 0, C_), ones, v("aa"), -1.0, ALU.mult, ALU.add)
+        ts(col("vo", 0), col("zo", ZS - 1), col("zo", ZW - 1), ALU.min, col("xs", 4), ALU.subtract)
+        cp(v("xo", 0, 2), v("zo", 2, ZW, ZS))
+        cp(v("xo", 2, 4), v("zo", ZS - 2, ZW, ZS))
+        tt(v("sm", 16, 32), v("lv", by=col("vo", 0)), v("mw"), ALU.add)
+        act(v("gq"), v("tab", by=v("xo")))
+        for b in (2, 3):
             stayers(b)
-        if t == R_ - 1:
-            act("pls", "olw0", T.olw[:, 0:K_], T.pls[:, 0:K_], AF.Copy)
         for b in range(4):
-            mm("qe qba qbo", "p%d" % b, PS[b][:, 0:128], T.qe[:, 128 * b:128 * b + 128], T.se[:, 128 * b:128 * b + 128], qb[:, 0:128], sb[:, 96:224])
+            mm("p%d" % b, 128, v("qe", 128 * b, 128 * b + 128), v("se", 128 * b, 128 * b + 128), v(qb, 0, 128), v(sb, 96, 224))
         for b in range(4):
-            act("", "tca%d p%d" % (b, b), T.tc[:, PW * b + K_:PW * b + C_], PS[b][:, 0:32], AF.Copy)
-        ts("cn1 col8", "qob", T.qo[:, 1:2], T.cn[:, 319:320], col(8), ALU.add)
-        cp("qoa qob zr", "aa", T.aa[:].indirect(T.qo[:]), T.zr[:])
-        scan("aa ones", "tb", T.tb[:, 0:C_], T.ones[:, 0:C_], T.aa[:], -1.0, ALU.mult, ALU.add)
-        tt("hi0 hi1 yd4 yd5", "yd1", T.yd[:, 1:3], T.sig[:, 4:6], T.yd[:, 4:6], ALU.subtract)
-        ts("yd1 col5", "sm0", T.sm[:, 0:1], T.yd[:, 2:3], col(5), ALU.is_gt, 32.0 * 64, ALU.mult)
-        ts("yd1 sm0", "voff", T.voff[:, 0:1], T.yd[:, 1:2], T.sm[:, 0:1], ALU.add, 1.0 / 32, ALU.mult)
-        cp("qoa qob idr", "tb", T.tb[:, 0:C_].indirect(T.qo[:]), T.idr[:])
-        tt("gx voff mm", "sm1", T.sm[:, 16:32], T.gx[:].indirect(T.voff[:, 0:1]), T.mm[:], ALU.add)
-        op("V", "sm1", "sm2", lambda: V.tensor_reduce(T.sm[:, 1:2], T.sm[:, 16:32], AX.X, ALU.max))
-        if t < R_ - 1:
-            op("V", "ax0 ax1", "ay", lambda: V.transpose(T.ay[:], T.ax[:]))
-        ts("sm2 thr thr1", "sm3", T.sm[:, 32:39], T.thr[:, 0:7], T.sm[:, 1:2], ALU.is_lt)
-        tt("sm3 yd0 yd1 yd3 yd4 yd5 yd6", "sm4", T.sm[:, 40:47], T.sm[:, 32:39], T.yd[:, 0:7], ALU.mult)
-        scan("sm4 rs", "sm5", T.sm[:, 48:55], T.rs[:, 0:7], T.sm[:, 40:47], 0.0, ALU.mult, ALU.max)
-        ts("sm5", "xo", T.xo[:], T.sm[:, 51:55:3], 1.0 / 32, ALU.mult)
-        cp("xo tabj tabk tabi tabt tabn tab16 tab64 tab256", "gq", T.gq[:], T.tab[:].indirect(T.xo[:]))
-        tt("gq", "qq", T.qq[:], T.gq[:, 0:16], T.gq[:, 16:32], ALU.add)
-        if t < R_ - 1:
-            act("ay aoff", "kwa", T.kw[:, K_:C_], T.ay[:].indirect(T.aoff[:]), AF.Copy)
-        new_state(t < R_ - 1)
+            act(plane("tc", b, L_, PW, K_), v("p%d" % b, 0, L_))
+        if last:
+            act(v("olw", 0, K_), stay)
+        else:
+            act(v("ax"), v(ka, 0, 2, by=axo))
+        ts(col("sm", 1), col("zo", ZS - 2), col("sm", 0), ALU.is_gt, 16.0, ALU.mult)
+        reduce(col("sm", 2), v("sm", 16, 32), ALU.max)
+        cp(v("tb", 0, C_, by=v("qo")), v("idr"))
+        ts(col("vo", 2), col("sm", 2), col("sm", 1), ALU.max, I_, ALU.add)
+        tt(v("cand", 16, 48), v("gq", 0, 32), v("gq", 32, 64), ALU.add)
+        tt(v("cand", 0, 16), v("gq", 0, 16), v("tn"), ALU.add)
+        ts(v("qoff"), v("cand", by=col("vo", 2)), float(C_), ALU.min)
+        tt(v("m1"), v("tb", 0, C_ + 1, by=v("qoff")), v("dm"), ALU.mult)
+        new_state(S_, not last)
 
-    mm("qv qf", "py", T.py[:, 0:S_], T.qv[:], T.sv[:], T.qf[:], T.sf[:])
-    act("olw0 olw1 olw2 to", "olr", T.olr[:], T.olw[:].indirect(T.to[:]), AF.Copy)
-    dma("Y", "qf", "", T.oc[:], T.qf[:].bitcast(dt.uint8))
-    act("", "ys py", T.ys[:], T.py[:, 0:S_], AF.Copy)
-    dma("S", "ys", "", T.y[:], T.ys[:])
+    mm("pp", S_, v("qv"), v("sv"), v("qf"), v("sf"))
+    act(v("olr"), v("olw", 0, C_ + 1, by=v("to")))
+    dma("Y", [v("qf")], [], T.oc[:], T.qf[:].bitcast(dt.uint8))
+    cp(v("ys"), v("pp", 0, S_))
+    dma("S", [v("olr")], [], T.ol[:], T.olr[0:128:16, :])
+    dma("S", [v("ys")], [], T.y[:], T.ys[:])
     for k in range(4):
-        dma("Y", "qf", "", T.osc[4 * k:4 * k + 4, :], T.sf[32 * k:32 * k + 4, :])
-    dma("S", "olr", "", T.ol[:], T.olr[0:128:16, :])
-    for s, v in cnt.items():
-        if v:
-            g.wait_ge(T.sem[s], v)
+        dma("Y", [v("sf")], [], T.osc[4 * k:4 * k + 4, :], T.sf[32 * k:32 * k + 4, :])
+    for s, k in cnt.items():
+        if k:
+            g.wait_ge(T.sem[s], k)

@@ -8,12 +8,15 @@ K_ = C_ - L_
 NV = 7
 NS = 12 - NV
 CW = C_ + 1
-PW = 208
+ST = 64
+PW = ST + K_
+MW = 208
+PR1 = 12
 GAP = 512
 B64, IO, TABW = 16, 224, 424
 ZS = L_ + 6
 ZW = 2 * ZS - 1
-KW = K_ + 2
+KW = C_ + 2
 CX, U8, BF, F32, I32, U16 = "float8_e4m3fn_x4", "uint8", "bfloat16", "float32", "int32", "uint16"
 
 
@@ -30,18 +33,18 @@ SCRATCH = {
     "pi": _sb(8, I32), "ic": _sb(4, F32), "iu": _sb(24, I32), "cu": _sb(24, U16), "aoff": _sb(2, U16),
     "ioj": _sb(256, BF), "iob": _sb(256, BF), "iof": _sb(64, F32), "cr": _sb(8, F32), "dc": _sb(16, F32),
     "dm": _sb(256, BF), "rm": _sb(256, BF), "gt": _sb(192, BF), "bm": _sb(192, BF), "wt": _sb(256, BF), "rs": _sb(4 * CW, BF), "rk2": _sb(2 * KW, BF),
-    "eqt": _sb(208, BF), "eqs": _sb(192, BF), "nst": _sb(192, BF), "yc": _sb(12, F32), "kc": _sb(16, F32), "idr": _sb(32, BF), "zr": _sb(32, BF),
+    "eqt": _sb(208, BF), "eqs": _sb(192, BF), "nst": _sb(192, BF), "yc": _sb(12, F32), "kc": _sb(16, F32), "zr": _sb(32, BF),
     "lv": _sb(112, BF), "mw": _sb(16, F32), "tab": _sb(TABW, F32), "yy": _sb(384, F32), "yr": _sb(384, F32), "xs": _sb(8, F32),
     "zi": _sb(ZW, F32), "zm": _sb(ZW, F32), "zz": _sb(ZW, F32), "zo": _sb(ZW, F32),
     "psb": _sb(256, F32), "pc": _sb(192, F32), "msk": _sb(192, F32), "sc": _sb(192, F32), "eq": _sb(192, BF), "cor": _sb(192, BF),
     "cmp": _sb(CW * 12, BF), "cs": _sb(CW * NV, BF), "gl": _sb(24, F32), "roff": _sb(12, U16), "k0": _sb(192, F32), "k1": _sb(192, F32),
-    "nsr": _sb(PW, BF), "pre": _sb(192, BF), "hh": _sb(32, F32), "doff": _sb(12, U16), "jk": _sb(4 * 192, BF),
-    "pr": _sb(C_ + S_, BF), "pls": _sb((K_ + 16) * L_ + 16, BF), "m1": _sb(256, BF), "m2": _sb(256, BF), "m3": _sb(256, BF), "m4": _sb(256, BF),
-    "m5": _sb(192, BF), "pl": _sb(12, U16), "poff": _sb(12, U16),
-    "kw": _sb(PW, F32), "kp": _sb(256, F32), "ck": _sb(2 * KW, BF), "cn": _sb(2 * KW, BF), "noff": _sb(2, U16), "qo": _sb(2, U16),
-    "aa": _sb(192, BF), "tb": _sb(PW, BF), "ju": _sb(64, BF), "sm": _sb(32, F32), "tn": _sb(16, F32),
-    "xo": _sb(4, U16), "vo": _sb(4, U16), "gq": _sb(64, F32), "cand": _sb(96, F32), "qoff": _sb(16, U16), "to": _sb(16, U16),
-    "uq": _sb(16, U16), "ax": _sb(64, F32), "ay": _sb(64, F32), "olw": _sb(PW, F32), "olr": _sb(256, F32), "ys": _sb(256, F32),
+    "nsr": _sb(MW, BF), "pre": _sb(192, BF), "hh": _sb(32, F32), "doff": _sb(12, U16), "jk": _sb(4 * 192, BF),
+    "pr": _sb(C_ + S_, BF), "pls": _sb((K_ + 16) * L_ + 16, BF), "m3": _sb(256, BF), "m4": _sb(256, BF),
+    "m5": _sb(192, BF), "m6": _sb(160, BF), "pl": _sb(12, U16), "poff": _sb(12, U16), "mq": _sb(4 * MW, BF), "nb": _sb(192, BF), "ndm": _sb(192, BF),
+    "kw": _sb(PW, F32), "ks": _sb(MW, F32), "km": _sb(192, F32), "kp": _sb(256, F32), "ck": _sb(2 * KW, BF), "cn": _sb(2 * KW, BF), "noff": _sb(2, U16), "qo": _sb(2, U16),
+    "aa": _sb(192, BF), "tb": _sb(192, BF), "idv": _sb(32, BF), "ju": _sb(64, BF), "sm": _sb(32, F32), "tn": _sb(16, F32),
+    "xo": _sb(4, U16), "vo": _sb(4, U16), "gq": _sb(64, F32), "cand": _sb(96, F32), "qoff": _sb(16, U16), "to": _sb(12, U16),
+    "uq": _sb(16, U16), "ax": _sb(64, F32), "ay": _sb(64, F32), "olw": _sb(PW, F32),
 }
 for _t in ["p0", "p1", "p2", "p3", "pp", "pq"]:
     SCRATCH[_t] = ("psum", [128, 512], F32)
@@ -255,12 +258,11 @@ def rank_program(g, core, T, topo):
                     (v("pls", 0, 16), 0), (v("bt", 0, 384), 0), (v("rk2"), 1), (v("rk2", 0, 2 * KW, KW), 0), (v("ck", 0, 2 * KW, KW), 15),
                     (v("zi"), 2), (v("zi", 0, ZW, ZS), 0), (v("zi", 2, ZW, ZS), 1), (v("zi", 3, ZW, ZS), -4), (v("zi", 4, ZW, ZS), 1),
                     (col("zi", ZS - 1), 2 * GAP), (v("zz", 2, ZW, ZS), C_ // 2 + IO), (col("zz", ZS - 2), K_ // 2 + IO),
-                    (v("aa"), 1), (v("zr"), 0), (col("tb", C_), C_), (v("lv", 0, 2), -100), (v("lv", 2, Q2 + 3), 0), (v("lv", Q2 + 3), 48),
-                    (v("tab", 176, IO), 0), (v("cand", 64, 80), 0), (v("tc", C_, 4 * PW, PW), 0), (col("kw", C_), 0), (col("olw", C_), -1)]:
+                    (v("aa"), 1), (v("zr"), 0), (v("lv", 0, 2), -100), (v("lv", 2, Q2 + 3), 0), (v("lv", Q2 + 3), 48),
+                    (v("tab", 176, IO), 0), (v("cand", 64, 80), 0), (v("mq", C_, 4 * MW, MW), 0), (col("ks", C_), -1), (v("kw", L_, ST), 0)]:
         fill(view, c)
-    iota(v("idr"), [[1, 32]], K_)
     iota(v("tab", IO), [[1, TABW - IO]])
-    iota(v("olw", K_, C_), [[1, 32]], S_)
+    iota(v("olw", 0, ST), [[1, ST]], S_)
 
     ms(v("rs"), 1.0)
     for k, m in enumerate((15, 12, 3, 16)):
@@ -317,9 +319,11 @@ def rank_program(g, core, T, topo):
 
     def constants_3():
         ts(v("qoff"), v("cand", 48, 64), float(C_), ALU.min)
-        cp(v("cand", 80, 96), v("cand", 48, 64))
+        ts(v("nb"), v("nst"), 1e29, ALU.mult)
 
     def constants_4():
+        cp(v("cand", 80, 96), v("cand", 48, 64))
+        ts(v("ndm"), v("ioj", 0, C_), I_, ALU.not_equal, 255.0, ALU.mult)
         ts(v("ck", KW - 1, 2 * KW, KW), v("iof", 0, 32, 16), I_, ALU.add, -15.0, ALU.add)
         ts(v("zm"), v("zi"), 0.5, ALU.mult)
         ts(v("mw"), v("mw"), I12, ALU.is_equal, 32.0, ALU.mult)
@@ -328,7 +332,7 @@ def rank_program(g, core, T, topo):
         for b in range(4):
             quant(v("qe", 128 * b, 128 * b + 128), v("se", 128 * b, 128 * b + 128), v("et", 3 - b, 515 - b))
 
-    def ranks(row):
+    def ranks(row, in_psum):
         for a in (96, 0):
             scan(v("sc", a, a + 96), v("rm", 0, 96), v("msk", a, a + 96), 0.0, ALU.mult, ALU.add)
 
@@ -344,12 +348,18 @@ def rank_program(g, core, T, topo):
             ts(part(c, e, C_), v(row, e, C_), s(c), ALU.is_lt)
         for c in range(NV, 12):
             act(part(c, 0, C_), v(row, 0, C_), AF.Sign, -1.0, s(c))
-        tt(v("eq"), v("sc", by=bco), v(row, 0, C_), ALU.is_equal)
+        compare(NV - 1)
+        if in_psum:
+            tt(v("eq"), v("sc"), v("pp", 0, C_), ALU.is_equal)
+        else:
+            tt(v("eq"), v("sc", by=bco), v(row, 0, C_), ALU.is_equal)
         compare(0)
-        scan(v("cor"), v("eq"), v("gt"), 0.0, ALU.add, ALU.mult)
         compare(1)
+        scan(v("cor"), v("eq"), v("gt"), 0.0, ALU.add, ALU.mult)
+        compare(2)
+        compare(3)
         tt(v("cmp", C_, 12 * CW, CW), v("yc"), v("cor", 15, C_, 16), ALU.subtract)
-        for c in range(2, NV):
+        for c in range(4, NV - 1):
             compare(c)
         for c in range(NV, 12):
             act(part(c, 0, 16 * c + 16), part(c, 0, 16 * c + 16), AF.Relu, -1.0, acc=col("gl", c - NV))
@@ -365,34 +375,23 @@ def rank_program(g, core, T, topo):
         scan(v(buf, 0, w), v("bm", 0, w), a, 0.0, ALU.add, ALU.min)
         return v(buf, 15, w, 16)
 
-    def new_state(w, more):
-        if more:
-            tt(v("hh", 0, 16), v("cand", by=col("vo", 2)), v("kc"), ALU.min)
-        scan(v("m2", 0, w), v("rm", 0, w), v("m1", 0, w), 0.0, ALU.mult, ALU.add)
-        if more:
-            cp(v("uq"), v("hh", 0, 16))
-        cp(v("to", 0, w // 16), v("m2", 15, w, 16))
-        if more:
-            op("V", [v("ax")], [v("ay")], lambda: V.transpose(T.ay[:], T.ax[:]))
-        for b in range(4):
-            (cp if b < 2 else act)(v("ft", b, 4 * w, 4), plane("tc", b, min(w, C_ + 1), PW, by=v("to", 0, w // 16)))
-        if more:
-            cp(v("pr", by=v("uq", 0, 2)), v("iob", 0, 32))
-        quant(v("qf", 0, w), v("sf", 0, w), v("ft", 0, 4 * w))
-
     def scores_from_psum():
         for a in (96, 0):
             tt(v("msk", a, a + 96), v("pp", a, a + 96), v("dm", 0, 96), ALU.mult)
         act(v("pc"), v("pq", 0, C_))
 
     scores_from_psum()
-    ranks("pc")
+    ranks("pc", True)
     cp(v("tb", 0, C_, by=v("roff")), v("iob", 0, C_))
     for b in range(4):
         act(plane("tc", b, C_, PW), v("xt", b, 768, 4))
-    tt(v("m1", 0, C_), v("tb", 0, C_), v("dm", 0, C_), ALU.mult)
+    tt(v("eq"), v("tb"), v("dm", 0, C_), ALU.mult)
     constants_s()
-    new_state(C_, False)
+    scan(v("m5"), v("rm", 0, C_), v("eq"), 0.0, ALU.mult, ALU.add)
+    cp(v("to"), v("m5", 15, C_, 16))
+    for b in range(4):
+        (cp if b < 2 else act)(v("ft", b, 4 * C_, 4), plane("tc", b, C_, PW, by=v("to")))
+    quant(v("qf", 0, C_), v("sf", 0, C_), v("ft", 0, 4 * C_))
 
     for t in range(R_):
         first, last = t == 0, t == R_ - 1
@@ -405,30 +404,39 @@ def rank_program(g, core, T, topo):
         if first:
             constants_1()
         else:
-            cp(v("pr", by=v("uq", 2, 10)), v("iob", 32, 160))
+            cp(v("pr", by=v("uq", 0, PR1)), v("iob", 0, 16 * PR1))
+            act(v("ax"), v("ka%d" % (t - 1), 0, 2, by=axo))
         for b in range(4):
             tt(plane("t64", b, w), v("p%d" % b, 0, w), plane("f64", b, w), ALU.add)
             if b < 2:
                 act(v("tt", b, 4 * w, 4), plane("t64", b, w), scale=1.0 / 64)
+        if not first:
+            act(v("kw", ST), v("ks" if t == 1 else "kp", 0, C_ if t == 1 else S_, by=v("pl", 0, 10)))
+            op("V", [v("ax")], [v("ay")], lambda: V.transpose(T.ay[:], T.ax[:]))
         for b in range(2, 4):
             ts(v("tt", b, 4 * w, 4), plane("t64", b, w), 1.0 / 64, ALU.mult)
-        quant(v("qt", 0, w), v("st", 0, w), v("tt", 0, 4 * w))
-        for bank in ("pp", "pq") if first else ("pp",):
-            mm(bank, w, v("qur"), v("sur"), v("qt", 0, w), v("st", 0, w))
         if first:
-            act(v("kp", 0, C_), v("pc", by=v("to", 0, 12)))
+            quant(v("qt", 0, w), v("st", 0, w), v("tt", 0, 4 * w))
+            for bank in ("pp", "pq"):
+                mm(bank, w, v("qur"), v("sur"), v("qt", 0, w), v("st", 0, w))
+            act(v("ks", 0, C_), v("pc", by=v("to")))
             constants_2()
             scores_from_psum()
         else:
-            act(v("kw", K_, C_), v("ay", by=v("aoff")))
-            act(v("kp"), v("kw", 0, C_ + 1, by=v("to")))
-            act(v("psb"), v("pp", 0, S_))
-            cp(v("pr", by=v("uq", 10, 16)), v("iob", 160, 256))
-            cp(v("poff"), rising("m5", held, C_))
+            for h, bank in enumerate(("pp", "pq")):
+                quant(v("qt", 128 * h, 128 * h + 128), v("st", 128 * h, 128 * h + 128), v("tt", 512 * h, 512 * h + 512))
+                mm(bank, 128, v("qur"), v("sur"), v("qt", 128 * h, 128 * h + 128), v("st", 128 * h, 128 * h + 128))
+            act(v("kw", 0, L_), v("ay", by=v("aoff")))
+            act(v("ks", 0, C_), v("kw", by=v("to")))
+            act(v("psb", 0, 128), v("pp", 0, 128))
+            cp(v("pr", by=v("uq", PR1, 16)), v("iob", 16 * PR1, 256))
+            d = rising("m5", held, C_)
+            cp(v("psb", 128, 256), v("pq", 0, 128))
+            cp(v("poff"), d)
             for a in (6, 0):
                 tt(v("msk", 16 * a, 16 * a + 96), v("psb", by=v("poff", a, a + 6)), v("dm", 0, 96), ALU.mult)
             act(v("pc"), v("psb", by=v("poff")))
-        ranks("pc")
+        ranks("pc", first)
         act(v("nsr", 0, C_), v("nst", by=v("roff")))
         tt(v("k0"), v("eqt", 16, 208, by=v("roff")), v("pc"), ALU.mult)
         tt(v("k1"), v("eqt", 0, 192, by=v("roff")), v("pc"), ALU.mult)
@@ -441,96 +449,116 @@ def rank_program(g, core, T, topo):
         arrives([v(qb, 0, 32), v(sb, 96, 128)], "aB%d" % t, len(topo.engines(from_b, core)) + len(topo.engines(from_s, core)))
 
         scan(v("pre"), ones, v("nsr", 0, C_), 15.0, ALU.add, ALU.subtract)
+        for c, o in enumerate((ALU.max, ALU.min)):
+            scan(plane("jk", c, C_, C_), v("eq"), v("eq"), 0.0, o, o)
+        d = rising("m5", v("pre"), C_)
         ts(v("hh", 16, 28), v("roff"), -float(K_ + 16), ALU.mult, float((K_ + 16) * L_), ALU.add)
         for c in range(2):
-            act(plane("jk", c, C_, C_), v("eq"), AF.Relu, 1.0 - 2 * c, acc=col("gl", 22 + c))
-        d = rising("m5", v("pre"), C_)
+            ts(col("pl", 10 + c), col("jk", C_ * c + C_ - 1), 1.0 - 2 * c, ALU.mult)
+        if not first and not last:
+            act(v("kp"), v("ks", 0, C_ + 1, by=v("qoff")))
+        tt(v("hh", 0, 12), d, v("hh", 16, 28), ALU.max)
         if first:
             constants_3()
-        tt(v("hh", 0, 12), d, v("hh", 16, 28), ALU.max)
-        cp(v("pl", 10, 12), v("gl", 22, 24))
-        cp(v("doff"), v("hh", 0, 12))
         for b in range(4):
-            act(v("bt", 384 + b, 512, 4), plane("t64", b, w, by=v("pl", 10, 12)), scale=1.0 / 64)
-        cp(v("pls", by=v("doff")), held)
+            if b < 2:
+                ts(v("bt", 384 + b, 512, 4), plane("t64", b, w, by=v("pl", 10, 12)), 1.0 / 64, ALU.mult)
+            else:
+                act(v("bt", 384 + b, 512, 4), plane("t64", b, w, by=v("pl", 10, 12)), scale=1.0 / 64)
+        cp(v("doff"), v("hh", 0, 12))
         quant(v(qb, 32, 160), v(sb, 128, 256), v("bt"))
         order("G", touches([v(qb, 128, 160), v(sb, 128, 256)], []))
         cnt["sent"] += _send_b(g, T, topo, core, relay_b, relay_s, T[qb][:, 128:160].bitcast(dt.uint8), T[sb][:, 128:256], t)
         if t:
             fill(v("aa"), 1)
+        cp(v("pls", by=v("doff")), held)
+        tt(v("km"), v("nb", by=v("roff")), v("ks", 0, C_), ALU.add)
         stay = v("pls", 16, 16 + K_)
-        d = rising("m5", stay, K_)
+        d = rising("m6", stay, K_)
         tt(v("m3"), v("nsr", 0, C_ + 1, by=v("qoff")), v("wt"), ALU.mult)
-        cp(v("pl", 0, 10), d)
-        unit = S_ / w
-        at = (0, 3, ZS, ZS + 3)
-
-        def count(f):
-            act(plane("jk", f, K_, C_), stay, AF.Sign, -unit, col("xs", f), acc=col("zz", at[f]))
-        count(0)
-        count(1)
-        act(v("kw", 0, K_), v("kp", 0, w, by=v("pl", 0, 10)))
-        count(2)
-        count(3)
-        scan(v("m4"), v("rm"), v("m3"), 0.0, ALU.mult, ALU.add)
-        ts(col("sm", 0), col("zz", 3), col("zz", 0), ALU.subtract, 0.5, ALU.mult)
-        ts(v("tn"), v("m4", 15, S_, 16), I_, ALU.add)
-        ts(col("zz", ZS - 1), col("sm", 0), float(Q1), ALU.max, -float(GAP), ALU.mult)
         if first:
             constants_4()
         if last:
             quant(v("qv"), v("sv"), v("vt"))
+        cp(v("pl", 0, 10), d)
+        unit = S_ / w
+        at = (0, 3, ZS, ZS + 3)
+        for f in range(4):
+            act(plane("jk", f, K_, C_), stay, AF.Sign, -unit, col("xs", f), acc=col("zz", at[f]))
 
         def stayers(b):
-            act(plane("tc", b, K_, PW), plane("t64", b, w, by=v("pl", 0, 10)), scale=1.0 / 64)
+            act(plane("tc", b, K_, PW, ST), plane("t64", b, w, by=v("pl", 0, 10)), scale=1.0 / 64)
         stayers(0)
+        stayers(1)
+        if last:
+            act(v("olw", ST), stay)
 
         for c in range(2):
-            ts(v("ck", KW * c + 1, KW * c + 1 + K_), v("kw", 0, K_), col(ka, c), ALU.is_le)
+            ts(v("ck", KW * c + 1, KW * c + 1 + C_), v("km"), col(ka, c), ALU.is_le)
+        scan(v("m4"), v("rm"), v("m3"), 0.0, ALU.mult, ALU.add)
+        ts(col("sm", 0), col("zz", 3), col("zz", 0), ALU.subtract, 0.5, ALU.mult)
         scan(v("cn"), v("rk2"), v("ck"), 0.0, ALU.mult, ALU.add)
-        cp(v("noff"), v("cn", K_, 2 * KW, KW))
-        cp(v("qo"), v("cn", K_ + 1, 2 * KW, KW))
+        ts(v("tn"), v("m4", 15, S_, 16), I_, ALU.add)
+        ts(col("zz", ZS - 1), col("sm", 0), float(Q1), ALU.max, -float(GAP), ALU.mult)
+        cp(v("qo"), v("cn", C_ + 1, 2 * KW, KW))
+        cp(v("noff"), v("cn", C_, 2 * KW, KW))
+        cp(v("aa", by=v("qo")), v("zr"))
         before = v("pls", 0, 16 + K_, by=v("noff"))
         for f in (0, 2):
             act(v("ju", 16 * f, 16 * f + 32), before, AF.Sign, -unit, col("xs", f), acc=col("zz", at[f] + 1))
             ts(v("zz", at[f + 1] + 1, at[f + 1] + 1 + L_), before, unit, ALU.mult, col("xs", f + 1), ALU.is_lt)
-        stayers(1)
-        cp(v("aa", by=v("qo")), v("zr"))
+        stayers(2)
+        stayers(3)
+        tt(v("idv"), v("ndm", by=v("qo")), v("iob", 0, L_), ALU.add)
+        scan(v("tb"), ones, v("aa"), ST - 1.0, ALU.mult, ALU.add)
         scan(v("zo"), v("zm"), v("zz"), 0.0, ALU.mult, ALU.add)
-        scan(v("tb", 0, C_), ones, v("aa"), -1.0, ALU.mult, ALU.add)
+        cp(v("tb", by=v("qo")), v("idv"))
         ts(col("vo", 0), col("zo", ZS - 1), col("zo", ZW - 1), ALU.min, col("xs", 4), ALU.subtract)
         cp(v("xo", 0, 2), v("zo", 2, ZW, ZS))
         cp(v("xo", 2, 4), v("zo", ZS - 2, ZW, ZS))
+        d = rising("m5", v("tb"), C_)
         tt(v("sm", 16, 32), v("lv", by=col("vo", 0)), v("mw"), ALU.add)
-        act(v("gq"), v("tab", by=v("xo")))
-        for b in (2, 3):
-            stayers(b)
-        for b in range(4):
+        for b in (0, 2, 1, 3):
             mm("p%d" % b, 128, v("qe", 128 * b, 128 * b + 128), v("se", 128 * b, 128 * b + 128), v(qb, 0, 128), v(sb, 96, 224))
-        for b in range(4):
-            act(plane("tc", b, L_, PW, K_), v("p%d" % b, 0, L_))
-        if last:
-            act(v("olw", 0, K_), stay)
-        else:
-            act(v("ax"), v(ka, 0, 2, by=axo))
+        for b in (0, 2, 1, 3):
+            act(plane("tc", b, L_, PW), v("p%d" % b, 0, L_))
+            if b == 2:
+                act(v("gq"), v("tab", by=v("xo")))
         ts(col("sm", 1), col("zo", ZS - 2), col("sm", 0), ALU.is_gt, 16.0, ALU.mult)
+        cp(v("to"), d)
         reduce(col("sm", 2), v("sm", 16, 32), ALU.max)
-        cp(v("tb", 0, C_, by=v("qo")), v("idr"))
-        ts(col("vo", 2), col("sm", 2), col("sm", 1), ALU.max, I_, ALU.add)
         tt(v("cand", 16, 48), v("gq", 0, 32), v("gq", 32, 64), ALU.add)
         tt(v("cand", 0, 16), v("gq", 0, 16), v("tn"), ALU.add)
-        ts(v("qoff"), v("cand", by=col("vo", 2)), float(C_), ALU.min)
-        tt(v("m1"), v("tb", 0, C_ + 1, by=v("qoff")), v("dm"), ALU.mult)
-        new_state(S_, not last)
+        ts(col("vo", 2), col("sm", 2), col("sm", 1), ALU.max, I_, ALU.add)
 
-    mm("pp", S_, v("qv"), v("sv"), v("qf"), v("sf"))
-    act(v("olr"), v("olw", 0, C_ + 1, by=v("to")))
+        def merged(b):
+            (cp if b < 2 else act)(plane("mq", b, C_, MW), plane("tc", b, PW, PW, by=v("to")))
+
+        def placed(b):
+            (cp if b < 2 else act)(v("ft", b, 4 * S_, 4), plane("mq", b, C_ + 1, MW, by=v("qoff")))
+        merged(0)
+        ts(v("qoff"), v("cand", by=col("vo", 2)), float(C_), ALU.min)
+        for b in (1, 2, 3):
+            merged(b)
+        for b in range(4):
+            placed(b)
+        if not last:
+            tt(v("hh", 0, 16), v("cand", by=col("vo", 2)), v("kc"), ALU.min)
+            quant(v("qf"), v("sf"), v("ft"))
+            cp(v("uq"), v("hh", 0, 16))
+
+    act(v("ks", 0, C_), v("olw", by=v("to")))
+    for h, bank in enumerate(("pp", "pq")):
+        quant(v("qf", 128 * h, 128 * h + 128), v("sf", 128 * h, 128 * h + 128), v("ft", 512 * h, 512 * h + 512))
+        mm(bank, 128, v("qv"), v("sv"), v("qf", 128 * h, 128 * h + 128), v("sf", 128 * h, 128 * h + 128))
     dma("Y", [v("qf")], [], T.oc[:], T.qf[:].bitcast(dt.uint8))
-    cp(v("ys"), v("pp", 0, S_))
-    dma("S", [v("olr")], [], T.ol[:], T.olr[0:128:16, :])
-    dma("S", [v("ys")], [], T.y[:], T.ys[:])
+    act(v("psb", 0, 128), v("pp", 0, 128))
+    cp(v("kp"), v("ks", 0, C_ + 1, by=v("qoff")))
+    cp(v("psb", 128, 256), v("pq", 0, 128))
+    dma("S", [v("psb")], [], T.y[:], T.psb[:])
     for k in range(4):
         dma("Y", [v("sf")], [], T.osc[4 * k:4 * k + 4, :], T.sf[32 * k:32 * k + 4, :])
+    dma("Y", [v("kp")], [], T.ol[:], T.kp[0:128:16, :])
     for s, k in cnt.items():
         if k:
             g.wait_ge(T.sem[s], k)

@@ -11,12 +11,11 @@ CW = C_ + 1
 ST = 64
 PW = ST + K_
 MW = 208
-PR1 = 12
+PR1 = 10
 GAP = 512
 B64, IO, TABW = 16, 224, 424
 ZS = L_ + 6
 ZW = 2 * ZS - 1
-KW = C_ + 2
 CX, U8, BF, F32, I32, U16 = "float8_e4m3fn_x4", "uint8", "bfloat16", "float32", "int32", "uint16"
 
 
@@ -31,29 +30,29 @@ SCRATCH = {
     "qf": _sb(256, CX), "sf": _sb(256, U8), "qt": _sb(256, CX), "st": _sb(256, U8),
     "ft": _sb(1024, BF), "f64": _sb(1024, BF), "tt": _sb(1024, BF), "t64": _sb(1024, BF), "tc": _sb(4 * PW, BF), "bt": _sb(512, BF),
     "pi": _sb(8, I32), "ic": _sb(4, F32), "iu": _sb(24, I32), "cu": _sb(24, U16), "aoff": _sb(2, U16),
-    "ioj": _sb(256, BF), "iob": _sb(256, BF), "iof": _sb(64, F32), "cr": _sb(8, F32), "dc": _sb(16, F32),
-    "dm": _sb(256, BF), "rm": _sb(256, BF), "gt": _sb(192, BF), "bm": _sb(192, BF), "wt": _sb(256, BF), "rs": _sb(4 * CW, BF), "rk2": _sb(2 * KW, BF),
+    "ioj": _sb(256, BF), "iob": _sb(256, BF), "iof": _sb(64, F32), "dc": _sb(24, F32),
+    "dm": _sb(256, BF), "rm": _sb(256, BF), "gt": _sb(192, BF), "bm": _sb(192, BF), "wt": _sb(128, BF), "rs": _sb(4 * CW, BF),
     "eqt": _sb(208, BF), "eqs": _sb(192, BF), "nst": _sb(192, BF), "yc": _sb(12, F32), "kc": _sb(16, F32), "zr": _sb(32, BF),
     "lv": _sb(112, BF), "mw": _sb(16, F32), "tab": _sb(TABW, F32), "yy": _sb(384, F32), "yr": _sb(384, F32), "xs": _sb(8, F32),
-    "zi": _sb(ZW, F32), "zm": _sb(ZW, F32), "zz": _sb(ZW, F32), "zo": _sb(ZW, F32),
+    "la": _sb(8, U16), "zm": _sb(ZW, F32), "zz": _sb(ZW, F32), "zo": _sb(ZW, F32),
     "psb": _sb(256, F32), "pc": _sb(192, F32), "msk": _sb(192, F32), "sc": _sb(192, F32), "eq": _sb(192, BF), "cor": _sb(192, BF),
     "cmp": _sb(CW * 12, BF), "cs": _sb(CW * NV, BF), "gl": _sb(24, F32), "roff": _sb(12, U16), "k0": _sb(192, F32), "k1": _sb(192, F32),
     "nsr": _sb(MW, BF), "pre": _sb(192, BF), "hh": _sb(32, F32), "doff": _sb(12, U16), "jk": _sb(4 * 192, BF),
     "pr": _sb(C_ + S_, BF), "pls": _sb((K_ + 16) * L_ + 16, BF), "m3": _sb(256, BF), "m4": _sb(256, BF),
     "m5": _sb(192, BF), "m6": _sb(160, BF), "pl": _sb(12, U16), "poff": _sb(12, U16), "mq": _sb(4 * MW, BF), "nb": _sb(192, BF), "ndm": _sb(192, BF),
-    "kw": _sb(PW, F32), "ks": _sb(MW, F32), "km": _sb(192, F32), "kp": _sb(256, F32), "ck": _sb(2 * KW, BF), "cn": _sb(2 * KW, BF), "noff": _sb(2, U16), "qo": _sb(2, U16),
+    "kw": _sb(PW, F32), "ks": _sb(MW, F32), "km": _sb(192, F32), "kp": _sb(256, F32), "ck": _sb(C_ + 1, BF), "cn": _sb(C_ + 2, F32), "noff": _sb(2, U16), "qo": _sb(2, U16),
     "aa": _sb(192, BF), "tb": _sb(192, BF), "idv": _sb(32, BF), "ju": _sb(64, BF), "sm": _sb(32, F32), "tn": _sb(16, F32),
     "xo": _sb(4, U16), "vo": _sb(4, U16), "gq": _sb(64, F32), "cand": _sb(96, F32), "qoff": _sb(16, U16), "to": _sb(12, U16),
     "uq": _sb(16, U16), "ax": _sb(64, F32), "ay": _sb(64, F32), "olw": _sb(PW, F32),
 }
-for _t in ["p0", "p1", "p2", "p3", "pp", "pq"]:
-    SCRATCH[_t] = ("psum", [128, 512], F32)
+for _t in range(8):
+    SCRATCH["p%d" % _t] = ("psum", [128, 512], F32)
 for _t in range(R_):
     SCRATCH["ko%d" % _t] = _sb(8, F32)
     SCRATCH["ka%d" % _t] = _sb(8, F32)
-    SCRATCH["qb%d" % _t] = _sb(160, CX)
+    SCRATCH["qb%d" % _t] = _sb(160 if _t else 256, CX)
     SCRATCH["sb%d" % _t] = _sb(256, U8)
-SEMAPHORES = ["cV", "cS", "cP", "cG", "sent"] + ["d%d" % _t for _t in range(14)] + ["aK%d" % _t for _t in range(R_)] + ["aB%d" % _t for _t in range(R_)]
+SEMAPHORES = ["cV", "cS", "cP", "cG", "sent", "aT", "lT", "lL"] + ["d%d" % _t for _t in range(14)] + ["aK%d" % _t for _t in range(R_)] + ["aB%d" % _t for _t in range(R_)]
 
 
 def _bits(es):
@@ -66,10 +65,10 @@ def _relays(src, dst, topo):
     return c[0], c[1], c[2]
 
 
-def _send(g, T, topo, src, dst, out, in_, sem):
+def _send(g, T, topo, src, dst, out, in_, sem, left="sent"):
     rid, pid = topo.addr(dst, src)
     es = topo.engines(src, dst)
-    g.remote_dma(out, in_, T.sem[sem], T.sem.sent, pid, rid, _bits(es))
+    g.remote_dma(out, in_, T.sem[sem], T.sem[left], pid, rid, _bits(es))
     return len(es)
 
 
@@ -90,11 +89,18 @@ def _hand_on(g, core, T, topo):
         src, dst = cores[r], cores[(r + 1) % len(cores)]
         rk, rb, rs = _relays(src, dst, topo)
         sent = 0
+        if core in (rk, rb, rs):
+            ap = T.sb0[:] if core == rs else T.qb0[:, 128 * (core == rb):128 * (core == rb) + 128].bitcast(dt.uint8)
+            g.wait_ge(T.sem.aT, len(topo.engines(src, core)))
+            sent += _send(g, T, topo, core, dst, ap, ap, "aT")
         for t in range(R_):
             if core == rk:
                 g.wait_ge(T.sem["aK%d" % t], len(topo.engines(src, core)))
                 sent += _send(g, T, topo, core, dst, T["ka%d" % t][:, 0:2], T["ka%d" % t][:, 0:2], "aK%d" % t)
-            if core in (rb, rs):
+            if core == rb and t == 0:
+                g.wait_ge(T.sem.aB0, len(topo.engines(src, core)))
+                sent += _send(g, T, topo, core, dst, T.la[:, 0:2], T.la[:, 0:2], "aB0")
+            if core in (rb, rs) and t > 0:
                 ap = T["qb%d" % t][:, 0:32].bitcast(dt.uint8) if core == rb else T["sb%d" % t][:, 96:128]
                 g.wait_ge(T.sem["aB%d" % t], len(topo.engines(src, core)) // 2)
                 sent += _send(g, T, topo, core, dst, ap, ap, "aB%d" % t)
@@ -125,7 +131,7 @@ def rank_program(g, core, T, topo):
         return v(name, k, k + 1)
 
     Q = {"V": g.vector, "S": g.scalar, "P": g.tensor, "G": g, "Y": g.sync}
-    cnt = {"cV": 0, "cS": 0, "cP": 0, "cG": 0, "sent": 0}
+    cnt = {"cV": 0, "cS": 0, "cP": 0, "cG": 0, "sent": 0, "lT": 0, "lL": 0}
     clock = {q: {} for q in Q}
     snap, seen = {}, {}
     ndma = [0]
@@ -182,6 +188,11 @@ def rank_program(g, core, T, topo):
         for name, bits, w in touches([], views):
             seen.setdefault(name, []).append(((sem, val), bits, True))
 
+    def leaves(views, sem):
+        snap[(sem, cnt[sem])] = {sem: cnt[sem]}
+        for name, bits, w in touches(views, []):
+            seen[name].append(((sem, cnt[sem]), bits, False))
+
     V, A = g.vector, g.scalar
 
     def x(a):
@@ -236,14 +247,14 @@ def rank_program(g, core, T, topo):
 
     dma("Y", [], [v("ut")], T.ut[:], T.u[:])
     dma("S", [], [v("xt")], T.xt[:], T.x[:])
-    dma("Y", [], [v("qw")], T.qw[:].bitcast(dt.uint8), T.wc[:])
+    dma("Y", [v("xt")], [v("qw")], T.qw[:].bitcast(dt.uint8), T.wc[:])
     dma("Y", [], [v("sw")], T.sw[:], T.ws[:])
     dma("Y", [], [v("vt")], T.vt[:], T.v[:])
 
     iota(col("pi", 0), [[0, 1]], 0, 1)
     iota(v("iu", 0, 8), [[16, 8]])
     iota(v("iof"), [[1, 64]])
-    iota(v("cr"), [[16, 4], [1, 2]])
+    iota(v("dc", 16), [[16, 4], [1, 2]])
     iota(v("ioj"), [[0, 16], [1, 16]])
     iota(v("iu", 8, 20), [[16, 12]], 15)
     iota(v("iu", 20, 24), [[1, 2], [0, 2]])
@@ -255,9 +266,9 @@ def rank_program(g, core, T, topo):
     iota(v("mw"), [[4, 4], [0, 4]])
     iota(v("kc"), [[16, 16]], C_)
     for view, c in [(v("eqt", 0, 16), 0), (v("eqt", 32), 0), (v("eqs", 32), 0), (v("nst", 0, L_), 1), (v("nst", L_), 0), (col("nsr", C_), 1),
-                    (v("pls", 0, 16), 0), (v("bt", 0, 384), 0), (v("rk2"), 1), (v("rk2", 0, 2 * KW, KW), 0), (v("ck", 0, 2 * KW, KW), 15),
-                    (v("zi"), 2), (v("zi", 0, ZW, ZS), 0), (v("zi", 2, ZW, ZS), 1), (v("zi", 3, ZW, ZS), -4), (v("zi", 4, ZW, ZS), 1),
-                    (col("zi", ZS - 1), 2 * GAP), (v("zz", 2, ZW, ZS), C_ // 2 + IO), (col("zz", ZS - 2), K_ // 2 + IO),
+                    (v("pls", 0, 16), 0), (v("bt", 0, 384), 0), (col("ck", C_), 16),
+                    (v("zo"), 2), (v("zo", 0, ZW, ZS), 0), (v("zo", 2, ZW, ZS), 1), (v("zo", 3, ZW, ZS), -4), (v("zo", 4, ZW, ZS), 1),
+                    (col("zo", ZS - 1), 2 * GAP), (v("zz", 2, ZW, ZS), C_ // 2 + IO), (col("zz", ZS - 2), K_ // 2 + IO),
                     (v("aa"), 1), (v("zr"), 0), (v("lv", 0, 2), -100), (v("lv", 2, Q2 + 3), 0), (v("lv", Q2 + 3), 48),
                     (v("tab", 176, IO), 0), (v("cand", 64, 80), 0), (v("mq", C_, 4 * MW, MW), 0), (col("ks", C_), -1), (v("kw", L_, ST), 0)]:
         fill(view, c)
@@ -270,22 +281,24 @@ def rank_program(g, core, T, topo):
     ms(v("rs", 0, 4 * CW, CW), 0.0)
     cp(v("ic"), v("pi", 4, 8))
     cp(offu, v("iu", 0, 8))
-    ts(v("dc", 0, 8), v("cr"), I_, ALU.add, 1.0 / 64, ALU.mult)
-    ts(v("dc", 8, 10), v("cr", 0, 2), I_, ALU.add, 1.0 / 16, ALU.mult)
+    ts(v("dc", 0, 8), v("dc", 16), I_, ALU.add, 1.0 / 64, ALU.mult)
+    ts(v("dc", 8, 10), v("dc", 16, 18), I_, ALU.add, 1.0 / 16, ALU.mult)
     ts(v("dm"), v("ioj"), I_, ALU.is_equal)
+    quant(v("qu"), v("su"), v("ut"))
     ts(v("rm"), v("ioj"), 1.0, ALU.min)
     ts(v("gt"), v("ioj", 0, C_), I_, ALU.is_gt)
     ts(v("bm"), v("ioj", 0, C_), I_, ALU.is_le, 512.0, ALU.mult)
+    cp(v("qur", cast=dt.uint32), v("qu", cast=dt.uint32, by=offu))
+    act(v("sur"), v("su", by=offu))
+    quant(v("qt", 0, C_), v("st", 0, C_), v("xt"))
+    ts(v("ndm"), v("ioj", 0, C_), I_, ALU.not_equal, 255.0, ALU.mult)
     cp(v("cu", 8, 24), v("iu", 8, 24))
     ts(v("m3", 0, 16), v("ioj", 0, 16), I_, ALU.is_lt)
     ts(v("m3", 16, 32), v("dm", 0, 16), float(GAP), ALU.mult)
     cp(v("eqt", 16, 32), v("dm", 0, 16))
     cp(v("eqs", 0, 16), v("dm", 0, 16))
-    tt(v("wt", 0, 16), v("m3", 16, 32), v("m3", 0, 16), ALU.subtract)
     ts(v("eqs", 16, 32), v("dm", 0, 16), -1.0, ALU.mult)
-    quant(v("qu"), v("su"), v("ut"))
-    quant(v("qt", 0, C_), v("st", 0, C_), v("xt"))
-    cp(v("qur", cast=dt.uint32), v("qu", cast=dt.uint32, by=offu))
+    tt(v("wt", 0, 16), v("m3", 16, 32), v("m3", 0, 16), ALU.subtract)
 
     HALF, BIG = 0.4921875, 12582912.0
     for h in range(2):
@@ -296,17 +309,17 @@ def rank_program(g, core, T, topo):
             a = 192 * h + 16 + 40 * lp
             act(v("yy", a, a + 40), v("iof", Q1, Q1 + 40), AF.Identity, col("dc", 2 * lp + h), HALF)
         act(v("yy", 192 * h + 176, 192 * h + 192), v("iof", 0, 16), AF.Identity, 12.0, col("dc", 10 + h))
-    act(v("sur"), v("su", by=offu))
-    for bank in ("pp", "pq"):
+    for bank in ("p4", "p5"):
         mm(bank, C_, v("qur"), v("sur"), v("qt", 0, C_), v("st", 0, C_))
-    act(v("yr"), v("yy"), AF.Identity, 1.0, BIG)
 
     def constants_s():
-        for k in range(4):
+        act(v("yr"), v("yy"), AF.Identity, 1.0, BIG)
+        for k in range(3):
             act(v("wt", 16 << k, 32 << k), v("wt", 0, 16 << k))
         for k, c, b in ((0, I_, 0), (1, I_, 16), (2, I12, 0), (3, I12, 64)):
             act(col("xs", k), c, AF.Identity, 16.0, b - 0.5)
         act(col("xs", 4), I3, AF.Identity, 40.0)
+        act(col("xs", 5), I_, AF.Identity, 1.0, C_ + 16.0)
         act(col("zz", ZW - 1), I3, AF.Identity, 40.0, float(K_ // 2 + IO + B64 - Q1))
 
     def constants_1():
@@ -323,19 +336,20 @@ def rank_program(g, core, T, topo):
 
     def constants_4():
         cp(v("cand", 80, 96), v("cand", 48, 64))
-        ts(v("ndm"), v("ioj", 0, C_), I_, ALU.not_equal, 255.0, ALU.mult)
-        ts(v("ck", KW - 1, 2 * KW, KW), v("iof", 0, 32, 16), I_, ALU.add, -15.0, ALU.add)
-        ts(v("zm"), v("zi"), 0.5, ALU.mult)
+        ts(v("zm"), v("zo"), 0.5, ALU.mult)
+
+    def constants_5():
         ts(v("mw"), v("mw"), I12, ALU.is_equal, 32.0, ALU.mult)
         ts(v("aoff"), v("iof", 0, 64, 32), I_, ALU.add, I16, ALU.add)
         ts(v("kc"), v("kc"), I_, ALU.add)
-        for b in range(4):
-            quant(v("qe", 128 * b, 128 * b + 128), v("se", 128 * b, 128 * b + 128), v("et", 3 - b, 515 - b))
 
-    def ranks(row, in_psum):
-        for a in (96, 0):
-            scan(v("sc", a, a + 96), v("rm", 0, 96), v("msk", a, a + 96), 0.0, ALU.mult, ALU.add)
+    def quant_e(b):
+        quant(v("qe", 128 * b, 128 * b + 128), v("se", 128 * b, 128 * b + 128), v("et", 3 - b, 515 - b))
 
+    def own(a, b):
+        scan(v("sc", a, b), v("rm", 0, b - a), v("msk", a, b), 0.0, ALU.mult, ALU.add)
+
+    def ranks(late, equal):
         def s(c):
             return col("sc", 16 * c + 15)
 
@@ -344,99 +358,158 @@ def rank_program(g, core, T, topo):
 
         def compare(c):
             e = 16 * c + 16
-            ts(part(c, 0, e), v(row, 0, e), s(c), ALU.is_le)
-            ts(part(c, e, C_), v(row, e, C_), s(c), ALU.is_lt)
-        for c in range(NV, 12):
-            act(part(c, 0, C_), v(row, 0, C_), AF.Sign, -1.0, s(c))
-        compare(NV - 1)
-        if in_psum:
-            tt(v("eq"), v("sc"), v("pp", 0, C_), ALU.is_equal)
-        else:
-            tt(v("eq"), v("sc", by=bco), v(row, 0, C_), ALU.is_equal)
+            ts(part(c, 0, e), v("pc", 0, e), s(c), ALU.is_le)
+            ts(part(c, e, C_), v("pc", e, C_), s(c), ALU.is_lt)
+        late()
+        for c in reversed(range(NV, 12)):
+            act(part(c, 0, C_), v("pc"), AF.Sign, -1.0, s(c))
         compare(0)
+        equal()
         compare(1)
-        scan(v("cor"), v("eq"), v("gt"), 0.0, ALU.add, ALU.mult)
         compare(2)
+        scan(v("cor"), v("eq"), v("gt"), 0.0, ALU.add, ALU.mult)
         compare(3)
+        compare(4)
         tt(v("cmp", C_, 12 * CW, CW), v("yc"), v("cor", 15, C_, 16), ALU.subtract)
-        for c in range(4, NV - 1):
+        for c in range(5, NV):
             compare(c)
-        for c in range(NV, 12):
+        for c in reversed(range(NV, 12)):
             act(part(c, 0, 16 * c + 16), part(c, 0, 16 * c + 16), AF.Relu, -1.0, acc=col("gl", c - NV))
-        for c in range(NV, 12):
+        for c in range(NV, 11):
             act(part(c, 16 * c + 16, CW), part(c, 16 * c + 16, CW), AF.Relu, acc=col("gl", 8 + c - NV))
         for a, b in ((0, 4), (4, NV)):
             scan(v("cs", CW * a, CW * b), v("rs", 0, CW * (b - a)), v("cmp", CW * a, CW * b), 0.0, ALU.mult, ALU.add)
-        tt(v("gl", 16, 16 + NS), v("gl", 8, 8 + NS), v("gl", 0, NS), ALU.subtract)
+        ts(col("roff", 11), part(11, C_, CW), col("gl", NS - 1), ALU.subtract)
+        for k in range(NS - 1):
+            ts(col("roff", NV + k), col("gl", 8 + k), col("gl", k), ALU.subtract)
         cp(v("roff", 0, NV), v("cs", C_, CW * NV, CW))
-        cp(v("roff", NV), v("gl", 16, 16 + NS))
 
     def rising(buf, a, w):
         scan(v(buf, 0, w), v("bm", 0, w), a, 0.0, ALU.add, ALU.min)
         return v(buf, 15, w, 16)
 
-    def scores_from_psum():
-        for a in (96, 0):
-            tt(v("msk", a, a + 96), v("pp", a, a + 96), v("dm", 0, 96), ALU.mult)
-        act(v("pc"), v("pq", 0, C_))
+    def span(w, h):
+        return (0, 128) if h == 0 else (128, w)
 
-    scores_from_psum()
-    ranks("pc", True)
-    cp(v("tb", 0, C_, by=v("roff")), v("iob", 0, C_))
+    def quant_half(q, s, tile, w, h):
+        a = h * (w - 128)
+        quant(v(q, 128 * h, 128 * h + 128), v(s, 128 * h, 128 * h + 128), v(tile, 4 * a, 4 * a + 512))
+
+    def mm_half(bank, lq, ls, q, s, h):
+        mm(bank, 128, lq, ls, v(q, 128 * h, 128 * h + 128), v(s, 128 * h, 128 * h + 128))
+
+    def result(bank, w, h):
+        return v(bank, h * (S_ - w), 128)
+
+    def cols(tile, b, w, h):
+        return v(tile, 4 * span(w, h)[0] + b, 4 * span(w, h)[1], 4)
+
+    def part_of(name, b, w, h):
+        return v(name, S_ * b + span(w, h)[0], S_ * b + span(w, h)[1])
+
+    def gather_state(src, stride, width, by, w, pause):
+        for h in range(2):
+            a, b_ = span(w, h)
+            for b in range(4):
+                (cp if b < 2 else act)(cols("ft", b, w, h), plane(src, b, width, stride, by=v(by, a // 16, b_ // 16)))
+                if b == 0:
+                    pause[h]()
+        quant_half("qf", "sf", "ft", w, 0)
+        pause[2]()
+        quant_half("qf", "sf", "ft", w, 1)
+
+    def nothing():
+        pass
+
+    for a in (0, 96):
+        tt(v("msk", a, a + 96), v("p4", a, a + 96), v("dm", 0, 96), ALU.mult)
+    act(v("pc"), v("p5", 0, C_))
+    own(0, 96)
+    ranks(lambda: own(96, C_), lambda: tt(v("eq"), v("sc"), v("p4", 0, C_), ALU.is_equal))
+    tt(v("eq"), v("ndm", by=v("roff")), v("iob", 0, C_), ALU.add)
     for b in range(4):
         act(plane("tc", b, C_, PW), v("xt", b, 768, 4))
-    tt(v("eq"), v("tb"), v("dm", 0, C_), ALU.mult)
+    quant_e(0)
+    quant_e(1)
+    cp(v("tb", by=v("roff")), v("eq"))
     constants_s()
-    scan(v("m5"), v("rm", 0, C_), v("eq"), 0.0, ALU.mult, ALU.add)
-    cp(v("to"), v("m5", 15, C_, 16))
-    for b in range(4):
-        (cp if b < 2 else act)(v("ft", b, 4 * C_, 4), plane("tc", b, C_, PW, by=v("to")))
-    quant(v("qf", 0, C_), v("sf", 0, C_), v("ft", 0, 4 * C_))
+    quant_e(2)
+    quant_e(3)
+    cp(v("to"), rising("m5", v("tb"), C_))
+    gather_state("tc", PW, C_, "to", C_, [nothing] * 3)
+
+    def in_order(a, b):
+        cp(v("pr", by=v("uq", a, b)), v("iob", 16 * a, 16 * b))
 
     for t in range(R_):
         first, last = t == 0, t == R_ - 1
         w = C_ if first else S_
         ko, ka, qb, sb = ["%s%d" % (k, t) for k in ("ko", "ka", "qb", "sb")]
         held = v("iob", 0, C_) if first else v("pr", 0, C_)
-        for b in range(4):
-            mm("p%d" % b, w, v("qw", 128 * b, 128 * b + 128), v("sw", 128 * b, 128 * b + 128), v("qf", 0, w), v("sf", 0, w))
-            act(plane("f64", b, w), v("ft", b, 4 * w, 4), scale=64.0)
+        for h in range(2):
+            for b in range(4):
+                mm_half("p%d" % (4 * h + b), v("qw", 128 * b, 128 * b + 128), v("sw", 128 * b, 128 * b + 128), "qf", "sf", h)
+            act(v("f64", 512 * h, 4 * span(w, h)[1]), v("ft", 512 * h, 4 * span(w, h)[1]), scale=64.0)
         if first:
             constants_1()
         else:
-            cp(v("pr", by=v("uq", 0, PR1)), v("iob", 0, 16 * PR1))
             act(v("ax"), v("ka%d" % (t - 1), 0, 2, by=axo))
-        for b in range(4):
-            tt(plane("t64", b, w), v("p%d" % b, 0, w), plane("f64", b, w), ALU.add)
-            if b < 2:
-                act(v("tt", b, 4 * w, 4), plane("t64", b, w), scale=1.0 / 64)
+        for h in range(2):
+            for b in range(4):
+                tt(part_of("t64", b, w, h), result("p%d" % (4 * h + b), w, h), cols("f64", b, w, h), ALU.add)
+                if 4 * h + b < 6:
+                    act(cols("tt", b, w, h), part_of("t64", b, w, h), scale=1.0 / 64)
         if not first:
-            act(v("kw", ST), v("ks" if t == 1 else "kp", 0, C_ if t == 1 else S_, by=v("pl", 0, 10)))
             op("V", [v("ax")], [v("ay")], lambda: V.transpose(T.ay[:], T.ax[:]))
-        for b in range(2, 4):
-            ts(v("tt", b, 4 * w, 4), plane("t64", b, w), 1.0 / 64, ALU.mult)
+            in_order(PR1, 16)
+            act(v("kw", ST), v("ks" if t == 1 else "kp", 0, C_ if t == 1 else S_, by=v("pl", 0, 10)))
+        for b in (2, 3):
+            ts(cols("tt", b, w, 1), part_of("t64", b, w, 1), 1.0 / 64, ALU.mult)
+        quant_half("qt", "st", "tt", w, 0)
+        for bank in ("p0", "p1") if first else ("p0",):
+            mm_half(bank, v("qur"), v("sur"), "qt", "st", 0)
         if first:
-            quant(v("qt", 0, w), v("st", 0, w), v("tt", 0, 4 * w))
-            for bank in ("pp", "pq"):
-                mm(bank, w, v("qur"), v("sur"), v("qt", 0, w), v("st", 0, w))
             act(v("ks", 0, C_), v("pc", by=v("to")))
-            constants_2()
-            scores_from_psum()
         else:
-            for h, bank in enumerate(("pp", "pq")):
-                quant(v("qt", 128 * h, 128 * h + 128), v("st", 128 * h, 128 * h + 128), v("tt", 512 * h, 512 * h + 512))
-                mm(bank, 128, v("qur"), v("sur"), v("qt", 128 * h, 128 * h + 128), v("st", 128 * h, 128 * h + 128))
             act(v("kw", 0, L_), v("ay", by=v("aoff")))
             act(v("ks", 0, C_), v("kw", by=v("to")))
-            act(v("psb", 0, 128), v("pp", 0, 128))
-            cp(v("pr", by=v("uq", PR1, 16)), v("iob", 16 * PR1, 256))
             d = rising("m5", held, C_)
-            cp(v("psb", 128, 256), v("pq", 0, 128))
+        quant_half("qt", "st", "tt", w, 1)
+        if first:
+            constants_2()
+        else:
             cp(v("poff"), d)
-            for a in (6, 0):
-                tt(v("msk", 16 * a, 16 * a + 96), v("psb", by=v("poff", a, a + 6)), v("dm", 0, 96), ALU.mult)
-            act(v("pc"), v("psb", by=v("poff")))
-        ranks("pc", first)
+        for bank in ("p2", "p3") if first else ("p2",):
+            mm_half(bank, v("qur"), v("sur"), "qt", "st", 1)
+        if first:
+            for relay, src, dst in ((relay_k, v("qt", 0, 128, cast=dt.uint8), v(qb, 0, 128, cast=dt.uint8)),
+                                    (relay_b, v("qt", 128, 256, cast=dt.uint8), v(qb, 128, 256, cast=dt.uint8)), (relay_s, v("st"), v(sb))):
+                order("G", touches([src], []))
+                cnt["lT"] += _send(g, T, topo, core, relay, dst[0], src[0], "aT", "lT")
+            leaves([v("qt"), v("st")], "lT")
+            arrives([v(qb), v(sb)], "aT", sum(len(topo.engines(k, core)) for k in (from_k, from_b, from_s)))
+            tt(v("msk", 0, 128), v("p0", 0, 128), v("dm", 0, 128), ALU.mult)
+            act(v("pc", 0, 128), v("p1", 0, 128))
+            tt(v("msk", 128), result("p2", w, 1), v("dm", 0, 64), ALU.mult)
+            act(v("pc", 128), result("p3", w, 1))
+            own(0, 128)
+
+            def equal():
+                tt(v("eq", 0, 128), v("sc", 0, 128), v("p0", 0, 128), ALU.is_equal)
+                tt(v("eq", 128), v("sc", 128), result("p2", w, 1), ALU.is_equal)
+            own(128, C_)
+            ranks(constants_5, equal)
+        else:
+            act(v("psb", 0, 128), v("p0", 0, 128))
+            cp(v("psb", 128), v("p2", 0, 128))
+            act(v("pc", 0, 64), v("psb", 0, 128, by=v("poff", 0, 4)))
+            tt(v("msk", 0, 64), v("psb", 0, 128, by=v("poff", 0, 4)), v("dm", 0, 64), ALU.mult)
+            for c in (8, 4):
+                tt(v("msk", 16 * c, 16 * c + 64), v("psb", by=v("poff", c, c + 4)), v("dm", 0, 64), ALU.mult)
+            act(v("pc", 64), v("psb", by=v("poff", 4, 12)))
+            own(0, 64)
+            own(128, C_)
+            ranks(lambda: own(64, 128), lambda: tt(v("eq"), v("sc", by=bco), v("pc"), ALU.is_equal))
         act(v("nsr", 0, C_), v("nst", by=v("roff")))
         tt(v("k0"), v("eqt", 16, 208, by=v("roff")), v("pc"), ALU.mult)
         tt(v("k1"), v("eqt", 0, 192, by=v("roff")), v("pc"), ALU.mult)
@@ -446,9 +519,19 @@ def rank_program(g, core, T, topo):
         order("G", touches([v(ko, 0, 2)], []))
         cnt["sent"] += _send(g, T, topo, core, relay_k, T[ka][:, 0:2], T[ko][:, 0:2], "aK%d" % t)
         arrives([v(ka, 0, 2)], "aK%d" % t, len(topo.engines(from_k, core)))
-        arrives([v(qb, 0, 32), v(sb, 96, 128)], "aB%d" % t, len(topo.engines(from_b, core)) + len(topo.engines(from_s, core)))
+        if first:
+            arrives([v("la", 0, 2)], "aB0", len(topo.engines(from_b, core)))
+            for b in range(4):
+                mm("p%d" % (4 + b), S_, v("qe", 128 * b, 128 * b + 128), v("se", 128 * b, 128 * b + 128), v(qb), v(sb))
+            for b in range(4):
+                act(part_of("f64", b, w, 0), v("p%d" % (4 + b), 0, 128))
+                act(part_of("f64", b, w, 1), v("p%d" % (4 + b), C_, S_))
+        else:
+            arrives([v(qb, 0, 32), v(sb, 96, 128)], "aB%d" % t, len(topo.engines(from_b, core)) + len(topo.engines(from_s, core)))
 
         scan(v("pre"), ones, v("nsr", 0, C_), 15.0, ALU.add, ALU.subtract)
+        if first:
+            constants_4()
         for c, o in enumerate((ALU.max, ALU.min)):
             scan(plane("jk", c, C_, C_), v("eq"), v("eq"), 0.0, o, o)
         d = rising("m5", v("pre"), C_)
@@ -459,56 +542,59 @@ def rank_program(g, core, T, topo):
             act(v("kp"), v("ks", 0, C_ + 1, by=v("qoff")))
         tt(v("hh", 0, 12), d, v("hh", 16, 28), ALU.max)
         if first:
+            order("G", touches([v("pl", 10, 12)], []))
+            cnt["lL"] += _send(g, T, topo, core, relay_b, T.la[:, 0:2], T.pl[:, 10:12], "aB0", "lL")
+            leaves([v("pl", 10, 12)], "lL")
             constants_3()
-        for b in range(4):
-            if b < 2:
-                ts(v("bt", 384 + b, 512, 4), plane("t64", b, w, by=v("pl", 10, 12)), 1.0 / 64, ALU.mult)
-            else:
-                act(v("bt", 384 + b, 512, 4), plane("t64", b, w, by=v("pl", 10, 12)), scale=1.0 / 64)
+        else:
+            for b in range(4):
+                if b < 2:
+                    ts(v("bt", 384 + b, 512, 4), plane("t64", b, w, by=v("pl", 10, 12)), 1.0 / 64, ALU.mult)
+                else:
+                    act(v("bt", 384 + b, 512, 4), plane("t64", b, w, by=v("pl", 10, 12)), scale=1.0 / 64)
         cp(v("doff"), v("hh", 0, 12))
-        quant(v(qb, 32, 160), v(sb, 128, 256), v("bt"))
-        order("G", touches([v(qb, 128, 160), v(sb, 128, 256)], []))
-        cnt["sent"] += _send_b(g, T, topo, core, relay_b, relay_s, T[qb][:, 128:160].bitcast(dt.uint8), T[sb][:, 128:256], t)
-        if t:
+        tt(v("km"), v("nb", by=v("roff")), v("ks", 0, C_), ALU.add)
+        if not first:
+            quant(v(qb, 32, 160), v(sb, 128, 256), v("bt"))
+            order("G", touches([v(qb, 128, 160), v(sb, 128, 256)], []))
+            cnt["sent"] += _send_b(g, T, topo, core, relay_b, relay_s, T[qb][:, 128:160].bitcast(dt.uint8), T[sb][:, 128:256], t)
             fill(v("aa"), 1)
         cp(v("pls", by=v("doff")), held)
-        tt(v("km"), v("nb", by=v("roff")), v("ks", 0, C_), ALU.add)
+        tt(v("m3", 0, 128), v("nsr", 0, C_ + 1, by=v("qoff", 0, 8)), v("wt"), ALU.mult)
         stay = v("pls", 16, 16 + K_)
         d = rising("m6", stay, K_)
-        tt(v("m3"), v("nsr", 0, C_ + 1, by=v("qoff")), v("wt"), ALU.mult)
-        if first:
-            constants_4()
-        if last:
-            quant(v("qv"), v("sv"), v("vt"))
-        cp(v("pl", 0, 10), d)
         unit = S_ / w
         at = (0, 3, ZS, ZS + 3)
-        for f in range(4):
+
+        def count(f):
             act(plane("jk", f, K_, C_), stay, AF.Sign, -unit, col("xs", f), acc=col("zz", at[f]))
 
         def stayers(b):
             act(plane("tc", b, K_, PW, ST), plane("t64", b, w, by=v("pl", 0, 10)), scale=1.0 / 64)
-        stayers(0)
-        stayers(1)
-        if last:
-            act(v("olw", ST), stay)
 
-        for c in range(2):
-            ts(v("ck", KW * c + 1, KW * c + 1 + C_), v("km"), col(ka, c), ALU.is_le)
+        ts(v("ck", 0, C_), v("km"), col(ka, 0), ALU.is_gt)
+        act(v("eq"), v("km"), AF.Sign, -1.0, col(ka, 1))
+        count(0)
+        act(v("eq"), v("eq"), AF.Relu, -1.0, acc=col("cn", C_ + 1))
+        for f in (1, 2, 3):
+            count(f)
+        cp(v("pl", 0, 10), d)
+        tt(v("m3", 128), v("nsr", 0, C_ + 1, by=v("qoff", 8, 16)), v("wt"), ALU.mult)
+        scan(v("cn", 0, C_ + 1), v("ck"), v("ck"), 0.0, ALU.add, ALU.max)
         scan(v("m4"), v("rm"), v("m3"), 0.0, ALU.mult, ALU.add)
+        if last:
+            quant(v("qv"), v("sv"), v("vt"))
+        ts(v("qo"), v("cn", C_, C_ + 2), -1.0, ALU.mult, col("xs", 5), ALU.add)
+        ts(v("noff"), v("cn", C_ - 1, C_ + 2, 2), -1.0, ALU.mult, C_ + 15.0, ALU.add)
         ts(col("sm", 0), col("zz", 3), col("zz", 0), ALU.subtract, 0.5, ALU.mult)
-        scan(v("cn"), v("rk2"), v("ck"), 0.0, ALU.mult, ALU.add)
         ts(v("tn"), v("m4", 15, S_, 16), I_, ALU.add)
-        ts(col("zz", ZS - 1), col("sm", 0), float(Q1), ALU.max, -float(GAP), ALU.mult)
-        cp(v("qo"), v("cn", C_ + 1, 2 * KW, KW))
-        cp(v("noff"), v("cn", C_, 2 * KW, KW))
         cp(v("aa", by=v("qo")), v("zr"))
         before = v("pls", 0, 16 + K_, by=v("noff"))
         for f in (0, 2):
             act(v("ju", 16 * f, 16 * f + 32), before, AF.Sign, -unit, col("xs", f), acc=col("zz", at[f] + 1))
             ts(v("zz", at[f + 1] + 1, at[f + 1] + 1 + L_), before, unit, ALU.mult, col("xs", f + 1), ALU.is_lt)
-        stayers(2)
-        stayers(3)
+            if f == 0:
+                ts(col("zz", ZS - 1), col("sm", 0), float(Q1), ALU.max, -float(GAP), ALU.mult)
         tt(v("idv"), v("ndm", by=v("qo")), v("iob", 0, L_), ALU.add)
         scan(v("tb"), ones, v("aa"), ST - 1.0, ALU.mult, ALU.add)
         scan(v("zo"), v("zm"), v("zz"), 0.0, ALU.mult, ALU.add)
@@ -519,11 +605,20 @@ def rank_program(g, core, T, topo):
         d = rising("m5", v("tb"), C_)
         tt(v("sm", 16, 32), v("lv", by=col("vo", 0)), v("mw"), ALU.add)
         for b in (0, 2, 1, 3):
-            mm("p%d" % b, 128, v("qe", 128 * b, 128 * b + 128), v("se", 128 * b, 128 * b + 128), v(qb, 0, 128), v(sb, 96, 224))
-        for b in (0, 2, 1, 3):
-            act(plane("tc", b, L_, PW), v("p%d" % b, 0, L_))
-            if b == 2:
-                act(v("gq"), v("tab", by=v("xo")))
+            if not first:
+                mm("p%d" % b, 128, v("qe", 128 * b, 128 * b + 128), v("se", 128 * b, 128 * b + 128), v(qb, 0, 128), v(sb, 96, 224))
+
+        def arrived(b):
+            act(plane("tc", b, L_, PW), plane("f64", b, w, by=v("la", 0, 2)) if first else v("p%d" % b, 0, L_))
+        stayers(0)
+        stayers(2)
+        stayers(1)
+        arrived(0)
+        arrived(2)
+        act(v("gq"), v("tab", by=v("xo")))
+        stayers(3)
+        arrived(1)
+        arrived(3)
         ts(col("sm", 1), col("zo", ZS - 2), col("sm", 0), ALU.is_gt, 16.0, ALU.mult)
         cp(v("to"), d)
         reduce(col("sm", 2), v("sm", 16, 32), ALU.max)
@@ -534,28 +629,28 @@ def rank_program(g, core, T, topo):
         def merged(b):
             (cp if b < 2 else act)(plane("mq", b, C_, MW), plane("tc", b, PW, PW, by=v("to")))
 
-        def placed(b):
-            (cp if b < 2 else act)(v("ft", b, 4 * S_, 4), plane("mq", b, C_ + 1, MW, by=v("qoff")))
         merged(0)
         ts(v("qoff"), v("cand", by=col("vo", 2)), float(C_), ALU.min)
         for b in (1, 2, 3):
             merged(b)
-        for b in range(4):
-            placed(b)
-        if not last:
-            tt(v("hh", 0, 16), v("cand", by=col("vo", 2)), v("kc"), ALU.min)
-            quant(v("qf"), v("sf"), v("ft"))
-            cp(v("uq"), v("hh", 0, 16))
+        if last:
+            gather_state("mq", MW, C_ + 1, "qoff", S_, [nothing] * 3)
+        else:
+            gather_state("mq", MW, C_ + 1, "qoff", S_, [lambda: tt(v("hh", 0, 16), v("cand", by=col("vo", 2)), v("kc"), ALU.min),
+                                                        lambda: cp(v("uq"), v("hh", 0, 16)), lambda: in_order(0, PR1)])
 
+    act(v("olw", ST), v("pls", 16, 16 + K_))
     act(v("ks", 0, C_), v("olw", by=v("to")))
-    for h, bank in enumerate(("pp", "pq")):
-        quant(v("qf", 128 * h, 128 * h + 128), v("sf", 128 * h, 128 * h + 128), v("ft", 512 * h, 512 * h + 512))
-        mm(bank, 128, v("qv"), v("sv"), v("qf", 128 * h, 128 * h + 128), v("sf", 128 * h, 128 * h + 128))
-    dma("Y", [v("qf")], [], T.oc[:], T.qf[:].bitcast(dt.uint8))
-    act(v("psb", 0, 128), v("pp", 0, 128))
+    for h in range(2):
+        mm_half("p%d" % (4 + h), v("qv"), v("sv"), "qf", "sf", h)
+        codes = v("qf", 128 * h, 128 * h + 128, cast=dt.uint8)
+        dma("Y", [codes], [], T.oc[:, 512 * h:512 * h + 512], codes[0])
+    act(v("psb", 0, 128), v("p4", 0, 128))
+    cp(v("psb", 128, 256), v("p5", 0, 128))
     cp(v("kp"), v("ks", 0, C_ + 1, by=v("qoff")))
-    cp(v("psb", 128, 256), v("pq", 0, 128))
-    dma("S", [v("psb")], [], T.y[:], T.psb[:])
+    for h in range(2):
+        half = v("psb", 128 * h, 128 * h + 128)
+        dma("S", [half], [], T.y[:, 128 * h:128 * h + 128], half[0])
     for k in range(4):
         dma("Y", [v("sf")], [], T.osc[4 * k:4 * k + 4, :], T.sf[32 * k:32 * k + 4, :])
     dma("Y", [v("kp")], [], T.ol[:], T.kp[0:128:16, :])

from concourse.bass import DstId, RemoteDMATransfer
from concourse.mybir import dt, AluOpType, AxisListType, ActivationFunctionType

ALU, AF, AX = AluOpType, ActivationFunctionType, AxisListType
S_, C_, L_, R_ = 256, 192, 32, 3
Q1, Q2 = 14, 52
K_ = C_ - L_
NV = 7
NS = 12 - NV
CW = C_ + 1
ST = 64
PW = ST + K_
MW = 208
PR1 = 10
GAP = 512
B64, IO, TABW = 16, 224, 424
ZS = L_ + 6
ZW = 2 * ZS - 1
CX, U8, BF, F32, I32, U16 = "float8_e4m3fn_x4", "uint8", "bfloat16", "float32", "int32", "uint16"


def _sb(n, d):
    return ("sbuf", [128, n], d)


SCRATCH = {
    "xt": _sb(768, BF), "ut": _sb(512, BF), "vt": _sb(512, BF), "et": _sb(528, BF),
    "qu": _sb(128, CX), "su": _sb(128, U8), "qur": _sb(128, CX), "sur": _sb(128, U8),
    "qv": _sb(128, CX), "sv": _sb(128, U8), "qw": _sb(512, CX), "sw": _sb(512, U8), "qe": _sb(512, CX), "se": _sb(512, U8),
    "qf": _sb(256, CX), "sf": _sb(256, U8), "qt": _sb(256, CX), "st": _sb(256, U8),
    "ft": _sb(1024, BF), "f64": _sb(1024, BF), "tt": _sb(1024, BF), "t64": _sb(1024, BF), "tc": _sb(4 * PW, BF), "bt": _sb(512, BF),
    "pi": _sb(8, I32), "ic": _sb(4, F32), "iu": _sb(24, I32), "cu": _sb(24, U16), "aoff": _sb(2, U16),
    "ioj": _sb(256, BF), "iob": _sb(256, BF), "iof": _sb(64, F32), "dc": _sb(24, F32),
    "dm": _sb(256, BF), "rm": _sb(256, BF), "gt": _sb(192, BF), "bm": _sb(192, BF), "wt": _sb(128, BF), "rs": _sb(4 * CW, BF),
    "eqt": _sb(208, BF), "eqs": _sb(192, BF), "nst": _sb(192, BF), "yc": _sb(12, F32), "kc": _sb(16, F32), "zr": _sb(32, BF),
    "lv": _sb(112, BF), "mw": _sb(16, F32), "tab": _sb(TABW, F32), "yy": _sb(384, F32), "yr": _sb(384, F32), "xs": _sb(8, F32),
    "la": _sb(8, U16), "zm": _sb(ZW, F32), "zz": _sb(ZW, F32), "zo": _sb(ZW, F32),
    "psb": _sb(256, F32), "pc": _sb(192, F32), "msk": _sb(192, F32), "sc": _sb(192, F32), "eq": _sb(192, BF), "cor": _sb(192, BF),
    "cmp": _sb(CW * 12, BF), "cs": _sb(CW * NV, BF), "gl": _sb(24, F32), "roff": _sb(12, U16), "k0": _sb(192, F32), "k1": _sb(192, F32),
    "nsr": _sb(MW, BF), "pre": _sb(192, BF), "hh": _sb(32, F32), "doff": _sb(12, U16), "jk": _sb(4 * 192, BF),
    "pr": _sb(C_ + S_, BF), "pls": _sb((K_ + 16) * L_ + 16, BF), "m3": _sb(256, BF), "m4": _sb(256, BF),
    "m5": _sb(192, BF), "m6": _sb(160, BF), "pl": _sb(12, U16), "poff": _sb(12, U16), "mq": _sb(4 * MW, BF), "nb": _sb(192, BF), "ndm": _sb(192, BF),
    "kw": _sb(PW, F32), "ks": _sb(MW, F32), "km": _sb(192, F32), "kp": _sb(256, F32), "ck": _sb(C_ + 1, BF), "cn": _sb(C_ + 2, F32), "noff": _sb(2, U16), "qo": _sb(2, U16),
    "aa": _sb(192, BF), "tb": _sb(192, BF), "idv": _sb(32, BF), "ju": _sb(64, BF), "sm": _sb(32, F32), "tn": _sb(16, F32),
    "xo": _sb(4, U16), "vo": _sb(4, U16), "gq": _sb(64, F32), "cand": _sb(96, F32), "qoff": _sb(16, U16), "to": _sb(12, U16),
    "uq": _sb(16, U16), "ax": _sb(64, F32), "ay": _sb(64, F32), "olw": _sb(PW, F32),
}
for _t in range(8):
    SCRATCH["p%d" % _t] = ("psum", [128, 512], F32)
for _t in range(R_):
    SCRATCH["ko%d" % _t] = _sb(8, F32)
    SCRATCH["ka%d" % _t] = _sb(8, F32)
    SCRATCH["qb%d" % _t] = _sb(160 if _t else 256, CX)
    SCRATCH["sb%d" % _t] = _sb(256, U8)
SEMAPHORES = ["cV", "cS", "cP", "cG", "sent", "aT", "lT", "lL"] + ["d%d" % _t for _t in range(14)] + ["aK%d" % _t for _t in range(R_)] + ["aB%d" % _t for _t in range(R_)]


def _bits(es):
    return sum(1 << e for e in es)


def _relays(src, dst, topo):
    c = [k for k in topo.cores_of(src) if k != src and topo.may_write(k, dst)]
    c.sort(key=lambda k: topo.die(k) != topo.die(src))
    return c[0], c[1], c[2]


def _send(g, T, topo, src, dst, out, in_, sem, left="sent"):
    rid, pid = topo.addr(dst, src)
    es = topo.engines(src, dst)
    g.remote_dma(out, in_, T.sem[sem], T.sem[left], pid, rid, _bits(es))
    return len(es)


def _send_b(g, T, topo, src, dst, dst2, codes, scales, t):
    es = [e for e in topo.engines(src, dst) if e in topo.engines(src, dst2)]
    h = len(es) // 2
    d, d2 = [[DstId(rid=a[0], pnc=a[1])] for a in (topo.addr(dst, src), topo.addr(dst2, src))]
    g.remote_dma_fused([
        RemoteDMATransfer(dst_ids=d, dma_engine_mask=_bits(es[:h]), remote_sem=T.sem["aB%d" % t], src=codes, dst=T["qb%d" % t][:, 0:32].bitcast(dt.uint8)),
        RemoteDMATransfer(dst_ids=d2, dma_engine_mask=_bits(es[h:]), remote_sem=T.sem["aB%d" % t], src=scales, dst=T["sb%d" % t][:, 0:128]),
    ], local_sem=T.sem.sent)
    return 2 * h


def _hand_on(g, core, T, topo):
    cores = list(T.cores)
    for r in range(len(cores)):
        src, dst = cores[r], cores[(r + 1) % len(cores)]
        rk, rb, rs = _relays(src, dst, topo)
        sent = 0
        if core in (rk, rb, rs):
            ap = T.sb0[:] if core == rs else T.qb0[:, 128 * (core == rb):128 * (core == rb) + 128].bitcast(dt.uint8)
            g.wait_ge(T.sem.aT, len(topo.engines(src, core)))
            sent += _send(g, T, topo, core, dst, ap, ap, "aT")
        for t in range(R_):
            if core == rk:
                g.wait_ge(T.sem["aK%d" % t], len(topo.engines(src, core)))
                sent += _send(g, T, topo, core, dst, T["ka%d" % t][:, 0:2], T["ka%d" % t][:, 0:2], "aK%d" % t)
            if core == rb and t == 0:
                g.wait_ge(T.sem.aB0, len(topo.engines(src, core)))
                sent += _send(g, T, topo, core, dst, T.la[:, 0:2], T.la[:, 0:2], "aB0")
            if core in (rb, rs) and t > 0:
                ap = T["qb%d" % t][:, 0:32].bitcast(dt.uint8) if core == rb else T["sb%d" % t][:, 96:128]
                g.wait_ge(T.sem["aB%d" % t], len(topo.engines(src, core)) // 2)
                sent += _send(g, T, topo, core, dst, ap, ap, "aB%d" % t)
        if sent:
            g.wait_ge(T.sem.sent, sent)


def rank_program(g, core, T, topo):
    cores = list(T.cores)
    n = len(cores)
    rank = T.rank_of(core)
    if rank is None:
        return _hand_on(g, core, T, topo)
    relay_k, relay_b, relay_s = _relays(core, cores[(rank + 1) % n], topo)
    from_k, from_b, from_s = _relays(cores[(rank - 1) % n], core, topo)

    def v(name, a=0, b=None, s=1, by=None, cast=None):
        b = SCRATCH[name][1][1] if b is None else b
        ap = T[name][:, a:b:s]
        if cast is not None:
            ap = ap.bitcast(cast)
        use = [(name, _bits(range(a, b, s)))]
        if by is not None:
            ap, use = ap.indirect(by[0]), use + by[1]
        return ap, use

    def col(name, k):
        return v(name, k, k + 1)

    Q = {"V": g.vector, "S": g.scalar, "P": g.tensor, "G": g, "Y": g.sync}
    cnt = {"cV": 0, "cS": 0, "cP": 0, "cG": 0, "sent": 0, "lT": 0, "lL": 0}
    clock = {q: {} for q in Q}
    snap, seen = {}, {}
    ndma = [0]

    def touches(rd, wr):
        out = []
        for views, w in ((rd, False), (wr, True)):
            for x in views:
                if isinstance(x, tuple):
                    for k, (name, bits) in enumerate(x[1]):
                        out.append((name, 1, w or "bank") if SCRATCH[name][0] == "psum" else (name, bits, w and k == 0))
        return out

    def order(q, use):
        ev = {}
        for name, bits, w in use:
            for e, b2, w2 in seen.get(name, []):
                if bits & b2 and (w or w2) and clock[q].get(e[0], 0) < e[1] and not (w == w2 == "bank" and e[0] == "c" + q):
                    ev[e] = 1
        for e in ev:
            if not any(o != e and snap[o].get(e[0], 0) >= e[1] for o in ev):
                Q[q].wait_ge(T.sem[e[0]], e[1])
                for s, k in snap[e].items():
                    clock[q][s] = max(clock[q].get(s, 0), k)

    def done(q, e, use):
        snap[e] = dict(clock[q])
        snap[e][e[0]] = e[1]
        for name, bits, w in use:
            if w is True:
                seen[name] = [o for o in seen.get(name, []) if o[1] & ~bits]
        for name, bits, w in use:
            seen.setdefault(name, []).append((e, bits, w))

    def op(q, rd, wr, fn):
        use = touches(rd, wr)
        order(q, use)
        s = "c" + q
        cnt[s] += 1
        fn().then_inc(T.sem[s], 1)
        done(q, (s, cnt[s]), use)

    def dma(q, rd, wr, out, in_):
        use = touches(rd, wr)
        order(q, use)
        s = "d%d" % ndma[0]
        ndma[0] += 1
        cnt[s] = 16
        Q[q].dma_start(out, in_).then_inc(T.sem[s], 16)
        done(q, (s, 16), use)

    def arrives(views, sem, val):
        snap[(sem, val)] = {sem: val}
        for name, bits, w in touches([], views):
            seen.setdefault(name, []).append(((sem, val), bits, True))

    def leaves(views, sem):
        snap[(sem, cnt[sem])] = {sem: cnt[sem]}
        for name, bits, w in touches(views, []):
            seen[name].append(((sem, cnt[sem]), bits, False))

    V, A = g.vector, g.scalar

    def x(a):
        return a[0] if isinstance(a, tuple) else a

    def ts(out, a, s1, o0, s2=None, o1=None):
        if o1 is None:
            op("V", [a, s1], [out], lambda: V.tensor_scalar(out[0], a[0], x(s1), None, o0))
        else:
            op("V", [a, s1, s2], [out], lambda: V.tensor_scalar(out[0], a[0], x(s1), x(s2), o0, o1))

    def tt(out, a, b, o):
        op("V", [a, b], [out], lambda: V.tensor_tensor(out[0], a[0], b[0], o))

    def cp(out, a):
        op("V", [a], [out], lambda: V.tensor_copy(out[0], a[0]))

    def ms(out, c):
        op("V", [], [out], lambda: V.memset(out[0], c))

    def scan(out, a, b, init, o0, o1):
        op("V", [a, b, init], [out], lambda: V.tensor_tensor_scan(out[0], a[0], b[0], x(init), o0, o1))

    def reduce(out, a, o):
        op("V", [a], [out], lambda: V.tensor_reduce(out[0], a[0], AX.X, o))

    def act(out, a, f=AF.Copy, scale=None, bias=None, acc=None):
        kw = {k: x(p) for k, p in (("scale", scale), ("bias", bias), ("accum_out", acc)) if p is not None}
        op("S", [a, scale, bias], [out, acc], lambda: A.activation(out[0], a[0], f, **kw))

    def quant(q, s, a):
        op("V", [a], [q, s], lambda: V.quantize_mx(q[0], s[0], a[0]))

    def mm(bank, w, lq, ls, rq, rs):
        op("P", [lq, ls, rq, rs], [v(bank)], lambda: g.tensor.matmul_mx(v(bank, 0, w)[0], lq[0], ls[0], rq[0], rs[0], True, True))

    def iota(out, pat, base=0, cm=0):
        if SCRATCH[out[1][0][0]][2] == I32:
            op("G", [], [out], lambda: g.iota(out[0], pat, base, cm))
        else:
            op("G", [], [out], lambda: g.iota(out[0], pat, base, cm, allow_small_or_imprecise_dtypes=True))

    def fill(out, c):
        iota(out, [[0, bin(out[1][0][1]).count("1")]], c)

    def plane(name, b, w, stride=S_, at=0, by=None):
        return v(name, stride * b + at, stride * b + at + w, by=by)

    I_, I12, I3, I16 = [col("ic", k) for k in range(4)]
    ones = v("rs", 1, CW)
    offu, bco, axo = v("cu", 0, 8), v("cu", 8, 20), v("cu", 20, 24)

    dma("Y", [], [v("ut")], T.ut[:], T.u[:])
    dma("S", [], [v("xt")], T.xt[:], T.x[:])
    dma("Y", [v("xt")], [v("qw")], T.qw[:].bitcast(dt.uint8), T.wc[:])
    dma("Y", [], [v("sw")], T.sw[:], T.ws[:])
    dma("Y", [], [v("vt")], T.vt[:], T.v[:])

    iota(col("pi", 0), [[0, 1]], 0, 1)
    iota(v("iu", 0, 8), [[16, 8]])
    iota(v("iof"), [[1, 64]])
    iota(v("dc", 16), [[16, 4], [1, 2]])
    iota(v("ioj"), [[0, 16], [1, 16]])
    iota(v("iu", 8, 20), [[16, 12]], 15)
    iota(v("iu", 20, 24), [[1, 2], [0, 2]])
    fill(v("yc", 0, NV), -1)
    iota(v("yc", NV), [[16, NS]], 16 * NV + 15)
    ms(v("et"), 1.0)
    op("G", [v("et")], [v("et")], lambda: g.affine_select(T.et[:], T.et[:], [[-1, 528]], ALU.is_equal, 0.0, 3, 4))
    iota(v("iob"), [[1, 256]])
    iota(v("mw"), [[4, 4], [0, 4]])
    iota(v("kc"), [[16, 16]], C_)
    for view, c in [(v("eqt", 0, 16), 0), (v("eqt", 32), 0), (v("eqs", 32), 0), (v("nst", 0, L_), 1), (v("nst", L_), 0), (col("nsr", C_), 1),
                    (v("pls", 0, 16), 0), (v("bt", 0, 384), 0), (col("ck", C_), 16),
                    (v("zo"), 2), (v("zo", 0, ZW, ZS), 0), (v("zo", 2, ZW, ZS), 1), (v("zo", 3, ZW, ZS), -4), (v("zo", 4, ZW, ZS), 1),
                    (col("zo", ZS - 1), 2 * GAP), (v("zz", 2, ZW, ZS), C_ // 2 + IO), (col("zz", ZS - 2), K_ // 2 + IO),
                    (v("aa"), 1), (v("zr"), 0), (v("lv", 0, 2), -100), (v("lv", 2, Q2 + 3), 0), (v("lv", Q2 + 3), 48),
                    (v("tab", 176, IO), 0), (v("cand", 64, 80), 0), (v("mq", C_, 4 * MW, MW), 0), (col("ks", C_), -1), (v("kw", L_, ST), 0)]:
        fill(view, c)
    iota(v("tab", IO), [[1, TABW - IO]])
    iota(v("olw", 0, ST), [[1, ST]], S_)

    ms(v("rs"), 1.0)
    for k, m in enumerate((15, 12, 3, 16)):
        ts(col("pi", 4 + k), col("pi", 0), m, ALU.bitwise_and)
    ms(v("rs", 0, 4 * CW, CW), 0.0)
    cp(v("ic"), v("pi", 4, 8))
    cp(offu, v("iu", 0, 8))
    ts(v("dc", 0, 8), v("dc", 16), I_, ALU.add, 1.0 / 64, ALU.mult)
    ts(v("dc", 8, 10), v("dc", 16, 18), I_, ALU.add, 1.0 / 16, ALU.mult)
    ts(v("dm"), v("ioj"), I_, ALU.is_equal)
    quant(v("qu"), v("su"), v("ut"))
    ts(v("rm"), v("ioj"), 1.0, ALU.min)
    ts(v("gt"), v("ioj", 0, C_), I_, ALU.is_gt)
    ts(v("bm"), v("ioj", 0, C_), I_, ALU.is_le, 512.0, ALU.mult)
    cp(v("qur", cast=dt.uint32), v("qu", cast=dt.uint32, by=offu))
    act(v("sur"), v("su", by=offu))
    quant(v("qt", 0, C_), v("st", 0, C_), v("xt"))
    ts(v("ndm"), v("ioj", 0, C_), I_, ALU.not_equal, 255.0, ALU.mult)
    cp(v("cu", 8, 24), v("iu", 8, 24))
    ts(v("m3", 0, 16), v("ioj", 0, 16), I_, ALU.is_lt)
    ts(v("m3", 16, 32), v("dm", 0, 16), float(GAP), ALU.mult)
    cp(v("eqt", 16, 32), v("dm", 0, 16))
    cp(v("eqs", 0, 16), v("dm", 0, 16))
    ts(v("eqs", 16, 32), v("dm", 0, 16), -1.0, ALU.mult)
    tt(v("wt", 0, 16), v("m3", 16, 32), v("m3", 0, 16), ALU.subtract)

    HALF, BIG = 0.4921875, 12582912.0
    for h in range(2):
        act(col("dc", 10 + h), I_, AF.Identity, 0.75, HALF + 0.75 * h)
    for h in range(2):
        act(v("yy", 192 * h, 192 * h + 16), v("iof", 0, 16), AF.Identity, col("dc", 8 + h), HALF)
        for lp in range(4):
            a = 192 * h + 16 + 40 * lp
            act(v("yy", a, a + 40), v("iof", Q1, Q1 + 40), AF.Identity, col("dc", 2 * lp + h), HALF)
        act(v("yy", 192 * h + 176, 192 * h + 192), v("iof", 0, 16), AF.Identity, 12.0, col("dc", 10 + h))
    for bank in ("p4", "p5"):
        mm(bank, C_, v("qur"), v("sur"), v("qt", 0, C_), v("st", 0, C_))

    def constants_s():
        act(v("yr"), v("yy"), AF.Identity, 1.0, BIG)
        for k in range(3):
            act(v("wt", 16 << k, 32 << k), v("wt", 0, 16 << k))
        for k, c, b in ((0, I_, 0), (1, I_, 16), (2, I12, 0), (3, I12, 64)):
            act(col("xs", k), c, AF.Identity, 16.0, b - 0.5)
        act(col("xs", 4), I3, AF.Identity, 40.0)
        act(col("xs", 5), I_, AF.Identity, 1.0, C_ + 16.0)
        act(col("zz", ZW - 1), I3, AF.Identity, 40.0, float(K_ // 2 + IO + B64 - Q1))

    def constants_1():
        ts(v("yy", 0, 192), v("yr", 0, 192), BIG, ALU.subtract, GAP + 1.0, ALU.mult)
        ts(v("yy", 192, 384), v("yr", 192, 384), BIG + 1, ALU.subtract, float(GAP), ALU.mult)

    def constants_2():
        tt(v("tab", 0, 176), v("yy", 0, 176), v("yy", 192, 368), ALU.subtract)
        tt(v("cand", 48, 64), v("yy", 176, 192), v("yy", 368, 384), ALU.subtract)

    def constants_3():
        ts(v("qoff"), v("cand", 48, 64), float(C_), ALU.min)
        ts(v("nb"), v("nst"), 1e29, ALU.mult)

    def constants_4():
        cp(v("cand", 80, 96), v("cand", 48, 64))
        ts(v("zm"), v("zo"), 0.5, ALU.mult)

    def constants_5():
        ts(v("mw"), v("mw"), I12, ALU.is_equal, 32.0, ALU.mult)
        ts(v("aoff"), v("iof", 0, 64, 32), I_, ALU.add, I16, ALU.add)
        ts(v("kc"), v("kc"), I_, ALU.add)

    def quant_e(b):
        quant(v("qe", 128 * b, 128 * b + 128), v("se", 128 * b, 128 * b + 128), v("et", 3 - b, 515 - b))

    def own(a, b):
        scan(v("sc", a, b), v("rm", 0, b - a), v("msk", a, b), 0.0, ALU.mult, ALU.add)

    def ranks(late, equal):
        def s(c):
            return col("sc", 16 * c + 15)

        def part(c, a, b):
            return v("cmp", CW * c + a, CW * c + b)

        def compare(c):
            e = 16 * c + 16
            ts(part(c, 0, e), v("pc", 0, e), s(c), ALU.is_le)
            ts(part(c, e, C_), v("pc", e, C_), s(c), ALU.is_lt)
        late()
        for c in reversed(range(NV, 12)):
            act(part(c, 0, C_), v("pc"), AF.Sign, -1.0, s(c))
        compare(0)
        equal()
        compare(1)
        compare(2)
        scan(v("cor"), v("eq"), v("gt"), 0.0, ALU.add, ALU.mult)
        compare(3)
        compare(4)
        tt(v("cmp", C_, 12 * CW, CW), v("yc"), v("cor", 15, C_, 16), ALU.subtract)
        for c in range(5, NV):
            compare(c)
        for c in reversed(range(NV, 12)):
            act(part(c, 0, 16 * c + 16), part(c, 0, 16 * c + 16), AF.Relu, -1.0, acc=col("gl", c - NV))
        for c in range(NV, 11):
            act(part(c, 16 * c + 16, CW), part(c, 16 * c + 16, CW), AF.Relu, acc=col("gl", 8 + c - NV))
        for a, b in ((0, 4), (4, NV)):
            scan(v("cs", CW * a, CW * b), v("rs", 0, CW * (b - a)), v("cmp", CW * a, CW * b), 0.0, ALU.mult, ALU.add)
        ts(col("roff", 11), part(11, C_, CW), col("gl", NS - 1), ALU.subtract)
        for k in range(NS - 1):
            ts(col("roff", NV + k), col("gl", 8 + k), col("gl", k), ALU.subtract)
        cp(v("roff", 0, NV), v("cs", C_, CW * NV, CW))

    def rising(buf, a, w):
        scan(v(buf, 0, w), v("bm", 0, w), a, 0.0, ALU.add, ALU.min)
        return v(buf, 15, w, 16)

    def span(w, h):
        return (0, 128) if h == 0 else (128, w)

    def quant_half(q, s, tile, w, h):
        a = h * (w - 128)
        quant(v(q, 128 * h, 128 * h + 128), v(s, 128 * h, 128 * h + 128), v(tile, 4 * a, 4 * a + 512))

    def mm_half(bank, lq, ls, q, s, h):
        mm(bank, 128, lq, ls, v(q, 128 * h, 128 * h + 128), v(s, 128 * h, 128 * h + 128))

    def result(bank, w, h):
        return v(bank, h * (S_ - w), 128)

    def cols(tile, b, w, h):
        return v(tile, 4 * span(w, h)[0] + b, 4 * span(w, h)[1], 4)

    def part_of(name, b, w, h):
        return v(name, S_ * b + span(w, h)[0], S_ * b + span(w, h)[1])

    def gather_state(src, stride, width, by, w, pause):
        for h in range(2):
            a, b_ = span(w, h)
            for b in range(4):
                (cp if b < 2 else act)(cols("ft", b, w, h), plane(src, b, width, stride, by=v(by, a // 16, b_ // 16)))
                if b == 0:
                    pause[h]()
        quant_half("qf", "sf", "ft", w, 0)
        pause[2]()
        quant_half("qf", "sf", "ft", w, 1)

    def nothing():
        pass

    for a in (0, 96):
        tt(v("msk", a, a + 96), v("p4", a, a + 96), v("dm", 0, 96), ALU.mult)
    act(v("pc"), v("p5", 0, C_))
    own(0, 96)
    ranks(lambda: own(96, C_), lambda: tt(v("eq"), v("sc"), v("p4", 0, C_), ALU.is_equal))
    tt(v("eq"), v("ndm", by=v("roff")), v("iob", 0, C_), ALU.add)
    for b in range(4):
        act(plane("tc", b, C_, PW), v("xt", b, 768, 4))
    quant_e(0)
    quant_e(1)
    cp(v("tb", by=v("roff")), v("eq"))
    constants_s()
    quant_e(2)
    quant_e(3)
    cp(v("to"), rising("m5", v("tb"), C_))
    gather_state("tc", PW, C_, "to", C_, [nothing] * 3)

    def in_order(a, b):
        cp(v("pr", by=v("uq", a, b)), v("iob", 16 * a, 16 * b))

    for t in range(R_):
        first, last = t == 0, t == R_ - 1
        w = C_ if first else S_
        ko, ka, qb, sb = ["%s%d" % (k, t) for k in ("ko", "ka", "qb", "sb")]
        held = v("iob", 0, C_) if first else v("pr", 0, C_)
        for h in range(2):
            for b in range(4):
                mm_half("p%d" % (4 * h + b), v("qw", 128 * b, 128 * b + 128), v("sw", 128 * b, 128 * b + 128), "qf", "sf", h)
            act(v("f64", 512 * h, 4 * span(w, h)[1]), v("ft", 512 * h, 4 * span(w, h)[1]), scale=64.0)
        if first:
            constants_1()
        else:
            act(v("ax"), v("ka%d" % (t - 1), 0, 2, by=axo))
        for h in range(2):
            for b in range(4):
                tt(part_of("t64", b, w, h), result("p%d" % (4 * h + b), w, h), cols("f64", b, w, h), ALU.add)
                if 4 * h + b < 6:
                    act(cols("tt", b, w, h), part_of("t64", b, w, h), scale=1.0 / 64)
        if not first:
            op("V", [v("ax")], [v("ay")], lambda: V.transpose(T.ay[:], T.ax[:]))
            in_order(PR1, 16)
            act(v("kw", ST), v("ks" if t == 1 else "kp", 0, C_ if t == 1 else S_, by=v("pl", 0, 10)))
        for b in (2, 3):
            ts(cols("tt", b, w, 1), part_of("t64", b, w, 1), 1.0 / 64, ALU.mult)
        quant_half("qt", "st", "tt", w, 0)
        for bank in ("p0", "p1") if first else ("p0",):
            mm_half(bank, v("qur"), v("sur"), "qt", "st", 0)
        if first:
            act(v("ks", 0, C_), v("pc", by=v("to")))
        else:
            act(v("kw", 0, L_), v("ay", by=v("aoff")))
            act(v("ks", 0, C_), v("kw", by=v("to")))
            d = rising("m5", held, C_)
        quant_half("qt", "st", "tt", w, 1)
        if first:
            constants_2()
        else:
            cp(v("poff"), d)
        for bank in ("p2", "p3") if first else ("p2",):
            mm_half(bank, v("qur"), v("sur"), "qt", "st", 1)
        if first:
            for relay, src, dst in ((relay_k, v("qt", 0, 128, cast=dt.uint8), v(qb, 0, 128, cast=dt.uint8)),
                                    (relay_b, v("qt", 128, 256, cast=dt.uint8), v(qb, 128, 256, cast=dt.uint8)), (relay_s, v("st"), v(sb))):
                order("G", touches([src], []))
                cnt["lT"] += _send(g, T, topo, core, relay, dst[0], src[0], "aT", "lT")
            leaves([v("qt"), v("st")], "lT")
            arrives([v(qb), v(sb)], "aT", sum(len(topo.engines(k, core)) for k in (from_k, from_b, from_s)))
            tt(v("msk", 0, 128), v("p0", 0, 128), v("dm", 0, 128), ALU.mult)
            act(v("pc", 0, 128), v("p1", 0, 128))
            tt(v("msk", 128), result("p2", w, 1), v("dm", 0, 64), ALU.mult)
            act(v("pc", 128), result("p3", w, 1))
            own(0, 128)

            def equal():
                tt(v("eq", 0, 128), v("sc", 0, 128), v("p0", 0, 128), ALU.is_equal)
                tt(v("eq", 128), v("sc", 128), result("p2", w, 1), ALU.is_equal)
            own(128, C_)
            ranks(constants_5, equal)
        else:
            act(v("psb", 0, 128), v("p0", 0, 128))
            cp(v("psb", 128), v("p2", 0, 128))
            act(v("pc", 0, 64), v("psb", 0, 128, by=v("poff", 0, 4)))
            tt(v("msk", 0, 64), v("psb", 0, 128, by=v("poff", 0, 4)), v("dm", 0, 64), ALU.mult)
            for c in (8, 4):
                tt(v("msk", 16 * c, 16 * c + 64), v("psb", by=v("poff", c, c + 4)), v("dm", 0, 64), ALU.mult)
            act(v("pc", 64), v("psb", by=v("poff", 4, 12)))
            own(0, 64)
            own(128, C_)
            ranks(lambda: own(64, 128), lambda: tt(v("eq"), v("sc", by=bco), v("pc"), ALU.is_equal))
        act(v("nsr", 0, C_), v("nst", by=v("roff")))
        tt(v("k0"), v("eqt", 16, 208, by=v("roff")), v("pc"), ALU.mult)
        tt(v("k1"), v("eqt", 0, 192, by=v("roff")), v("pc"), ALU.mult)
        act(v("k0"), v("k0"), AF.Identity, acc=col(ko, 0))
        tt(v("eq"), v("eqs", by=v("roff")), held, ALU.mult)
        act(v("k1"), v("k1"), AF.Identity, acc=col(ko, 1))
        order("G", touches([v(ko, 0, 2)], []))
        cnt["sent"] += _send(g, T, topo, core, relay_k, T[ka][:, 0:2], T[ko][:, 0:2], "aK%d" % t)
        arrives([v(ka, 0, 2)], "aK%d" % t, len(topo.engines(from_k, core)))
        if first:
            arrives([v("la", 0, 2)], "aB0", len(topo.engines(from_b, core)))
            for b in range(4):
                mm("p%d" % (4 + b), S_, v("qe", 128 * b, 128 * b + 128), v("se", 128 * b, 128 * b + 128), v(qb), v(sb))
            for b in range(4):
                act(part_of("f64", b, w, 0), v("p%d" % (4 + b), 0, 128))
                act(part_of("f64", b, w, 1), v("p%d" % (4 + b), C_, S_))
        else:
            arrives([v(qb, 0, 32), v(sb, 96, 128)], "aB%d" % t, len(topo.engines(from_b, core)) + len(topo.engines(from_s, core)))

        scan(v("pre"), ones, v("nsr", 0, C_), 15.0, ALU.add, ALU.subtract)
        if first:
            constants_4()
        for c, o in enumerate((ALU.max, ALU.min)):
            scan(plane("jk", c, C_, C_), v("eq"), v("eq"), 0.0, o, o)
        d = rising("m5", v("pre"), C_)
        ts(v("hh", 16, 28), v("roff"), -float(K_ + 16), ALU.mult, float((K_ + 16) * L_), ALU.add)
        for c in range(2):
            ts(col("pl", 10 + c), col("jk", C_ * c + C_ - 1), 1.0 - 2 * c, ALU.mult)
        if not first and not last:
            act(v("kp"), v("ks", 0, C_ + 1, by=v("qoff")))
        tt(v("hh", 0, 12), d, v("hh", 16, 28), ALU.max)
        if first:
            order("G", touches([v("pl", 10, 12)], []))
            cnt["lL"] += _send(g, T, topo, core, relay_b, T.la[:, 0:2], T.pl[:, 10:12], "aB0", "lL")
            leaves([v("pl", 10, 12)], "lL")
            constants_3()
        else:
            for b in range(4):
                if b < 2:
                    ts(v("bt", 384 + b, 512, 4), plane("t64", b, w, by=v("pl", 10, 12)), 1.0 / 64, ALU.mult)
                else:
                    act(v("bt", 384 + b, 512, 4), plane("t64", b, w, by=v("pl", 10, 12)), scale=1.0 / 64)
        cp(v("doff"), v("hh", 0, 12))
        tt(v("km"), v("nb", by=v("roff")), v("ks", 0, C_), ALU.add)
        if not first:
            quant(v(qb, 32, 160), v(sb, 128, 256), v("bt"))
            order("G", touches([v(qb, 128, 160), v(sb, 128, 256)], []))
            cnt["sent"] += _send_b(g, T, topo, core, relay_b, relay_s, T[qb][:, 128:160].bitcast(dt.uint8), T[sb][:, 128:256], t)
            fill(v("aa"), 1)
        cp(v("pls", by=v("doff")), held)
        tt(v("m3", 0, 128), v("nsr", 0, C_ + 1, by=v("qoff", 0, 8)), v("wt"), ALU.mult)
        stay = v("pls", 16, 16 + K_)
        d = rising("m6", stay, K_)
        unit = S_ / w
        at = (0, 3, ZS, ZS + 3)

        def count(f):
            act(plane("jk", f, K_, C_), stay, AF.Sign, -unit, col("xs", f), acc=col("zz", at[f]))

        def stayers(b):
            act(plane("tc", b, K_, PW, ST), plane("t64", b, w, by=v("pl", 0, 10)), scale=1.0 / 64)

        ts(v("ck", 0, C_), v("km"), col(ka, 0), ALU.is_gt)
        act(v("eq"), v("km"), AF.Sign, -1.0, col(ka, 1))
        count(0)
        act(v("eq"), v("eq"), AF.Relu, -1.0, acc=col("cn", C_ + 1))
        for f in (1, 2, 3):
            count(f)
        cp(v("pl", 0, 10), d)
        tt(v("m3", 128), v("nsr", 0, C_ + 1, by=v("qoff", 8, 16)), v("wt"), ALU.mult)
        scan(v("cn", 0, C_ + 1), v("ck"), v("ck"), 0.0, ALU.add, ALU.max)
        scan(v("m4"), v("rm"), v("m3"), 0.0, ALU.mult, ALU.add)
        if last:
            quant(v("qv"), v("sv"), v("vt"))
        ts(v("qo"), v("cn", C_, C_ + 2), -1.0, ALU.mult, col("xs", 5), ALU.add)
        ts(v("noff"), v("cn", C_ - 1, C_ + 2, 2), -1.0, ALU.mult, C_ + 15.0, ALU.add)
        ts(col("sm", 0), col("zz", 3), col("zz", 0), ALU.subtract, 0.5, ALU.mult)
        ts(v("tn"), v("m4", 15, S_, 16), I_, ALU.add)
        cp(v("aa", by=v("qo")), v("zr"))
        before = v("pls", 0, 16 + K_, by=v("noff"))
        for f in (0, 2):
            act(v("ju", 16 * f, 16 * f + 32), before, AF.Sign, -unit, col("xs", f), acc=col("zz", at[f] + 1))
            ts(v("zz", at[f + 1] + 1, at[f + 1] + 1 + L_), before, unit, ALU.mult, col("xs", f + 1), ALU.is_lt)
            if f == 0:
                ts(col("zz", ZS - 1), col("sm", 0), float(Q1), ALU.max, -float(GAP), ALU.mult)
        tt(v("idv"), v("ndm", by=v("qo")), v("iob", 0, L_), ALU.add)
        scan(v("tb"), ones, v("aa"), ST - 1.0, ALU.mult, ALU.add)
        scan(v("zo"), v("zm"), v("zz"), 0.0, ALU.mult, ALU.add)
        cp(v("tb", by=v("qo")), v("idv"))
        ts(col("vo", 0), col("zo", ZS - 1), col("zo", ZW - 1), ALU.min, col("xs", 4), ALU.subtract)
        cp(v("xo", 0, 2), v("zo", 2, ZW, ZS))
        cp(v("xo", 2, 4), v("zo", ZS - 2, ZW, ZS))
        d = rising("m5", v("tb"), C_)
        tt(v("sm", 16, 32), v("lv", by=col("vo", 0)), v("mw"), ALU.add)
        for b in (0, 2, 1, 3):
            if not first:
                mm("p%d" % b, 128, v("qe", 128 * b, 128 * b + 128), v("se", 128 * b, 128 * b + 128), v(qb, 0, 128), v(sb, 96, 224))

        def arrived(b):
            act(plane("tc", b, L_, PW), plane("f64", b, w, by=v("la", 0, 2)) if first else v("p%d" % b, 0, L_))
        stayers(0)
        stayers(2)
        stayers(1)
        arrived(0)
        arrived(2)
        act(v("gq"), v("tab", by=v("xo")))
        stayers(3)
        arrived(1)
        arrived(3)
        ts(col("sm", 1), col("zo", ZS - 2), col("sm", 0), ALU.is_gt, 16.0, ALU.mult)
        cp(v("to"), d)
        reduce(col("sm", 2), v("sm", 16, 32), ALU.max)
        tt(v("cand", 16, 48), v("gq", 0, 32), v("gq", 32, 64), ALU.add)
        tt(v("cand", 0, 16), v("gq", 0, 16), v("tn"), ALU.add)
        ts(col("vo", 2), col("sm", 2), col("sm", 1), ALU.max, I_, ALU.add)

        def merged(b):
            (cp if b < 2 else act)(plane("mq", b, C_, MW), plane("tc", b, PW, PW, by=v("to")))

        merged(0)
        ts(v("qoff"), v("cand", by=col("vo", 2)), float(C_), ALU.min)
        for b in (1, 2, 3):
            merged(b)
        if last:
            gather_state("mq", MW, C_ + 1, "qoff", S_, [nothing] * 3)
        else:
            gather_state("mq", MW, C_ + 1, "qoff", S_, [lambda: tt(v("hh", 0, 16), v("cand", by=col("vo", 2)), v("kc"), ALU.min),
                                                        lambda: cp(v("uq"), v("hh", 0, 16)), lambda: in_order(0, PR1)])

    act(v("olw", ST), v("pls", 16, 16 + K_))
    act(v("ks", 0, C_), v("olw", by=v("to")))
    for h in range(2):
        mm_half("p%d" % (4 + h), v("qv"), v("sv"), "qf", "sf", h)
        codes = v("qf", 128 * h, 128 * h + 128, cast=dt.uint8)
        dma("Y", [codes], [], T.oc[:, 512 * h:512 * h + 512], codes[0])
    act(v("psb", 0, 128), v("p4", 0, 128))
    cp(v("psb", 128, 256), v("p5", 0, 128))
    cp(v("kp"), v("ks", 0, C_ + 1, by=v("qoff")))
    for h in range(2):
        half = v("psb", 128 * h, 128 * h + 128)
        dma("S", [half], [], T.y[:, 128 * h:128 * h + 128], half[0])
    for k in range(4):
        dma("Y", [v("sf")], [], T.osc[4 * k:4 * k + 4, :], T.sf[32 * k:32 * k + 4, :])
    dma("Y", [v("kp")], [], T.ol[:], T.kp[0:128:16, :])
    for s, k in cnt.items():
        if k:
            g.wait_ge(T.sem[s], k)
